import numpy as np
import ml_dtypes


def mxq(x, axis, fmt="e4m3"):
    dtype, down = {"e4m3": (ml_dtypes.float8_e4m3fn, 7), "e5m2": (ml_dtypes.float8_e5m2, 14)}[fmt]
    v = np.moveaxis(np.asarray(x, np.float32).astype(ml_dtypes.bfloat16).astype(np.float64), axis, -1)
    blocks = v.reshape(v.shape[:-1] + (-1, 32))
    amax = np.abs(blocks).max(-1, keepdims=True)
    byte = np.maximum(np.where(amax > 0, np.frexp(amax)[1] - 1 + 127, 0) - down, 1)
    scale = np.exp2(byte - 127.0)
    codes = (blocks / scale).astype(np.float32).astype(dtype).astype(np.float64)
    return np.moveaxis((codes * scale).reshape(v.shape), -1, axis)


WIDE = False


def mx_kscale(k):
    if not WIDE:
        return np.ones(k)
    levels = np.array([10, -10, 5, -5, 0])
    if k % 512:
        return np.exp2(np.random.permutation(np.resize(levels, k // 32))).repeat(32)
    a = np.empty((k // 512, 16))
    for p in range(k // 512):
        a[p, :8] = np.random.permutation(np.resize(levels, 8))
        for g in range(8):
            far = levels[np.abs(levels - a[p, g]) >= 10]
            a[p, g + 8] = far[np.random.randint(len(far))]
    return np.exp2(a.ravel()).repeat(32)


def f64(x):
    return np.asarray(x).astype(np.float64)


def striped(idx):
    return np.tile(idx.reshape(-1, 16).T, (8, 1)).astype(np.uint16)


def unstriped(offs):
    return offs[:16].T.reshape(-1).astype(np.int64)


E2M1 = np.array([0.0, 0.5, 1.0, 1.5, 2.0, 3.0, 4.0, 6.0, -0.0, -0.5, -1.0, -1.5, -2.0, -3.0, -4.0, -6.0])


def pack_weight(w, fmt):
    k, n = w.shape
    w = f64(np.asarray(w, np.float32).astype(ml_dtypes.bfloat16)).reshape(k // 32, 32, n)
    amax = np.abs(w).max(1)
    if fmt == "e4m3":
        byte = np.frexp(amax)[1] - 1 + 127 - 7
    else:
        mant, ex = np.frexp(amax / 6.0)
        byte = np.where(mant > 0.5, ex, ex - 1) + 127
    byte = np.clip(np.where(amax > 0, byte, 1), 1, 254)
    scaled = (w * np.exp2(127.0 - byte)[:, None, :]).reshape(k, n).astype(np.float32)
    by_word = np.ascontiguousarray(scaled.reshape(k // 512, 128, 4, n).transpose(0, 1, 3, 2))
    if fmt == "e4m3":
        words = by_word.astype(ml_dtypes.float8_e4m3fn).view(np.uint8)
    else:
        c = by_word.astype(ml_dtypes.float4_e2m1fn).view(np.uint8) & 0xF
        words = (c[..., 0::2] | (c[..., 1::2] << 4)).reshape(k // 512, 128, 2 * n)
    return np.ascontiguousarray(words), np.ascontiguousarray(byte.astype(np.uint8).reshape(k // 512, 16, n))


def unpack_weight(words, scales, fmt):
    g, _, n = scales.shape
    words = np.ascontiguousarray(words).reshape(g, 128, n, -1)
    if fmt == "e4m3":
        vals = words.view(ml_dtypes.float8_e4m3fn).astype(np.float64)
    else:
        nib = np.empty((g, 128, n, 4), np.uint8)
        nib[..., 0::2] = words & 0xF
        nib[..., 1::2] = words >> 4
        vals = E2M1[nib]
    vals = vals * np.repeat(np.exp2(scales.astype(np.float64) - 127.0), 8, axis=1)[..., None]
    return vals.transpose(0, 1, 3, 2).reshape(g * 512, n)


def relu(v):
    return np.maximum(v, 0.0)


K, T, E, C, H, N = 1536, 768, 4, 128, 512, 384


def by_expert(wq, xq):
    return np.concatenate([wq[e].T @ xq[:, e * C:(e + 1) * C] for e in range(E)], axis=1)


def setup_inputs():
    n = np.random.standard_normal
    s = mx_kscale(K)[:, None]
    u = mx_kscale(H)
    w1 = [pack_weight(m, "e2m1") for m in n((E, K, H)) / np.sqrt(K) / s[None] * u[None, None, :]]
    w2 = [pack_weight(m, "e2m1") for m in n((E, H, N)) / np.sqrt(H) / u[None, :, None]]
    return {
        "xT": (n((K, T)) * s).astype(np.float32),
        "w1_words": np.stack([m[0] for m in w1]),
        "w1_scales": np.stack([m[1] for m in w1]),
        "w2_words": np.stack([m[0] for m in w2]),
        "w2_scales": np.stack([m[1] for m in w2]),
        "gate": np.tile(np.random.uniform(0.2, 1.0, E * C), (K, 1)).astype(np.float32),
        "offs": striped(np.random.permutation(T)[:E * C]),
    }


def reference(xT, w1_words, w1_scales, w2_words, w2_scales, gate, offs):
    idx = unstriped(offs)
    w1 = np.stack([unpack_weight(w1_words[e], w1_scales[e], "e2m1") for e in range(E)])
    w2 = np.stack([unpack_weight(w2_words[e], w2_scales[e], "e2m1") for e in range(E)])
    xq = mxq(f64(gate) * f64(xT)[:, idx], 0, "e4m3")
    h = relu(by_expert(w1, xq))
    y = by_expert(w2, mxq(h, 0, "e4m3"))
    out = np.zeros((N, T))
    out[:, idx] = y
    return out

@@ -1,0 +1,182 @@
+from contextlib import ExitStack
+
+import concourse.mybir as mybir
+from concourse.masks import make_identity
+
+K, T, E, C, H, N = 1536, 768, 4, 128, 512, 384
+SLOTS = E * C
+FLOPS = 2 * SLOTS * (K * H + H * N)
+BYTES = 4 * K * T + E * (K * H + H * N) * 17 // 32 + 4 * SLOTS + 2 * SLOTS + 4 * N * T
+
+F32 = mybir.dt.float32
+BF16 = mybir.dt.bfloat16
+I32 = mybir.dt.int32
+U32 = mybir.dt.uint32
+U16 = mybir.dt.uint16
+U8 = mybir.dt.uint8
+FP8X4 = mybir.dt.float8_e4m3fn_x4
+FP4X4 = mybir.dt.float4_e2m1fn_x4
+MULT = mybir.AluOpType.mult
+RELU = mybir.ActivationFunctionType.Relu
+
+P = 128
+PACK = 4
+PASSES = K // (P * PACK)
+N_TILES = N // P
+PER_COL = 16
+
+
+def tile_moe_pre_mlp_relu_kernel(tc, xT, w1_words, w1_scales, w2_words, w2_scales, gate, offs, out):
+    nc = tc.nc
+    with ExitStack() as ctx:
+        keep = ctx.enter_context(tc.tile_pool(name="keep", bufs=1))
+        psum = ctx.enter_context(tc.psum_pool(name="psum", bufs=1))
+        ring = ctx.enter_context(tc.psum_pool(name="ring", bufs=2))
+
+        offsets = keep.tile([P, SLOTS // PER_COL], U16, name="offsets")
+        gate_sb = keep.tile([P, SLOTS], F32, name="gate_sb")
+        x_rows = [[keep.tile([P, T], F32, name=f"x_rows_{s}_{t}") for t in range(PACK)] for s in range(PASSES)]
+        gathered = [keep.tile([P, PACK, SLOTS], F32, name=f"gathered_{s}") for s in range(PASSES)]
+        x_bf = [keep.tile([P, SLOTS, PACK], BF16, name=f"x_bf_{s}", align_bytes=64) for s in range(PASSES)]
+        x_codes = keep.tile([P, PASSES, SLOTS], U32, name="x_codes", align_bytes=64)
+        x_scales = keep.tile([P, PASSES, SLOTS], U8, name="x_scales", align_bytes=64)
+        w1_sb = keep.tile([P, E, PASSES, 2 * H], U8, name="w1_sb", align_bytes=64)
+        w1_plane = keep.tile([P, E * PASSES, H], U8, name="w1_plane", align_bytes=64)
+        w2_sb = keep.tile([P, E, 2 * N], U8, name="w2_sb", align_bytes=64)
+        w2_plane = keep.tile([P, E, N], U8, name="w2_plane", align_bytes=64)
+        h_slot = keep.tile([P, E, H], BF16, name="h_slot", align_bytes=64)
+        h_bf = keep.tile([P, E, C * PACK], BF16, name="h_bf", align_bytes=64)
+        h_codes = keep.tile([P, SLOTS], U32, name="h_codes", align_bytes=64)
+        h_scales = keep.tile([P, SLOTS], U8, name="h_scales", align_bytes=64)
+        y_sb = keep.tile([P, N_TILES, SLOTS], F32, name="y_sb")
+        out_sb = [keep.tile([P, T], F32, name=f"out_sb_{c}") for c in range(N_TILES)]
+        ident = keep.tile([P, P], F32, name="ident")
+        a_acc = [psum.tile([P, H], F32, name=f"a_acc_{e}") for e in range(E)]
+
+        def slots_of(e0, e1):
+            return slice(e0 * C, e1 * C)
+
+        def offsets_of(e0, e1):
+            return offsets[:, e0 * C // PER_COL : e1 * C // PER_COL]
+
+        def load_x(s, t):
+            rows = xT.rearrange("(s p t) c -> s t p c", p=P, t=PACK)
+            nc.sync.dma_start(out=x_rows[s][t][:], in_=rows[s, t])
+
+        def load_plane(plane, scales, lo, hi):
+            rows = scales.rearrange("e s (q r) i -> r q (e s) i", r=4)
+            for r in range(4):
+                nc.sync.dma_start(out=plane[r:P:32, lo:hi, :].bitcast(I32), in_=rows[r, :, lo:hi, :].bitcast(I32))
+
+        def load_w1(e):
+            nc.sync.dma_start(out=w1_sb[:, e].bitcast(I32), in_=w1_words[e].rearrange("s p b -> p s b").bitcast(I32))
+
+        def gather(s, t, e0, e1):
+            cols = slots_of(e0, e1)
+            nc.vector.tensor_tensor(gathered[s][:, t, cols], x_rows[s][t][:].indirect(offsets_of(e0, e1)), gate_sb[:, cols], MULT)
+
+        def interleave(s, e0, e1):
+            cols = slots_of(e0, e1)
+            nc.scalar.copy(
+                out=x_bf[s][:, cols, :].rearrange("p (c i) t -> p c t i", i=4),
+                in_=gathered[s][:, :, cols].rearrange("p t (c i) -> p c t i", i=4),
+            )
+
+        def quantize_x(s, e0, e1):
+            cols = slots_of(e0, e1)
+            nc.vector.quantize_mx(
+                out=x_codes[:, s, cols].bitcast(FP8X4),
+                scales=x_scales[:, s, cols],
+                in_=x_bf[s][:, cols, :].rearrange("p c t -> p (c t)"),
+            )
+
+        def first_pass(s, e):
+            cols = slots_of(e, e + 1)
+            nc.tensor.matmul_mx(
+                out=a_acc[e][:],
+                lhsT=x_codes[:, s, cols].bitcast(FP8X4),
+                lhsT_scale=x_scales[:, s, cols],
+                rhs=w1_sb[:, e, s, :].bitcast(FP4X4),
+                rhs_scale=w1_plane[:, e * PASSES + s, :],
+                start=(s == 0),
+                stop=(s == PASSES - 1),
+            )
+
+        def second_layer(e):
+            cols = slots_of(e, e + 1)
+            nc.scalar.activation(
+                out=h_slot[:, e, :].rearrange("j (u p d) -> j u p d", u=2, d=2),
+                in_=a_acc[e][:].rearrange("j (p u d) -> j u p d", u=2, d=2),
+                func=RELU,
+            )
+            pairs = h_slot[:, e, :].bitcast(F32)
+            turned = ring.tile([P, 2, C], F32, name="turned")
+            for u in range(2):
+                nc.tensor.transpose(turned[:, u, :], pairs[:, u * P : (u + 1) * P], ident[:])
+            nc.scalar.copy(
+                out=h_bf[:, e, :].bitcast(F32).rearrange("p (j u) -> p j u", u=2),
+                in_=turned[:].rearrange("p u j -> p j u"),
+            )
+            nc.vector.quantize_mx(out=h_codes[:, cols].bitcast(FP8X4), scales=h_scales[:, cols], in_=h_bf[:, e, :])
+            y_acc = ring.tile([P, N_TILES, C], F32, name="y_acc")
+            for c in range(N_TILES):
+                nc.tensor.matmul_mx(
+                    out=y_acc[:, c, :],
+                    lhsT=w2_sb[:, e, 2 * P * c : 2 * P * (c + 1)].bitcast(FP4X4),
+                    lhsT_scale=w2_plane[:, e, P * c : P * (c + 1)],
+                    rhs=h_codes[:, cols].bitcast(FP8X4),
+                    rhs_scale=h_scales[:, cols],
+                    start=True,
+                    stop=True,
+                )
+            nc.scalar.copy(out=y_sb[:, :, cols], in_=y_acc[:])
+
+        def scatter(c, e0, e1):
+            nc.vector.tensor_copy(out_sb[c][:].indirect(offsets_of(e0, e1)), y_sb[:, c, slots_of(e0, e1)])
+
+        nc.vector.memset(w1_plane[:].bitcast(I32), 0)
+        nc.vector.memset(w2_plane[:].bitcast(I32), 0)
+        nc.vector.memset(out_sb[0][:], 0.0)
+        for c in range(1, N_TILES):
+            nc.scalar.activation(out=out_sb[c][:], in_=out_sb[0][:], func=RELU)
+        make_identity(nc, ident[:])
+
+        nc.sync.dma_start(offsets[:], offs)
+        load_x(0, 0)
+        nc.sync.dma_start(out=gate_sb[:], in_=gate[0:P, :])
+        for s in range(PASSES):
+            for t in range(PACK):
+                if (s, t) != (0, 0):
+                    load_x(s, t)
+        load_plane(w1_plane, w1_scales, 0, 2 * PASSES)
+        load_w1(0)
+        load_w1(1)
+        load_plane(w2_plane, w2_scales, 0, E)
+        nc.sync.dma_start(out=w2_sb[:].bitcast(I32), in_=w2_words.rearrange("e s p b -> p (e s) b").bitcast(I32))
+        load_plane(w1_plane, w1_scales, 2 * PASSES, E * PASSES)
+        load_w1(2)
+        load_w1(3)
+
+        for t in range(PACK):
+            gather(0, t, 0, E)
+        for e0, e1 in ((0, 2), (2, 4)):
+            for s in range(PASSES):
+                if s > 0:
+                    for t in range(PACK):
+                        gather(s, t, e0, e1)
+                if s < PASSES - 1:
+                    interleave(s, e0, e1)
+                    quantize_x(s, e0, e1)
+                    for e in range(e0, e1):
+                        first_pass(s, e)
+            for e in range(e0, e1):
+                interleave(PASSES - 1, e, e + 1)
+                quantize_x(PASSES - 1, e, e + 1)
+                first_pass(PASSES - 1, e)
+                second_layer(e)
+
+        for e in range(E):
+            for c in range(N_TILES):
+                scatter(c, e, e + 1)
+                if e == E - 1:
+                    nc.sync.dma_start(out=out[c * P : (c + 1) * P, :], in_=out_sb[c][:])

@@ -23,7 +23,10 @@ P = 128
 PACK = 4
 PASSES = K // (P * PACK)
 N_TILES = N // P
-PER_COL = 16
+LIST_ROWS = 16
+SCALE_ROWS = 4
+LINE = 4
+PAIR = 2
 
 
 def tile_moe_pre_mlp_relu_kernel(tc, xT, w1_words, w1_scales, w2_words, w2_scales, gate, offs, out):
@@ -33,150 +36,227 @@ def tile_moe_pre_mlp_relu_kernel(tc, xT, w1_words, w1_scales, w2_words, w2_scale
         psum = ctx.enter_context(tc.psum_pool(name="psum", bufs=1))
         ring = ctx.enter_context(tc.psum_pool(name="ring", bufs=2))
 
-        offsets = keep.tile([P, SLOTS // PER_COL], U16, name="offsets")
+        tiles = {}
+        place = {}
+
+        def new_tile(name, shape, dtype, after=None):
+            place[name] = place[after] if after else name
+            tiles[name] = keep.tile(shape, dtype, name=name, tag=place[name], align_bytes=64)
+            return tiles[name]
+
+        offsets = keep.tile([P, SLOTS // LIST_ROWS], U16, name="offsets")
         gate_sb = keep.tile([P, SLOTS], F32, name="gate_sb")
         x_rows = [[keep.tile([P, T], F32, name=f"x_rows_{s}_{t}") for t in range(PACK)] for s in range(PASSES)]
-        gathered = [keep.tile([P, PACK, SLOTS], F32, name=f"gathered_{s}") for s in range(PASSES)]
-        x_bf = [keep.tile([P, SLOTS, PACK], BF16, name=f"x_bf_{s}", align_bytes=64) for s in range(PASSES)]
-        x_codes = keep.tile([P, PASSES, SLOTS], U32, name="x_codes", align_bytes=64)
-        x_scales = keep.tile([P, PASSES, SLOTS], U8, name="x_scales", align_bytes=64)
-        w1_sb = keep.tile([P, E, PASSES, 2 * H], U8, name="w1_sb", align_bytes=64)
-        w1_plane = keep.tile([P, E * PASSES, H], U8, name="w1_plane", align_bytes=64)
-        w2_sb = keep.tile([P, E, 2 * N], U8, name="w2_sb", align_bytes=64)
-        w2_plane = keep.tile([P, E, N], U8, name="w2_plane", align_bytes=64)
-        h_slot = keep.tile([P, E, H], BF16, name="h_slot", align_bytes=64)
-        h_bf = keep.tile([P, E, C * PACK], BF16, name="h_bf", align_bytes=64)
-        h_codes = keep.tile([P, SLOTS], U32, name="h_codes", align_bytes=64)
-        h_scales = keep.tile([P, SLOTS], U8, name="h_scales", align_bytes=64)
-        y_sb = keep.tile([P, N_TILES, SLOTS], F32, name="y_sb")
+        w1_sb = [new_tile(f"w1_{e}", [P, PASSES, 2 * H], U8) for e in range(E)]
+        w1_plane = [new_tile(f"w1_plane_{half}", [P, PAIR * PASSES, H], U8) for half in range(2)]
+        w2_first = new_tile("w2_first", [P, 1, 2 * N], U8)
+        w2_rest = new_tile("w2_rest", [P, E - 1, 2 * N], U8)
+        w2_plane = new_tile("w2_plane", [P, E, N], U8)
         out_sb = [keep.tile([P, T], F32, name=f"out_sb_{c}") for c in range(N_TILES)]
         ident = keep.tile([P, P], F32, name="ident")
-        a_acc = [psum.tile([P, H], F32, name=f"a_acc_{e}") for e in range(E)]
 
-        def slots_of(e0, e1):
-            return slice(e0 * C, e1 * C)
+        x_mx = {}
+        a_acc, turned, y_acc = {}, {}, {}
+        y_sb = {}
 
-        def offsets_of(e0, e1):
-            return offsets[:, e0 * C // PER_COL : e1 * C // PER_COL]
+        def slots(experts, first=0):
+            return slice((experts.start - first) * C, (experts.stop - first) * C)
+
+        def entries(experts):
+            return offsets[:, experts.start * C // LIST_ROWS : experts.stop * C // LIST_ROWS]
 
         def load_x(s, t):
-            rows = xT.rearrange("(s p t) c -> s t p c", p=P, t=PACK)
-            nc.sync.dma_start(out=x_rows[s][t][:], in_=rows[s, t])
+            nc.sync.dma_start(out=x_rows[s][t][:], in_=xT.rearrange("(s p t) c -> s t p c", p=P, t=PACK)[s, t])
 
-        def load_plane(plane, scales, lo, hi):
-            rows = scales.rearrange("e s (q r) i -> r q (e s) i", r=4)
-            for r in range(4):
-                nc.sync.dma_start(out=plane[r:P:32, lo:hi, :].bitcast(I32), in_=rows[r, :, lo:hi, :].bitcast(I32))
+        def load_gate(experts):
+            nc.sync.dma_start(out=gate_sb[:, slots(experts)], in_=gate[0:P, slots(experts)])
+
+        def load_plane(plane, scales, passes):
+            rows = scales.rearrange("e s (g r) i -> r g (e s) i", r=SCALE_ROWS)
+            for r in range(SCALE_ROWS):
+                nc.sync.dma_start(out=plane[r:P:32, :, :].bitcast(I32), in_=rows[r, :, passes, :].bitcast(I32))
 
         def load_w1(e):
-            nc.sync.dma_start(out=w1_sb[:, e].bitcast(I32), in_=w1_words[e].rearrange("s p b -> p s b").bitcast(I32))
+            nc.sync.dma_start(out=w1_sb[e][:].bitcast(I32), in_=w1_words[e].rearrange("s p b -> p s b").bitcast(I32))
 
-        def gather(s, t, e0, e1):
-            cols = slots_of(e0, e1)
-            nc.vector.tensor_tensor(gathered[s][:, t, cols], x_rows[s][t][:].indirect(offsets_of(e0, e1)), gate_sb[:, cols], MULT)
+        def load_w2(tile, experts):
+            words = w2_words.rearrange("e s p b -> p (e s) b")
+            nc.sync.dma_start(out=tile[:].bitcast(I32), in_=words[:, experts.start : experts.stop, :].bitcast(I32))
 
-        def interleave(s, e0, e1):
-            cols = slots_of(e0, e1)
+        def own_gate(name, experts):
+            own = new_tile(name, [P, len(experts) * C], F32)
+            nc.scalar.copy(out=own[:], in_=gate_sb[:, slots(experts)])
+            return own[:]
+
+        def gather(dst, s, t, experts, gates=None):
+            gates = gate_sb[:, slots(experts)] if gates is None else gates
+            nc.vector.tensor_tensor(dst, x_rows[s][t][:].indirect(entries(experts)), gates, MULT)
+
+        def interleave(src, s, experts, after=None):
+            x_bf = new_tile(f"x_bf_{s}_{experts.start}", [P, len(experts) * C, PACK], BF16, after)
             nc.scalar.copy(
-                out=x_bf[s][:, cols, :].rearrange("p (c i) t -> p c t i", i=4),
-                in_=gathered[s][:, :, cols].rearrange("p t (c i) -> p c t i", i=4),
+                out=x_bf[:].rearrange("p (c i) t -> p c t i", i=LINE),
+                in_=src.rearrange("p t (c i) -> p c t i", i=LINE),
             )
 
-        def quantize_x(s, e0, e1):
-            cols = slots_of(e0, e1)
-            nc.vector.quantize_mx(
-                out=x_codes[:, s, cols].bitcast(FP8X4),
-                scales=x_scales[:, s, cols],
-                in_=x_bf[s][:, cols, :].rearrange("p c t -> p (c t)"),
-            )
+        def quantize_x(s, experts, after=None):
+            codes = new_tile(f"x_codes_{s}_{experts.start}", [P, len(experts) * C], U32, after)
+            scales = new_tile(f"x_scales_{s}_{experts.start}", [P, len(experts) * C], U8)
+            x_bf = tiles[f"x_bf_{s}_{experts.start}"]
+            nc.vector.quantize_mx(out=codes[:].bitcast(FP8X4), scales=scales[:], in_=x_bf[:].rearrange("p c t -> p (c t)"))
+            for e in experts:
+                cols = slots(range(e, e + 1), experts.start)
+                x_mx[s, e] = (codes[:, cols], scales[:, cols])
 
-        def first_pass(s, e):
-            cols = slots_of(e, e + 1)
-            nc.tensor.matmul_mx(
-                out=a_acc[e][:],
-                lhsT=x_codes[:, s, cols].bitcast(FP8X4),
-                lhsT_scale=x_scales[:, s, cols],
-                rhs=w1_sb[:, e, s, :].bitcast(FP4X4),
-                rhs_scale=w1_plane[:, e * PASSES + s, :],
-                start=(s == 0),
-                stop=(s == PASSES - 1),
-            )
-
-        def second_layer(e):
-            cols = slots_of(e, e + 1)
+        def first_layer(e):
+            a_acc[e] = psum.tile([P, H], F32, name=f"a_acc_{e}", tag=f"a_acc_{e % 2}")
+            for s in range(PASSES):
+                nc.tensor.matmul_mx(
+                    out=a_acc[e][:],
+                    lhsT=x_mx[s, e][0].bitcast(FP8X4),
+                    lhsT_scale=x_mx[s, e][1],
+                    rhs=w1_sb[e][:, s, :].bitcast(FP4X4),
+                    rhs_scale=w1_plane[e // PAIR][:, (e % PAIR) * PASSES + s, :],
+                    start=(s == 0),
+                    stop=(s == PASSES - 1),
+                )
+            h_slot = new_tile(f"h_slot_{e}", [P, H], BF16)
             nc.scalar.activation(
-                out=h_slot[:, e, :].rearrange("j (u p d) -> j u p d", u=2, d=2),
-                in_=a_acc[e][:].rearrange("j (p u d) -> j u p d", u=2, d=2),
+                out=h_slot[:].rearrange("j (u p d) -> j u p d", u=2, d=PAIR),
+                in_=a_acc[e][:].rearrange("j (p u d) -> j u p d", u=2, d=PAIR),
                 func=RELU,
             )
-            pairs = h_slot[:, e, :].bitcast(F32)
-            turned = ring.tile([P, 2, C], F32, name="turned")
+            turned[e] = ring.tile([P, 2, C], F32, name="turned")
             for u in range(2):
-                nc.tensor.transpose(turned[:, u, :], pairs[:, u * P : (u + 1) * P], ident[:])
+                nc.tensor.transpose(turned[e][:, u, :], h_slot[:].bitcast(F32)[:, u * P : (u + 1) * P], ident[:])
+            h_bf = new_tile(f"h_bf_{e}", [P, C * PACK], BF16)
             nc.scalar.copy(
-                out=h_bf[:, e, :].bitcast(F32).rearrange("p (j u) -> p j u", u=2),
-                in_=turned[:].rearrange("p u j -> p j u"),
+                out=h_bf[:].bitcast(F32).rearrange("p (j u) -> p j u", u=2),
+                in_=turned[e][:].rearrange("p u j -> p j u"),
             )
-            nc.vector.quantize_mx(out=h_codes[:, cols].bitcast(FP8X4), scales=h_scales[:, cols], in_=h_bf[:, e, :])
-            y_acc = ring.tile([P, N_TILES, C], F32, name="y_acc")
+
+        def second_layer(e, after=None):
+            codes = new_tile(f"h_codes_{e}", [P, C], U32, after)
+            scales = new_tile(f"h_scales_{e}", [P, C], U8)
+            nc.vector.quantize_mx(out=codes[:].bitcast(FP8X4), scales=scales[:], in_=tiles[f"h_bf_{e}"][:])
+            w2_e = w2_first[:, 0, :] if e == 0 else w2_rest[:, e - 1, :]
+            y_acc[e] = psum.tile([P, N_TILES, C], F32, name=f"y_acc_{e}")
             for c in range(N_TILES):
                 nc.tensor.matmul_mx(
-                    out=y_acc[:, c, :],
-                    lhsT=w2_sb[:, e, 2 * P * c : 2 * P * (c + 1)].bitcast(FP4X4),
+                    out=y_acc[e][:, c, :],
+                    lhsT=w2_e[:, 2 * P * c : 2 * P * (c + 1)].bitcast(FP4X4),
                     lhsT_scale=w2_plane[:, e, P * c : P * (c + 1)],
-                    rhs=h_codes[:, cols].bitcast(FP8X4),
-                    rhs_scale=h_scales[:, cols],
+                    rhs=codes[:].bitcast(FP8X4),
+                    rhs_scale=scales[:],
                     start=True,
                     stop=True,
                 )
-            nc.scalar.copy(out=y_sb[:, :, cols], in_=y_acc[:])
 
-        def scatter(c, e0, e1):
-            nc.vector.tensor_copy(out_sb[c][:].indirect(offsets_of(e0, e1)), y_sb[:, c, slots_of(e0, e1)])
+        def copy_y(e, row_tiles, after=None):
+            y = new_tile(f"y_{e}_{row_tiles.start}", [P, len(row_tiles), C], F32, after)
+            nc.scalar.copy(out=y[:], in_=y_acc[e][:, row_tiles.start : row_tiles.stop, :])
+            for c in row_tiles:
+                y_sb[c, e] = y[:, c - row_tiles.start, :]
 
-        nc.vector.memset(w1_plane[:].bitcast(I32), 0)
-        nc.vector.memset(w2_plane[:].bitcast(I32), 0)
+        def scatter(c, e):
+            nc.vector.tensor_copy(out_sb[c][:].indirect(entries(range(e, e + 1))), y_sb[c, e])
+
+        every, early, late = range(0, E), range(0, PAIR), range(PAIR, E)
+        one = [range(e, e + 1) for e in range(E)]
+        first_rows, other_rows = range(0, 1), range(1, N_TILES)
+
+        for plane in w1_plane + [w2_plane]:
+            nc.vector.memset(plane[:].bitcast(I32), 0)
         nc.vector.memset(out_sb[0][:], 0.0)
-        for c in range(1, N_TILES):
+        for c in other_rows:
             nc.scalar.activation(out=out_sb[c][:], in_=out_sb[0][:], func=RELU)
         make_identity(nc, ident[:])
 
-        nc.sync.dma_start(offsets[:], offs)
         load_x(0, 0)
-        nc.sync.dma_start(out=gate_sb[:], in_=gate[0:P, :])
+        nc.sync.dma_start(offsets[:], offs)
+        load_gate(early)
+        load_gate(late)
         for s in range(PASSES):
             for t in range(PACK):
                 if (s, t) != (0, 0):
                     load_x(s, t)
-        load_plane(w1_plane, w1_scales, 0, 2 * PASSES)
-        load_w1(0)
-        load_w1(1)
-        load_plane(w2_plane, w2_scales, 0, E)
-        nc.sync.dma_start(out=w2_sb[:].bitcast(I32), in_=w2_words.rearrange("e s p b -> p (e s) b").bitcast(I32))
-        load_plane(w1_plane, w1_scales, 2 * PASSES, E * PASSES)
-        load_w1(2)
-        load_w1(3)
+        load_plane(w1_plane[0], w1_scales, slice(0, PAIR * PASSES))
+        for e in early:
+            load_w1(e)
+        load_plane(w2_plane, w2_scales, slice(0, E))
+        load_w2(w2_first, one[0])
+        load_plane(w1_plane[1], w1_scales, slice(PAIR * PASSES, E * PASSES))
+        for e in late:
+            load_w1(e)
+        load_w2(w2_rest, range(1, E))
 
+        gate_early = [own_gate(f"gate_early_{t}", early) for t in range(PACK)]
+        gate_last = own_gate("gate_last", one[3])
+
+        g0 = new_tile("g0", [P, PACK, SLOTS], F32)
+        gather(g0[:, 0, slots(early)], 0, 0, early)
+        gather(g0[:, 0, slots(late)], 0, 0, late)
+        for t in range(1, PACK):
+            gather(g0[:, t, :], 0, t, every)
+
+        g1_early = new_tile("g1_early", [P, PACK, PAIR * C], F32)
         for t in range(PACK):
-            gather(0, t, 0, E)
-        for e0, e1 in ((0, 2), (2, 4)):
-            for s in range(PASSES):
-                if s > 0:
-                    for t in range(PACK):
-                        gather(s, t, e0, e1)
-                if s < PASSES - 1:
-                    interleave(s, e0, e1)
-                    quantize_x(s, e0, e1)
-                    for e in range(e0, e1):
-                        first_pass(s, e)
-            for e in range(e0, e1):
-                interleave(PASSES - 1, e, e + 1)
-                quantize_x(PASSES - 1, e, e + 1)
-                first_pass(PASSES - 1, e)
-                second_layer(e)
+            gather(g1_early[:, t, :], 1, t, early)
+        interleave(g0[:, :, slots(early)], 0, early)
+        interleave(g1_early[:], 1, early)
+        g2_early = new_tile("g2_early", [P, PACK, PAIR * C], F32)
+        for t in range(PACK):
+            gather(g2_early[:, t, :], 2, t, early, gate_early[t])
+            if t in (1, 2):
+                quantize_x(t - 1, early, after=f"gate_early_{t}")
+        for e in early:
+            interleave(g2_early[:, :, slots(one[e])], 2, one[e])
+            quantize_x(2, one[e])
+            first_layer(e)
+            if e == 0:
+                second_layer(0)
+                copy_y(0, first_rows)
+                copy_y(0, other_rows)
+        interleave(g0[:, :, slots(late)], 0, late)
+        quantize_x(0, late, after="gate_early_0")
 
-        for e in range(E):
+        g1_2 = new_tile("g1_2", [P, PACK, C], F32, after="gate_early_3")
+        for t in range(PACK):
+            gather(g1_2[:, t, :], 1, t, one[2])
+        interleave(g1_2[:], 1, one[2], after="g2_early")
+        g_held = new_tile("g_held", [P, 2, PACK, C], F32, after="x_bf_2_1")
+        g2_2, g1_3 = g_held[:, 1], g_held[:, 0]
+        for t in range(PACK):
+            gather(g2_2[:, t, :], 2, t, one[2])
+        interleave(g2_2, 2, one[2], after="h_slot_0")
+        quantize_x(2, one[2])
+        gather(g1_3[:, 0, :], 1, 0, one[3], gate_last)
+        quantize_x(1, one[2], after="gate_last")
+        for t in range(1, PACK):
+            gather(g1_3[:, t, :], 1, t, one[3])
+        first_layer(2)
+
+        second_layer(1)
+        copy_y(1, first_rows)
+        copy_y(1, other_rows, after="h_slot_2")
+        interleave(g1_3, 1, one[3], after="h_slot_1")
+        quantize_x(1, one[3])
+        g2_3 = new_tile("g2_3", [P, PACK, C], F32)
+        for t in range(PACK):
+            gather(g2_3[:, t, :], 2, t, one[3])
+        interleave(g2_3[:], 2, one[3])
+        quantize_x(2, one[3], after="h_bf_0")
+        first_layer(3)
+        scatter(0, 0)
+        second_layer(2, after="y_0_0")
+        copy_y(2, first_rows)
+        copy_y(2, other_rows, after="h_slot_3")
+        second_layer(3)
+        copy_y(3, range(0, N_TILES))
+
+        for e in every:
             for c in range(N_TILES):
-                scatter(c, e, e + 1)
+                if (c, e) != (0, 0):
+                    scatter(c, e)
                 if e == E - 1:
                     nc.sync.dma_start(out=out[c * P : (c + 1) * P, :], in_=out_sb[c][:])

@@ -45,15 +45,21 @@ def tile_moe_pre_mlp_relu_kernel(tc, xT, w1_words, w1_scales, w2_words, w2_scale
             return tiles[name]
 
         offsets = keep.tile([P, SLOTS // LIST_ROWS], U16, name="offsets")
-        gate_sb = keep.tile([P, SLOTS], F32, name="gate_sb")
+        gate_sb = new_tile("gate_sb", [P, SLOTS], F32)
+        gate_col = new_tile("gate_col", [P, PAIR], F32)
         x_rows = [[keep.tile([P, T], F32, name=f"x_rows_{s}_{t}") for t in range(PACK)] for s in range(PASSES)]
-        w1_sb = [new_tile(f"w1_{e}", [P, PASSES, 2 * H], U8) for e in range(E)]
+        w1_first = new_tile("w1_first", [P, 1, 2 * H], U8)
+        w1_sb = [new_tile(f"w1_{e}", [P, PASSES - (e == 0), 2 * H], U8) for e in range(E)]
+        w1_pass = {(s, e): w1_sb[e][:, s, :] for e in range(1, E) for s in range(PASSES)}
+        w1_pass[0, 0] = w1_first[:, 0, :]
+        for s in range(1, PASSES):
+            w1_pass[s, 0] = w1_sb[0][:, s - 1, :]
         w1_plane = [new_tile(f"w1_plane_{half}", [P, PAIR * PASSES, H], U8) for half in range(2)]
-        w2_first = new_tile("w2_first", [P, 1, 2 * N], U8)
-        w2_rest = new_tile("w2_rest", [P, E - 1, 2 * N], U8)
+        w2_early = [new_tile(f"w2_{e}", [P, 1, 2 * N], U8) for e in range(PAIR)]
+        w2_late = new_tile("w2_late", [P, PAIR, 2 * N], U8)
         w2_plane = new_tile("w2_plane", [P, E, N], U8)
         out_sb = [keep.tile([P, T], F32, name=f"out_sb_{c}") for c in range(N_TILES)]
-        ident = keep.tile([P, P], F32, name="ident")
+        ident = [new_tile(f"ident_{e}", [P, P], F32) for e in range(E)]
 
         x_mx = {}
         a_acc, turned, y_acc = {}, {}, {}
@@ -76,50 +82,51 @@ def tile_moe_pre_mlp_relu_kernel(tc, xT, w1_words, w1_scales, w2_words, w2_scale
             for r in range(SCALE_ROWS):
                 nc.sync.dma_start(out=plane[r:P:32, :, :].bitcast(I32), in_=rows[r, :, passes, :].bitcast(I32))
 
-        def load_w1(e):
-            nc.sync.dma_start(out=w1_sb[e][:].bitcast(I32), in_=w1_words[e].rearrange("s p b -> p s b").bitcast(I32))
+        def load_w1(tile, e, passes):
+            words = w1_words[e].rearrange("s p b -> p s b")
+            nc.sync.dma_start(out=tile[:].bitcast(I32), in_=words[:, passes, :].bitcast(I32))
 
         def load_w2(tile, experts):
             words = w2_words.rearrange("e s p b -> p (e s) b")
             nc.sync.dma_start(out=tile[:].bitcast(I32), in_=words[:, experts.start : experts.stop, :].bitcast(I32))
 
-        def own_gate(name, experts):
-            own = new_tile(name, [P, len(experts) * C], F32)
-            nc.scalar.copy(out=own[:], in_=gate_sb[:, slots(experts)])
-            return own[:]
-
-        def gather(dst, s, t, experts, gates=None):
-            gates = gate_sb[:, slots(experts)] if gates is None else gates
+        def gather(dst, s, t, experts, gates):
             nc.vector.tensor_tensor(dst, x_rows[s][t][:].indirect(entries(experts)), gates, MULT)
 
-        def interleave(src, s, experts, after=None):
-            x_bf = new_tile(f"x_bf_{s}_{experts.start}", [P, len(experts) * C, PACK], BF16, after)
+        def blocks(first, count):
+            return slice(first * C, (first + count) * C)
+
+        def interleave_blocks(dst, src):
             nc.scalar.copy(
-                out=x_bf[:].rearrange("p (c i) t -> p c t i", i=LINE),
+                out=dst.rearrange("p e (c i) t -> p e c t i", i=LINE),
+                in_=src.rearrange("p t (e c i) -> p e c t i", i=LINE, c=C // LINE),
+            )
+
+        def interleave(dst, src):
+            nc.scalar.copy(
+                out=dst.rearrange("p (c i) t -> p c t i", i=LINE),
                 in_=src.rearrange("p t (c i) -> p c t i", i=LINE),
             )
 
-        def quantize_x(s, experts, after=None):
-            codes = new_tile(f"x_codes_{s}_{experts.start}", [P, len(experts) * C], U32, after)
-            scales = new_tile(f"x_scales_{s}_{experts.start}", [P, len(experts) * C], U8)
-            x_bf = tiles[f"x_bf_{s}_{experts.start}"]
-            nc.vector.quantize_mx(out=codes[:].bitcast(FP8X4), scales=scales[:], in_=x_bf[:].rearrange("p c t -> p (c t)"))
-            for e in experts:
-                cols = slots(range(e, e + 1), experts.start)
-                x_mx[s, e] = (codes[:, cols], scales[:, cols])
+        def quantize_x(x_bf, codes, scales, held):
+            nc.vector.quantize_mx(out=codes.bitcast(FP8X4), scales=scales, in_=x_bf.rearrange("p c t -> p (c t)"))
+            for b, key in enumerate(held):
+                x_mx[key] = (codes[:, blocks(b, 1)], scales[:, blocks(b, 1)])
 
-        def first_layer(e):
-            a_acc[e] = psum.tile([P, H], F32, name=f"a_acc_{e}", tag=f"a_acc_{e % 2}")
+        def first_product(e):
+            a_acc[e] = psum.tile([P, H], F32, name=f"a_acc_{e}", tag="a_acc")
             for s in range(PASSES):
                 nc.tensor.matmul_mx(
                     out=a_acc[e][:],
                     lhsT=x_mx[s, e][0].bitcast(FP8X4),
                     lhsT_scale=x_mx[s, e][1],
-                    rhs=w1_sb[e][:, s, :].bitcast(FP4X4),
+                    rhs=w1_pass[s, e].bitcast(FP4X4),
                     rhs_scale=w1_plane[e // PAIR][:, (e % PAIR) * PASSES + s, :],
                     start=(s == 0),
                     stop=(s == PASSES - 1),
                 )
+
+        def turn_h(e):
             h_slot = new_tile(f"h_slot_{e}", [P, H], BF16)
             nc.scalar.activation(
                 out=h_slot[:].rearrange("j (u p d) -> j u p d", u=2, d=PAIR),
@@ -128,7 +135,7 @@ def tile_moe_pre_mlp_relu_kernel(tc, xT, w1_words, w1_scales, w2_words, w2_scale
             )
             turned[e] = ring.tile([P, 2, C], F32, name="turned")
             for u in range(2):
-                nc.tensor.transpose(turned[e][:, u, :], h_slot[:].bitcast(F32)[:, u * P : (u + 1) * P], ident[:])
+                nc.tensor.transpose(turned[e][:, u, :], h_slot[:].bitcast(F32)[:, u * P : (u + 1) * P], ident[e][:])
             h_bf = new_tile(f"h_bf_{e}", [P, C * PACK], BF16)
             nc.scalar.copy(
                 out=h_bf[:].bitcast(F32).rearrange("p (j u) -> p j u", u=2),
@@ -139,7 +146,7 @@ def tile_moe_pre_mlp_relu_kernel(tc, xT, w1_words, w1_scales, w2_words, w2_scale
             codes = new_tile(f"h_codes_{e}", [P, C], U32, after)
             scales = new_tile(f"h_scales_{e}", [P, C], U8)
             nc.vector.quantize_mx(out=codes[:].bitcast(FP8X4), scales=scales[:], in_=tiles[f"h_bf_{e}"][:])
-            w2_e = w2_first[:, 0, :] if e == 0 else w2_rest[:, e - 1, :]
+            w2_e = w2_early[e][:, 0, :] if e < PAIR else w2_late[:, e - PAIR, :]
             y_acc[e] = psum.tile([P, N_TILES, C], F32, name=f"y_acc_{e}")
             for c in range(N_TILES):
                 nc.tensor.matmul_mx(
@@ -162,101 +169,126 @@ def tile_moe_pre_mlp_relu_kernel(tc, xT, w1_words, w1_scales, w2_words, w2_scale
             nc.vector.tensor_copy(out_sb[c][:].indirect(entries(range(e, e + 1))), y_sb[c, e])
 
         every, early, late = range(0, E), range(0, PAIR), range(PAIR, E)
+        three = range(0, E - 1)
         one = [range(e, e + 1) for e in range(E)]
         first_rows, other_rows = range(0, 1), range(1, N_TILES)
 
-        for plane in w1_plane + [w2_plane]:
+        for plane in [w1_plane[1], w1_plane[0], w2_plane]:
             nc.vector.memset(plane[:].bitcast(I32), 0)
-        nc.vector.memset(out_sb[0][:], 0.0)
-        for c in other_rows:
-            nc.scalar.activation(out=out_sb[c][:], in_=out_sb[0][:], func=RELU)
-        make_identity(nc, ident[:])
+        zeros = w1_plane[1][:].rearrange("p s i -> p (s i)").bitcast(F32)
+        nc.scalar.activation(out=out_sb[0][:], in_=zeros, func=RELU)
+        make_identity(nc, ident[0][:])
 
+        nc.sync.dma_start(out=gate_col[:], in_=gate[0, slots(early)].rearrange("(p m) -> p m", m=PAIR))
         load_x(0, 0)
         nc.sync.dma_start(offsets[:], offs)
-        load_gate(early)
         load_gate(late)
         for s in range(PASSES):
             for t in range(PACK):
                 if (s, t) != (0, 0):
                     load_x(s, t)
         load_plane(w1_plane[0], w1_scales, slice(0, PAIR * PASSES))
-        for e in early:
-            load_w1(e)
+        load_w1(w1_first, 0, slice(0, 1))
+        load_w1(w1_sb[0], 0, slice(1, PASSES))
         load_plane(w2_plane, w2_scales, slice(0, E))
-        load_w2(w2_first, one[0])
+        load_w1(w1_sb[1], 1, slice(0, PASSES))
+        load_w2(w2_early[0], one[0])
         load_plane(w1_plane[1], w1_scales, slice(PAIR * PASSES, E * PASSES))
         for e in late:
-            load_w1(e)
-        load_w2(w2_rest, range(1, E))
+            load_w1(w1_sb[e], e, slice(0, PASSES))
+        load_w2(w2_early[1], one[1])
+        load_w2(w2_late, late)
 
-        gate_early = [own_gate(f"gate_early_{t}", early) for t in range(PACK)]
-        gate_last = own_gate("gate_last", one[3])
+        spread = ring.tile([P, 2, C], F32, name="turned")
+        for m in range(PAIR):
+            nc.tensor.transpose(spread[:, m, :], gate_col[:, m : m + 1].to_broadcast([P, P]), ident[0][:])
+        nc.scalar.copy(out=gate_sb[:, slots(early)].rearrange("p (j m) -> p j m", m=PAIR), in_=spread[:].rearrange("p m j -> p j m"))
+        own_gate = new_tile("own_gate_0", [P, C], F32)
+        nc.scalar.copy(out=own_gate[:], in_=gate_sb[:, slots(one[0])])
+        for e in range(1, E):
+            nc.scalar.copy(out=ident[e][:], in_=ident[0][:])
+        for c in other_rows:
+            nc.gpsimd.memset(out_sb[c][:], 0.0)
 
         g0 = new_tile("g0", [P, PACK, SLOTS], F32)
-        gather(g0[:, 0, slots(early)], 0, 0, early)
-        gather(g0[:, 0, slots(late)], 0, 0, late)
+        gather(g0[:, 0, slots(late)], 0, 0, late, gate_sb[:, slots(late)])
+        gather(g0[:, 0, slots(early)], 0, 0, early, gate_sb[:, slots(early)])
         for t in range(1, PACK):
-            gather(g0[:, t, :], 0, t, every)
+            gather(g0[:, t, :], 0, t, every, gate_sb[:])
+        held = [(s, e) for e in every for s in range(2)][:-1]
+        bf_head = new_tile("bf_head", [P, E, 2, C, PACK], BF16)
+        bf_flat = bf_head[:].rearrange("p e s c t -> p (e s c) t")
+        interleave_blocks(bf_head[:, 0:PAIR, 0], g0[:, :, slots(early)])
+        interleave_blocks(bf_head[:, PAIR:E, 0], g0[:, :, slots(late)])
 
-        g1_early = new_tile("g1_early", [P, PACK, PAIR * C], F32)
+        g1 = new_tile("g1", [P, PACK, len(three) * C], F32)
         for t in range(PACK):
-            gather(g1_early[:, t, :], 1, t, early)
-        interleave(g0[:, :, slots(early)], 0, early)
-        interleave(g1_early[:], 1, early)
-        g2_early = new_tile("g2_early", [P, PACK, PAIR * C], F32)
-        for t in range(PACK):
-            gather(g2_early[:, t, :], 2, t, early, gate_early[t])
-            if t in (1, 2):
-                quantize_x(t - 1, early, after=f"gate_early_{t}")
+            gather(g1[:, t, :], 1, t, three, gate_sb[:, slots(three)])
+        interleave(bf_head[:, 0, 1], g1[:, :, slots(one[0])])
+        interleave_blocks(bf_head[:, 1 : len(three), 1], g1[:, :, slots(range(1, E - 1))])
+        g2 = new_tile("g2", [P, PACK, PAIR * C], F32)
+        for t in range(PACK - 1):
+            gather(g2[:, t, :], 2, t, early, gate_sb[:, slots(early)])
         for e in early:
-            interleave(g2_early[:, :, slots(one[e])], 2, one[e])
-            quantize_x(2, one[e])
-            first_layer(e)
-            if e == 0:
-                second_layer(0)
-                copy_y(0, first_rows)
-                copy_y(0, other_rows)
-        interleave(g0[:, :, slots(late)], 0, late)
-        quantize_x(0, late, after="gate_early_0")
+            gather(g2[:, PACK - 1, slots(one[e])], 2, PACK - 1, one[e], own_gate[:] if e == 0 else gate_sb[:, slots(one[e])])
+        codes_head = new_tile("codes_head", [P, len(held) * C], U32, after="own_gate_0")
+        scales_head = new_tile("scales_head", [P, len(held) * C], U8)
 
-        g1_2 = new_tile("g1_2", [P, PACK, C], F32, after="gate_early_3")
-        for t in range(PACK):
-            gather(g1_2[:, t, :], 1, t, one[2])
-        interleave(g1_2[:], 1, one[2], after="g2_early")
-        g_held = new_tile("g_held", [P, 2, PACK, C], F32, after="x_bf_2_1")
-        g2_2, g1_3 = g_held[:, 1], g_held[:, 0]
-        for t in range(PACK):
-            gather(g2_2[:, t, :], 2, t, one[2])
-        interleave(g2_2, 2, one[2], after="h_slot_0")
-        quantize_x(2, one[2])
-        gather(g1_3[:, 0, :], 1, 0, one[3], gate_last)
-        quantize_x(1, one[2], after="gate_last")
-        for t in range(1, PACK):
-            gather(g1_3[:, t, :], 1, t, one[3])
-        first_layer(2)
+        def quantize_head(first, count):
+            cols = blocks(first, count)
+            quantize_x(bf_flat[:, cols, :], codes_head[:, cols], scales_head[:, cols], held[first : first + count])
 
+        def quantize_last(e):
+            x_bf = new_tile(f"bf_last_{e}", [P, C, PACK], BF16, "ident_0" if e == PAIR else None)
+            interleave(x_bf[:], g2[:, :, slots(one[e % PAIR])])
+            codes = new_tile(f"codes_last_{e}", [P, C], U32)
+            scales = new_tile(f"scales_last_{e}", [P, C], U8)
+            quantize_x(x_bf[:], codes[:], scales[:], [(2, e)])
+
+        quantize_head(0, 2)
+        quantize_last(0)
+        quantize_head(2, 4)
+        quantize_last(1)
+        first_product(0)
+        turn_h(0)
+        first_product(1)
+        second_layer(0)
+        turn_h(1)
         second_layer(1)
-        copy_y(1, first_rows)
-        copy_y(1, other_rows, after="h_slot_2")
-        interleave(g1_3, 1, one[3], after="h_slot_1")
-        quantize_x(1, one[3])
-        g2_3 = new_tile("g2_3", [P, PACK, C], F32)
+
         for t in range(PACK):
-            gather(g2_3[:, t, :], 2, t, one[3])
-        interleave(g2_3[:], 2, one[3])
-        quantize_x(2, one[3], after="h_bf_0")
-        first_layer(3)
-        scatter(0, 0)
-        second_layer(2, after="y_0_0")
+            gather(g2[:, t, slots(one[0])], 2, t, one[2], gate_sb[:, slots(one[2])])
+        quantize_head(6, 1)
+        for t in range(PACK):
+            gather(g2[:, t, slots(one[1])], 1, t, one[3], gate_sb[:, slots(one[3])])
+        quantize_last(2)
+        copy_y(0, range(0, 2))
+
+        bf_3 = new_tile("bf_3", [P, 2 * C, PACK], BF16, "w1_1")
+        interleave(bf_3[:, blocks(0, 1), :], g2[:, :, slots(one[1])])
+        g2_3 = new_tile("g2_3", [P, PACK, C], F32, "h_bf_0")
+        for t in range(PACK):
+            gather(g2_3[:, t, :], 2, t, one[3], gate_sb[:, slots(one[3])])
+        interleave(bf_3[:, blocks(1, 1), :], g2_3[:])
+        codes_3 = new_tile("codes_3", [P, 2 * C], U32)
+        scales_3 = new_tile("scales_3", [P, 2 * C], U8)
+        quantize_x(bf_3[:], codes_3[:], scales_3[:], [(1, 3), (2, 3)])
+        copy_y(0, range(2, 3), after="g2_3")
+        copy_y(1, first_rows)
+        first_product(2)
+        turn_h(2)
+        second_layer(2)
+        copy_y(1, other_rows, after="ident_2")
         copy_y(2, first_rows)
-        copy_y(2, other_rows, after="h_slot_3")
+        first_product(3)
+        turn_h(3)
         second_layer(3)
-        copy_y(3, range(0, N_TILES))
+        copy_y(2, other_rows, after="ident_3")
+        copy_y(3, first_rows)
+        copy_y(3, other_rows)
 
         for e in every:
             for c in range(N_TILES):
-                if (c, e) != (0, 0):
-                    scatter(c, e)
+                scatter(c, e)
                 if e == E - 1:
                     nc.sync.dma_start(out=out[c * P : (c + 1) * P, :], in_=out_sb[c][:])

@@ -48,13 +48,9 @@ def tile_moe_pre_mlp_relu_kernel(tc, xT, w1_words, w1_scales, w2_words, w2_scale
         gate_sb = new_tile("gate_sb", [P, SLOTS], F32)
         gate_col = new_tile("gate_col", [P, PAIR], F32)
         x_rows = [[keep.tile([P, T], F32, name=f"x_rows_{s}_{t}") for t in range(PACK)] for s in range(PASSES)]
-        w1_first = new_tile("w1_first", [P, 1, 2 * H], U8)
-        w1_sb = [new_tile(f"w1_{e}", [P, PASSES - (e == 0), 2 * H], U8) for e in range(E)]
-        w1_pass = {(s, e): w1_sb[e][:, s, :] for e in range(1, E) for s in range(PASSES)}
-        w1_pass[0, 0] = w1_first[:, 0, :]
-        for s in range(1, PASSES):
-            w1_pass[s, 0] = w1_sb[0][:, s - 1, :]
-        w1_plane = [new_tile(f"w1_plane_{half}", [P, PAIR * PASSES, H], U8) for half in range(2)]
+        w1_pass = {}
+        plane_groups = [range(0, 1), range(1, 2), range(2, E)]
+        w1_plane = [new_tile(f"w1_plane_{g.start}", [P, len(g) * PASSES, H], U8) for g in plane_groups]
         w2_early = [new_tile(f"w2_{e}", [P, 1, 2 * N], U8) for e in range(PAIR)]
         w2_late = new_tile("w2_late", [P, PAIR, 2 * N], U8)
         w2_plane = new_tile("w2_plane", [P, E, N], U8)
@@ -63,6 +59,7 @@ def tile_moe_pre_mlp_relu_kernel(tc, xT, w1_words, w1_scales, w2_words, w2_scale
 
         x_mx = {}
         a_acc, turned, y_acc = {}, {}, {}
+        h_words = {}
         y_sb = {}
 
         def slots(experts, first=0):
@@ -82,9 +79,12 @@ def tile_moe_pre_mlp_relu_kernel(tc, xT, w1_words, w1_scales, w2_words, w2_scale
             for r in range(SCALE_ROWS):
                 nc.sync.dma_start(out=plane[r:P:32, :, :].bitcast(I32), in_=rows[r, :, passes, :].bitcast(I32))
 
-        def load_w1(tile, e, passes):
+        def load_w1(e, passes):
+            tile = new_tile(f"w1_{e}_{passes.start}", [P, len(passes), 2 * H], U8)
             words = w1_words[e].rearrange("s p b -> p s b")
-            nc.sync.dma_start(out=tile[:].bitcast(I32), in_=words[:, passes, :].bitcast(I32))
+            nc.sync.dma_start(out=tile[:].bitcast(I32), in_=words[:, passes.start : passes.stop, :].bitcast(I32))
+            for s in passes:
+                w1_pass[s, e] = tile[:, s - passes.start, :]
 
         def load_w2(tile, experts):
             words = w2_words.rearrange("e s p b -> p (e s) b")
@@ -114,38 +114,39 @@ def tile_moe_pre_mlp_relu_kernel(tc, xT, w1_words, w1_scales, w2_words, w2_scale
                 x_mx[key] = (codes[:, blocks(b, 1)], scales[:, blocks(b, 1)])
 
         def first_product(e):
-            a_acc[e] = psum.tile([P, H], F32, name=f"a_acc_{e}", tag="a_acc")
+            a_acc[e] = psum.tile([P, H], F32, name=f"a_acc_{e}", tag=f"a_acc_{e % 2 if e < PAIR else 0}")
             for s in range(PASSES):
                 nc.tensor.matmul_mx(
                     out=a_acc[e][:],
                     lhsT=x_mx[s, e][0].bitcast(FP8X4),
                     lhsT_scale=x_mx[s, e][1],
                     rhs=w1_pass[s, e].bitcast(FP4X4),
-                    rhs_scale=w1_plane[e // PAIR][:, (e % PAIR) * PASSES + s, :],
+                    rhs_scale=w1_plane[min(e, PAIR)][:, max(e - PAIR, 0) * PASSES + s, :],
                     start=(s == 0),
                     stop=(s == PASSES - 1),
                 )
 
-        def turn_h(e):
+        def turn_h(e, h_bf=None):
             h_slot = new_tile(f"h_slot_{e}", [P, H], BF16)
-            nc.scalar.activation(
-                out=h_slot[:].rearrange("j (u p d) -> j u p d", u=2, d=PAIR),
-                in_=a_acc[e][:].rearrange("j (p u d) -> j u p d", u=2, d=PAIR),
-                func=RELU,
-            )
             turned[e] = ring.tile([P, 2, C], F32, name="turned")
             for u in range(2):
+                nc.scalar.activation(
+                    out=h_slot[:].rearrange("j (u p d) -> j u p d", u=2, d=PAIR)[:, u],
+                    in_=a_acc[e][:].rearrange("j (p u d) -> j u p d", u=2, d=PAIR)[:, u],
+                    func=RELU,
+                )
+            for u in range(2):
                 nc.tensor.transpose(turned[e][:, u, :], h_slot[:].bitcast(F32)[:, u * P : (u + 1) * P], ident[e][:])
-            h_bf = new_tile(f"h_bf_{e}", [P, C * PACK], BF16)
+            h_words[e] = new_tile(f"h_bf_{e}", [P, C * PAIR], F32)[:] if h_bf is None else h_bf
             nc.scalar.copy(
-                out=h_bf[:].bitcast(F32).rearrange("p (j u) -> p j u", u=2),
+                out=h_words[e].rearrange("p (j u) -> p j u", u=2),
                 in_=turned[e][:].rearrange("p u j -> p j u"),
             )
 
         def second_layer(e, after=None):
             codes = new_tile(f"h_codes_{e}", [P, C], U32, after)
             scales = new_tile(f"h_scales_{e}", [P, C], U8)
-            nc.vector.quantize_mx(out=codes[:].bitcast(FP8X4), scales=scales[:], in_=tiles[f"h_bf_{e}"][:])
+            nc.vector.quantize_mx(out=codes[:].bitcast(FP8X4), scales=scales[:], in_=h_words[e].bitcast(BF16))
             w2_e = w2_early[e][:, 0, :] if e < PAIR else w2_late[:, e - PAIR, :]
             y_acc[e] = psum.tile([P, N_TILES, C], F32, name=f"y_acc_{e}")
             for c in range(N_TILES):
@@ -173,31 +174,32 @@ def tile_moe_pre_mlp_relu_kernel(tc, xT, w1_words, w1_scales, w2_words, w2_scale
         one = [range(e, e + 1) for e in range(E)]
         first_rows, other_rows = range(0, 1), range(1, N_TILES)
 
-        for plane in [w1_plane[1], w1_plane[0], w2_plane]:
+        for plane in w1_plane + [w2_plane]:
             nc.vector.memset(plane[:].bitcast(I32), 0)
-        zeros = w1_plane[1][:].rearrange("p s i -> p (s i)").bitcast(F32)
-        nc.scalar.activation(out=out_sb[0][:], in_=zeros, func=RELU)
+        nc.vector.memset(out_sb[0][:], 0.0)
         make_identity(nc, ident[0][:])
 
-        nc.sync.dma_start(out=gate_col[:], in_=gate[0, slots(early)].rearrange("(p m) -> p m", m=PAIR))
         load_x(0, 0)
+        nc.sync.dma_start(out=gate_col[:], in_=gate[0, slots(early)].rearrange("(p m) -> p m", m=PAIR))
         nc.sync.dma_start(offsets[:], offs)
         load_gate(late)
         for s in range(PASSES):
             for t in range(PACK):
                 if (s, t) != (0, 0):
                     load_x(s, t)
-        load_plane(w1_plane[0], w1_scales, slice(0, PAIR * PASSES))
-        load_w1(w1_first, 0, slice(0, 1))
-        load_w1(w1_sb[0], 0, slice(1, PASSES))
+        load_plane(w1_plane[0], w1_scales, slice(0, PASSES))
+        load_w1(0, range(0, 1))
+        load_w1(0, range(1, PASSES))
+        load_plane(w1_plane[1], w1_scales, slice(PASSES, PAIR * PASSES))
+        load_w1(1, range(0, 2))
         load_plane(w2_plane, w2_scales, slice(0, E))
-        load_w1(w1_sb[1], 1, slice(0, PASSES))
+        load_w1(1, range(2, PASSES))
         load_w2(w2_early[0], one[0])
-        load_plane(w1_plane[1], w1_scales, slice(PAIR * PASSES, E * PASSES))
-        for e in late:
-            load_w1(w1_sb[e], e, slice(0, PASSES))
-        load_w2(w2_early[1], one[1])
+        load_plane(w1_plane[2], w1_scales, slice(PAIR * PASSES, E * PASSES))
+        load_w1(2, range(0, PASSES))
         load_w2(w2_late, late)
+        load_w2(w2_early[1], one[1])
+        load_w1(3, range(0, PASSES))
 
         spread = ring.tile([P, 2, C], F32, name="turned")
         for m in range(PAIR):
@@ -208,12 +210,13 @@ def tile_moe_pre_mlp_relu_kernel(tc, xT, w1_words, w1_scales, w2_words, w2_scale
         for e in range(1, E):
             nc.scalar.copy(out=ident[e][:], in_=ident[0][:])
         for c in other_rows:
-            nc.gpsimd.memset(out_sb[c][:], 0.0)
+            nc.scalar.activation(out=out_sb[c][:], in_=out_sb[0][:], func=RELU, scale=own_gate[:, 0:1])
 
         g0 = new_tile("g0", [P, PACK, SLOTS], F32)
-        gather(g0[:, 0, slots(late)], 0, 0, late, gate_sb[:, slots(late)])
-        gather(g0[:, 0, slots(early)], 0, 0, early, gate_sb[:, slots(early)])
-        for t in range(1, PACK):
+        for half in (late, early):
+            for t in range(2):
+                gather(g0[:, t, slots(half)], 0, t, half, gate_sb[:, slots(half)])
+        for t in range(2, PACK):
             gather(g0[:, t, :], 0, t, every, gate_sb[:])
         held = [(s, e) for e in every for s in range(2)][:-1]
         bf_head = new_tile("bf_head", [P, E, 2, C, PACK], BF16)
@@ -239,7 +242,7 @@ def tile_moe_pre_mlp_relu_kernel(tc, xT, w1_words, w1_scales, w2_words, w2_scale
             quantize_x(bf_flat[:, cols, :], codes_head[:, cols], scales_head[:, cols], held[first : first + count])
 
         def quantize_last(e):
-            x_bf = new_tile(f"bf_last_{e}", [P, C, PACK], BF16, "ident_0" if e == PAIR else None)
+            x_bf = new_tile(f"bf_last_{e}", [P, C, PACK], BF16, "w1_0_1" if e == PAIR else None)
             interleave(x_bf[:], g2[:, :, slots(one[e % PAIR])])
             codes = new_tile(f"codes_last_{e}", [P, C], U32)
             scales = new_tile(f"scales_last_{e}", [P, C], U8)
@@ -250,7 +253,8 @@ def tile_moe_pre_mlp_relu_kernel(tc, xT, w1_words, w1_scales, w2_words, w2_scale
         quantize_head(2, 4)
         quantize_last(1)
         first_product(0)
-        turn_h(0)
+        g2_3 = new_tile("g2_3", [P, PACK * C], F32, "bf_last_1")
+        turn_h(0, g2_3[:, blocks(2, 2)])
         first_product(1)
         second_layer(0)
         turn_h(1)
@@ -262,14 +266,14 @@ def tile_moe_pre_mlp_relu_kernel(tc, xT, w1_words, w1_scales, w2_words, w2_scale
         for t in range(PACK):
             gather(g2[:, t, slots(one[1])], 1, t, one[3], gate_sb[:, slots(one[3])])
         quantize_last(2)
-        copy_y(0, range(0, 2))
+        copy_y(0, range(0, 1))
+        copy_y(0, range(1, 2))
 
-        bf_3 = new_tile("bf_3", [P, 2 * C, PACK], BF16, "w1_1")
+        bf_3 = new_tile("bf_3", [P, 2 * C, PACK], BF16, "h_codes_0")
         interleave(bf_3[:, blocks(0, 1), :], g2[:, :, slots(one[1])])
-        g2_3 = new_tile("g2_3", [P, PACK, C], F32, "h_bf_0")
         for t in range(PACK):
-            gather(g2_3[:, t, :], 2, t, one[3], gate_sb[:, slots(one[3])])
-        interleave(bf_3[:, blocks(1, 1), :], g2_3[:])
+            gather(g2_3[:, blocks(t, 1)], 2, t, one[3], gate_sb[:, slots(one[3])])
+        interleave(bf_3[:, blocks(1, 1), :], g2_3[:].rearrange("p (t c) -> p t c", t=PACK))
         codes_3 = new_tile("codes_3", [P, 2 * C], U32)
         scales_3 = new_tile("scales_3", [P, 2 * C], U8)
         quantize_x(bf_3[:], codes_3[:], scales_3[:], [(1, 3), (2, 3)])

@@ -176,11 +176,12 @@ def tile_moe_pre_mlp_relu_kernel(tc, xT, w1_words, w1_scales, w2_words, w2_scale
 
         for plane in w1_plane + [w2_plane]:
             nc.vector.memset(plane[:].bitcast(I32), 0)
-        nc.vector.memset(out_sb[0][:], 0.0)
         make_identity(nc, ident[0][:])
+        for c in range(N_TILES):
+            nc.gpsimd.memset(out_sb[c][:], 0.0)
 
-        load_x(0, 0)
         nc.sync.dma_start(out=gate_col[:], in_=gate[0, slots(early)].rearrange("(p m) -> p m", m=PAIR))
+        load_x(0, 0)
         nc.sync.dma_start(offsets[:], offs)
         load_gate(late)
         for s in range(PASSES):
@@ -209,14 +210,11 @@ def tile_moe_pre_mlp_relu_kernel(tc, xT, w1_words, w1_scales, w2_words, w2_scale
         nc.scalar.copy(out=own_gate[:], in_=gate_sb[:, slots(one[0])])
         for e in range(1, E):
             nc.scalar.copy(out=ident[e][:], in_=ident[0][:])
-        for c in other_rows:
-            nc.scalar.activation(out=out_sb[c][:], in_=out_sb[0][:], func=RELU, scale=own_gate[:, 0:1])
 
         g0 = new_tile("g0", [P, PACK, SLOTS], F32)
         for half in (late, early):
-            for t in range(2):
-                gather(g0[:, t, slots(half)], 0, t, half, gate_sb[:, slots(half)])
-        for t in range(2, PACK):
+            gather(g0[:, 0, slots(half)], 0, 0, half, gate_sb[:, slots(half)])
+        for t in range(1, PACK):
             gather(g0[:, t, :], 0, t, every, gate_sb[:])
         held = [(s, e) for e in every for s in range(2)][:-1]
         bf_head = new_tile("bf_head", [P, E, 2, C, PACK], BF16)
@@ -287,12 +285,18 @@ def tile_moe_pre_mlp_relu_kernel(tc, xT, w1_words, w1_scales, w2_words, w2_scale
         first_product(3)
         turn_h(3)
         second_layer(3)
-        copy_y(2, other_rows, after="ident_3")
+        copy_y(2, range(1, 2), after="ident_3")
+        y_last = new_tile("y_last", [P, PAIR, C], F32)
         copy_y(3, first_rows)
-        copy_y(3, other_rows)
+        copy_y(3, range(1, 2))
+        for e in late:
+            nc.scalar.copy(out=y_last[:, e - PAIR, :], in_=y_acc[e][:, N_TILES - 1, :])
 
         for e in every:
-            for c in range(N_TILES):
+            for c in range(N_TILES if e < PAIR else N_TILES - 1):
                 scatter(c, e)
                 if e == E - 1:
                     nc.sync.dma_start(out=out[c * P : (c + 1) * P, :], in_=out_sb[c][:])
+        c = N_TILES - 1
+        nc.vector.tensor_copy(out_sb[c][:].indirect(entries(late)), y_last[:].rearrange("p e j -> p (e j)"))
+        nc.sync.dma_start(out=out[c * P : (c + 1) * P, :], in_=out_sb[c][:])

@@ -285,18 +285,12 @@ def tile_moe_pre_mlp_relu_kernel(tc, xT, w1_words, w1_scales, w2_words, w2_scale
         first_product(3)
         turn_h(3)
         second_layer(3)
-        copy_y(2, range(1, 2), after="ident_3")
-        y_last = new_tile("y_last", [P, PAIR, C], F32)
+        copy_y(2, other_rows, after="ident_3")
         copy_y(3, first_rows)
-        copy_y(3, range(1, 2))
-        for e in late:
-            nc.scalar.copy(out=y_last[:, e - PAIR, :], in_=y_acc[e][:, N_TILES - 1, :])
+        copy_y(3, other_rows)
 
         for e in every:
-            for c in range(N_TILES if e < PAIR else N_TILES - 1):
+            for c in range(N_TILES):
                 scatter(c, e)
                 if e == E - 1:
                     nc.sync.dma_start(out=out[c * P : (c + 1) * P, :], in_=out_sb[c][:])
-        c = N_TILES - 1
-        nc.vector.tensor_copy(out_sb[c][:].indirect(entries(late)), y_last[:].rearrange("p e j -> p (e j)"))
-        nc.sync.dma_start(out=out[c * P : (c + 1) * P, :], in_=out_sb[c][:])

@@ -46,7 +46,6 @@ def tile_moe_pre_mlp_relu_kernel(tc, xT, w1_words, w1_scales, w2_words, w2_scale
 
         offsets = keep.tile([P, SLOTS // LIST_ROWS], U16, name="offsets")
         gate_sb = new_tile("gate_sb", [P, SLOTS], F32)
-        gate_col = new_tile("gate_col", [P, PAIR], F32)
         x_rows = [[keep.tile([P, T], F32, name=f"x_rows_{s}_{t}") for t in range(PACK)] for s in range(PASSES)]
         w1_pass = {}
         plane_groups = [range(0, 1), range(1, 2), range(2, E)]
@@ -180,10 +179,10 @@ def tile_moe_pre_mlp_relu_kernel(tc, xT, w1_words, w1_scales, w2_words, w2_scale
         for c in range(N_TILES):
             nc.gpsimd.memset(out_sb[c][:], 0.0)
 
-        nc.sync.dma_start(out=gate_col[:], in_=gate[0, slots(early)].rearrange("(p m) -> p m", m=PAIR))
         load_x(0, 0)
         nc.sync.dma_start(offsets[:], offs)
         load_gate(late)
+        load_gate(early)
         for s in range(PASSES):
             for t in range(PACK):
                 if (s, t) != (0, 0):
@@ -202,10 +201,6 @@ def tile_moe_pre_mlp_relu_kernel(tc, xT, w1_words, w1_scales, w2_words, w2_scale
         load_w2(w2_early[1], one[1])
         load_w1(3, range(0, PASSES))
 
-        spread = ring.tile([P, 2, C], F32, name="turned")
-        for m in range(PAIR):
-            nc.tensor.transpose(spread[:, m, :], gate_col[:, m : m + 1].to_broadcast([P, P]), ident[0][:])
-        nc.scalar.copy(out=gate_sb[:, slots(early)].rearrange("p (j m) -> p j m", m=PAIR), in_=spread[:].rearrange("p m j -> p j m"))
         own_gate = new_tile("own_gate_0", [P, C], F32)
         nc.scalar.copy(out=own_gate[:], in_=gate_sb[:, slots(one[0])])
         for e in range(1, E):
@@ -252,7 +247,9 @@ def tile_moe_pre_mlp_relu_kernel(tc, xT, w1_words, w1_scales, w2_words, w2_scale
         quantize_last(1)
         first_product(0)
         g2_3 = new_tile("g2_3", [P, PACK * C], F32, "bf_last_1")
-        turn_h(0, g2_3[:, blocks(2, 2)])
+        turn_h(0)
+        gate_last = new_tile("gate_last", [P, C], F32, "ident_0")
+        nc.scalar.copy(out=gate_last[:], in_=gate_sb[:, slots(one[3])])
         first_product(1)
         second_layer(0)
         turn_h(1)
@@ -270,7 +267,7 @@ def tile_moe_pre_mlp_relu_kernel(tc, xT, w1_words, w1_scales, w2_words, w2_scale
         bf_3 = new_tile("bf_3", [P, 2 * C, PACK], BF16, "h_codes_0")
         interleave(bf_3[:, blocks(0, 1), :], g2[:, :, slots(one[1])])
         for t in range(PACK):
-            gather(g2_3[:, blocks(t, 1)], 2, t, one[3], gate_sb[:, slots(one[3])])
+            gather(g2_3[:, blocks(t, 1)], 2, t, one[3], gate_last[:])
         interleave(bf_3[:, blocks(1, 1), :], g2_3[:].rearrange("p (t c) -> p t c", t=PACK))
         codes_3 = new_tile("codes_3", [P, 2 * C], U32)
         scales_3 = new_tile("scales_3", [P, 2 * C], U8)

@@ -18,6 +18,7 @@ FP8X4 = mybir.dt.float8_e4m3fn_x4
 FP4X4 = mybir.dt.float4_e2m1fn_x4
 MULT = mybir.AluOpType.mult
 RELU = mybir.ActivationFunctionType.Relu
+COPY = mybir.ActivationFunctionType.Copy
 
 P = 128
 PACK = 4
@@ -34,7 +35,6 @@ def tile_moe_pre_mlp_relu_kernel(tc, xT, w1_words, w1_scales, w2_words, w2_scale
     with ExitStack() as ctx:
         keep = ctx.enter_context(tc.tile_pool(name="keep", bufs=1))
         psum = ctx.enter_context(tc.psum_pool(name="psum", bufs=1))
-        ring = ctx.enter_context(tc.psum_pool(name="ring", bufs=2))
 
         tiles = {}
         place = {}
@@ -46,20 +46,21 @@ def tile_moe_pre_mlp_relu_kernel(tc, xT, w1_words, w1_scales, w2_words, w2_scale
 
         offsets = keep.tile([P, SLOTS // LIST_ROWS], U16, name="offsets")
         gate_sb = new_tile("gate_sb", [P, SLOTS], F32)
-        x_rows = [[keep.tile([P, T], F32, name=f"x_rows_{s}_{t}") for t in range(PACK)] for s in range(PASSES)]
+        x_rows = [[new_tile(f"x_rows_{s}_{t}", [P, T], F32) for t in range(PACK)] for s in range(PASSES)]
         w1_pass = {}
         plane_groups = [range(0, 1), range(1, 2), range(2, E)]
         w1_plane = [new_tile(f"w1_plane_{g.start}", [P, len(g) * PASSES, H], U8) for g in plane_groups]
-        w2_early = [new_tile(f"w2_{e}", [P, 1, 2 * N], U8) for e in range(PAIR)]
-        w2_late = new_tile("w2_late", [P, PAIR, 2 * N], U8)
-        w2_plane = new_tile("w2_plane", [P, E, N], U8)
+        w2_sb = {}
+        w2_plane = [new_tile(f"w2_plane_{g.start}", [P, len(g), N], U8) for g in (range(0, 1), range(1, E))]
         out_sb = [keep.tile([P, T], F32, name=f"out_sb_{c}") for c in range(N_TILES)]
-        ident = [new_tile(f"ident_{e}", [P, P], F32) for e in range(E)]
+        ident = new_tile("ident", [P, P], F32)
 
         x_mx = {}
-        a_acc, turned, y_acc = {}, {}, {}
-        h_words = {}
-        y_sb = {}
+        a_acc, y_acc = {}, {}
+        h_slot, h_words = {}, {}
+        y_sb = new_tile("y_sb", [P, N_TILES, SLOTS], F32)
+        raw = {}
+        h_mx = {}
 
         def slots(experts, first=0):
             return slice((experts.start - first) * C, (experts.stop - first) * C)
@@ -69,9 +70,6 @@ def tile_moe_pre_mlp_relu_kernel(tc, xT, w1_words, w1_scales, w2_words, w2_scale
 
         def load_x(s, t):
             nc.sync.dma_start(out=x_rows[s][t][:], in_=xT.rearrange("(s p t) c -> s t p c", p=P, t=PACK)[s, t])
-
-        def load_gate(experts):
-            nc.sync.dma_start(out=gate_sb[:, slots(experts)], in_=gate[0:P, slots(experts)])
 
         def load_plane(plane, scales, passes):
             rows = scales.rearrange("e s (g r) i -> r g (e s) i", r=SCALE_ROWS)
@@ -85,35 +83,70 @@ def tile_moe_pre_mlp_relu_kernel(tc, xT, w1_words, w1_scales, w2_words, w2_scale
             for s in passes:
                 w1_pass[s, e] = tile[:, s - passes.start, :]
 
-        def load_w2(tile, experts):
+        def load_w2(experts):
+            tile = new_tile(f"w2_{experts.start}", [P, len(experts), 2 * N], U8)
             words = w2_words.rearrange("e s p b -> p (e s) b")
             nc.sync.dma_start(out=tile[:].bitcast(I32), in_=words[:, experts.start : experts.stop, :].bitcast(I32))
+            for e in experts:
+                w2_sb[e] = tile[:, e - experts.start, :]
 
-        def gather(dst, s, t, experts, gates):
-            nc.vector.tensor_tensor(dst, x_rows[s][t][:].indirect(entries(experts)), gates, MULT)
+        def woven(ap, order):
+            return ap.rearrange(order + " -> p c t i", i=PAIR)
 
-        def blocks(first, count):
-            return slice(first * C, (first + count) * C)
+        def gates(experts):
+            return gate_sb[:, slots(experts)]
 
-        def interleave_blocks(dst, src):
-            nc.scalar.copy(
-                out=dst.rearrange("p e (c i) t -> p e c t i", i=LINE),
-                in_=src.rearrange("p t (e c i) -> p e c t i", i=LINE, c=C // LINE),
+        def gather_gated(s, experts, after=None):
+            gated = new_tile(f"gated_{s}_{experts.start}", [P, PACK, len(experts) * C], F32, after)
+            for t in range(PACK):
+                nc.vector.tensor_tensor(gated[:, t, :], x_rows[s][t][:].indirect(entries(experts)), gates(experts), MULT)
+
+        def interleave(s, experts, x_bf=None):
+            if x_bf is None:
+                x_bf = new_tile(f"bf_{s}_{experts.start}", [P, len(experts) * C, PACK], BF16)
+            gated = tiles[f"gated_{s}_{experts.start}"]
+            nc.vector.tensor_copy(woven(x_bf[:, :, :], "p (c i) t"), woven(gated[:], "p t (c i)"))
+
+        def gather_raw(s, experts, after=None):
+            tile = new_tile(f"raw_{s}_{experts.start}", [P, PACK, len(experts) * C], F32, after)
+            for t in range(PACK):
+                nc.scalar.activation(tile[:, t, :], x_rows[s][t][:].indirect(entries(experts)), COPY)
+            for e in experts:
+                raw[s, e] = (tile, experts.start)
+
+        def gate_raw(s, experts, x_bf=None, after=None):
+            tile, base = raw[s, experts.start]
+            if x_bf is None:
+                x_bf = new_tile(f"bf_{s}_{experts.start}", [P, len(experts) * C, PACK], BF16, after)
+            per_pair = gates(experts).rearrange("p (c i) -> p c i", i=PAIR).unsqueeze(2)
+            nc.vector.tensor_tensor(
+                woven(x_bf[:, :, :], "p (c i) t"),
+                woven(tile[:, :, slots(experts, base)], "p t (c i)"),
+                per_pair.to_broadcast([P, len(experts) * C // PAIR, PACK, PAIR]),
+                MULT,
             )
 
-        def interleave(dst, src):
-            nc.scalar.copy(
-                out=dst.rearrange("p (c i) t -> p c t i", i=LINE),
-                in_=src.rearrange("p t (c i) -> p c t i", i=LINE),
-            )
+        def quantize_x(s, experts):
+            x_bf = tiles[f"bf_{s}_{experts.start}"][:]
+            codes = new_tile(f"x_codes_{s}_{experts.start}", [P, len(experts) * C], U32)
+            scales = new_tile(f"x_scales_{s}_{experts.start}", [P, len(experts) * C], U8)
+            nc.vector.quantize_mx(out=codes[:].bitcast(FP8X4), scales=scales[:], in_=x_bf.rearrange("p c t -> p (c t)"))
+            for e in experts:
+                cols = slots(range(e, e + 1), experts.start)
+                x_mx[s, e] = (codes[:, cols], scales[:, cols])
 
-        def quantize_x(x_bf, codes, scales, held):
-            nc.vector.quantize_mx(out=codes.bitcast(FP8X4), scales=scales, in_=x_bf.rearrange("p c t -> p (c t)"))
-            for b, key in enumerate(held):
-                x_mx[key] = (codes[:, blocks(b, 1)], scales[:, blocks(b, 1)])
+        def late_passes(e, after, codes_after=None):
+            x_bf = new_tile(f"bf_late_{e}", [P, 2 * C, PACK], BF16, after)
+            interleave(2, one[e], x_bf[:, C : 2 * C, :])
+            gate_raw(1, one[e], x_bf[:, 0:C, :])
+            codes = new_tile(f"late_codes_{e}", [P, 2 * C], U32, codes_after)
+            scales = new_tile(f"late_scales_{e}", [P, 2 * C], U8)
+            nc.vector.quantize_mx(out=codes[:].bitcast(FP8X4), scales=scales[:], in_=x_bf[:].rearrange("p c t -> p (c t)"))
+            for s in range(1, PASSES):
+                x_mx[s, e] = (codes[:, (s - 1) * C : s * C], scales[:, (s - 1) * C : s * C])
 
         def first_product(e):
-            a_acc[e] = psum.tile([P, H], F32, name=f"a_acc_{e}", tag=f"a_acc_{e % 2 if e < PAIR else 0}")
+            a_acc[e] = psum.tile([P, H], F32, name=f"a_acc_{e}", tag=f"bank_{e}")
             for s in range(PASSES):
                 nc.tensor.matmul_mx(
                     out=a_acc[e][:],
@@ -125,169 +158,154 @@ def tile_moe_pre_mlp_relu_kernel(tc, xT, w1_words, w1_scales, w2_words, w2_scale
                     stop=(s == PASSES - 1),
                 )
 
-        def turn_h(e, h_bf=None):
-            h_slot = new_tile(f"h_slot_{e}", [P, H], BF16)
-            turned[e] = ring.tile([P, 2, C], F32, name="turned")
+        def turn_h(e, after=None):
+            own = ident
+            if after:
+                own = new_tile(f"ident_{e}", [P, P], F32, after)
+                nc.scalar.copy(out=own[:], in_=ident[:])
+            h_slot[e] = new_tile(f"h_slot_{e}", [P, H], BF16)
+            turned = psum.tile([P, 2, C], F32, name=f"turned_{e}", tag=f"turn_{e}")
+            h_out = h_slot[e][:].rearrange("j (u p d) -> j u p d", u=2, d=PAIR)
+            a_in = a_acc[e][:].rearrange("j (p u d) -> j u p d", u=2, d=PAIR)
+            if e == 2:
+                nc.vector.tensor_scalar_max(h_out, a_in, 0.0)
+            else:
+                nc.scalar.activation(out=h_out, in_=a_in, func=RELU)
             for u in range(2):
-                nc.scalar.activation(
-                    out=h_slot[:].rearrange("j (u p d) -> j u p d", u=2, d=PAIR)[:, u],
-                    in_=a_acc[e][:].rearrange("j (p u d) -> j u p d", u=2, d=PAIR)[:, u],
-                    func=RELU,
-                )
-            for u in range(2):
-                nc.tensor.transpose(turned[e][:, u, :], h_slot[:].bitcast(F32)[:, u * P : (u + 1) * P], ident[e][:])
-            h_words[e] = new_tile(f"h_bf_{e}", [P, C * PAIR], F32)[:] if h_bf is None else h_bf
+                nc.tensor.transpose(turned[:, u, :], h_slot[e][:].bitcast(F32)[:, u * P : (u + 1) * P], own[:])
+            h_words[e] = new_tile(f"h_bf_{e}", [P, C * PAIR], F32)
             nc.scalar.copy(
-                out=h_words[e].rearrange("p (j u) -> p j u", u=2),
-                in_=turned[e][:].rearrange("p u j -> p j u"),
+                out=h_words[e][:].rearrange("p (j u) -> p j u", u=2),
+                in_=turned[:].rearrange("p u j -> p j u"),
             )
 
-        def second_layer(e, after=None):
-            codes = new_tile(f"h_codes_{e}", [P, C], U32, after)
+        def quantize_h(e):
+            codes = new_tile(f"h_codes_{e}", [P, C], U32)
             scales = new_tile(f"h_scales_{e}", [P, C], U8)
-            nc.vector.quantize_mx(out=codes[:].bitcast(FP8X4), scales=scales[:], in_=h_words[e].bitcast(BF16))
-            w2_e = w2_early[e][:, 0, :] if e < PAIR else w2_late[:, e - PAIR, :]
-            y_acc[e] = psum.tile([P, N_TILES, C], F32, name=f"y_acc_{e}")
+            nc.vector.quantize_mx(out=codes[:].bitcast(FP8X4), scales=scales[:], in_=h_words[e][:].bitcast(BF16))
+            h_mx[e] = (codes, scales)
+
+        def second_layer(e):
+            codes, scales = h_mx[e]
+            y_acc[e] = psum.tile([P, N_TILES, C], F32, name=f"y_acc_{e}", tag=f"bank_{e}")
             for c in range(N_TILES):
                 nc.tensor.matmul_mx(
                     out=y_acc[e][:, c, :],
-                    lhsT=w2_e[:, 2 * P * c : 2 * P * (c + 1)].bitcast(FP4X4),
-                    lhsT_scale=w2_plane[:, e, P * c : P * (c + 1)],
+                    lhsT=w2_sb[e][:, 2 * P * c : 2 * P * (c + 1)].bitcast(FP4X4),
+                    lhsT_scale=w2_plane[min(e, 1)][:, max(e - 1, 0), P * c : P * (c + 1)],
                     rhs=codes[:].bitcast(FP8X4),
                     rhs_scale=scales[:],
                     start=True,
                     stop=True,
                 )
 
-        def copy_y(e, row_tiles, after=None):
-            y = new_tile(f"y_{e}_{row_tiles.start}", [P, len(row_tiles), C], F32, after)
-            nc.scalar.copy(out=y[:], in_=y_acc[e][:, row_tiles.start : row_tiles.stop, :])
-            for c in row_tiles:
-                y_sb[c, e] = y[:, c - row_tiles.start, :]
+        def copy_y(e, row_tiles, dst):
+            nc.scalar.copy(out=dst, in_=y_acc[e][:, row_tiles.start : row_tiles.stop, :])
 
-        def scatter(c, e):
-            nc.vector.tensor_copy(out_sb[c][:].indirect(entries(range(e, e + 1))), y_sb[c, e])
+        def scatter(c, experts, on_vector, y=None):
+            window = out_sb[c][:].indirect(entries(experts))
+            y = y_sb[:, c, slots(experts)] if y is None else y
+            if on_vector:
+                nc.vector.tensor_copy(window, y)
+            else:
+                nc.scalar.activation(window, y, COPY)
 
-        every, early, late = range(0, E), range(0, PAIR), range(PAIR, E)
-        three = range(0, E - 1)
+        def store(c, queue):
+            queue.dma_start(out=out[c * P : (c + 1) * P, :], in_=out_sb[c][:])
+
         one = [range(e, e + 1) for e in range(E)]
-        first_rows, other_rows = range(0, 1), range(1, N_TILES)
+        early, late = range(0, PAIR), range(PAIR, E)
 
-        for plane in w1_plane + [w2_plane]:
+        for plane in w1_plane + w2_plane:
             nc.vector.memset(plane[:].bitcast(I32), 0)
-        make_identity(nc, ident[0][:])
+        make_identity(nc, ident[:])
         for c in range(N_TILES):
             nc.gpsimd.memset(out_sb[c][:], 0.0)
 
+        gate_col = new_tile("gate_col", [P, PACK], F32)
+        nc.sync.dma_start(out=gate_col[:], in_=gate[0:1, :].rearrange("o (p q) -> p (o q)", q=PACK))
         load_x(0, 0)
         nc.sync.dma_start(offsets[:], offs)
-        load_gate(late)
-        load_gate(early)
-        for s in range(PASSES):
-            for t in range(PACK):
-                if (s, t) != (0, 0):
-                    load_x(s, t)
+        for t in range(1, PACK):
+            load_x(0, t)
+        for t in range(PACK):
+            load_x(1, t)
+        load_x(2, 0)
         load_plane(w1_plane[0], w1_scales, slice(0, PASSES))
+        load_x(2, 1)
+        load_x(2, 2)
+        load_plane(w2_plane[0], w2_scales, slice(0, 1))
+        load_x(2, 3)
         load_w1(0, range(0, 1))
         load_w1(0, range(1, PASSES))
         load_plane(w1_plane[1], w1_scales, slice(PASSES, PAIR * PASSES))
         load_w1(1, range(0, 2))
-        load_plane(w2_plane, w2_scales, slice(0, E))
         load_w1(1, range(2, PASSES))
-        load_w2(w2_early[0], one[0])
         load_plane(w1_plane[2], w1_scales, slice(PAIR * PASSES, E * PASSES))
-        load_w1(2, range(0, PASSES))
-        load_w2(w2_late, late)
-        load_w2(w2_early[1], one[1])
-        load_w1(3, range(0, PASSES))
+        load_w1(2, range(0, 2))
+        load_w1(2, range(2, PASSES))
+        load_w2(one[0])
+        load_w1(3, range(0, 2))
+        load_w1(3, range(2, PASSES))
+        load_plane(w2_plane[1], w2_scales, slice(1, E))
+        load_w2(range(1, E))
 
-        own_gate = new_tile("own_gate_0", [P, C], F32)
-        nc.scalar.copy(out=own_gate[:], in_=gate_sb[:, slots(one[0])])
-        for e in range(1, E):
-            nc.scalar.copy(out=ident[e][:], in_=ident[0][:])
+        spread = psum.tile([P, PACK, P], F32, name="spread", tag="turn_3")
+        for q in range(PACK):
+            nc.tensor.transpose(spread[:, q, :], gate_col[:, q : q + 1].to_broadcast([P, P]), ident[:])
+        nc.vector.tensor_copy(gate_sb[:].rearrange("m (p q) -> m p q", q=PACK), spread[:].rearrange("m q p -> m p q"))
 
-        g0 = new_tile("g0", [P, PACK, SLOTS], F32)
-        for half in (late, early):
-            gather(g0[:, 0, slots(half)], 0, 0, half, gate_sb[:, slots(half)])
-        for t in range(1, PACK):
-            gather(g0[:, t, :], 0, t, every, gate_sb[:])
-        held = [(s, e) for e in every for s in range(2)][:-1]
-        bf_head = new_tile("bf_head", [P, E, 2, C, PACK], BF16)
-        bf_flat = bf_head[:].rearrange("p e s c t -> p (e s c) t")
-        interleave_blocks(bf_head[:, 0:PAIR, 0], g0[:, :, slots(early)])
-        interleave_blocks(bf_head[:, PAIR:E, 0], g0[:, :, slots(late)])
+        gather_raw(0, late)
+        gather_gated(0, early)
+        interleave(0, early)
+        gate_raw(0, late)
+        quantize_x(0, early)
+        quantize_x(0, late)
+        gather_raw(1, range(1, 3))
+        gather_raw(1, one[3])
+        gather_gated(1, one[0])
+        interleave(1, one[0])
+        gate_raw(1, range(1, 3))
+        quantize_x(1, one[0])
+        quantize_x(1, range(1, 3))
+        gather_raw(2, range(1, 3))
+        gather_raw(2, one[3])
+        gather_gated(2, one[0])
+        interleave(2, one[0])
+        quantize_x(2, one[0])
+        gate_raw(1, one[3], after="gated_2_0")
+        gate_raw(2, one[1], after="bf_2_0")
+        quantize_x(1, one[3])
+        gate_raw(2, one[2], after="bf_1_3")
+        quantize_x(2, one[1])
+        quantize_x(2, one[2])
+        gate_raw(2, one[3], after="bf_2_1")
 
-        g1 = new_tile("g1", [P, PACK, len(three) * C], F32)
-        for t in range(PACK):
-            gather(g1[:, t, :], 1, t, three, gate_sb[:, slots(three)])
-        interleave(bf_head[:, 0, 1], g1[:, :, slots(one[0])])
-        interleave_blocks(bf_head[:, 1 : len(three), 1], g1[:, :, slots(range(1, E - 1))])
-        g2 = new_tile("g2", [P, PACK, PAIR * C], F32)
-        for t in range(PACK - 1):
-            gather(g2[:, t, :], 2, t, early, gate_sb[:, slots(early)])
-        for e in early:
-            gather(g2[:, PACK - 1, slots(one[e])], 2, PACK - 1, one[e], own_gate[:] if e == 0 else gate_sb[:, slots(one[e])])
-        codes_head = new_tile("codes_head", [P, len(held) * C], U32, after="own_gate_0")
-        scales_head = new_tile("scales_head", [P, len(held) * C], U8)
-
-        def quantize_head(first, count):
-            cols = blocks(first, count)
-            quantize_x(bf_flat[:, cols, :], codes_head[:, cols], scales_head[:, cols], held[first : first + count])
-
-        def quantize_last(e):
-            x_bf = new_tile(f"bf_last_{e}", [P, C, PACK], BF16, "w1_0_1" if e == PAIR else None)
-            interleave(x_bf[:], g2[:, :, slots(one[e % PAIR])])
-            codes = new_tile(f"codes_last_{e}", [P, C], U32)
-            scales = new_tile(f"scales_last_{e}", [P, C], U8)
-            quantize_x(x_bf[:], codes[:], scales[:], [(2, e)])
-
-        quantize_head(0, 2)
-        quantize_last(0)
-        quantize_head(2, 4)
-        quantize_last(1)
         first_product(0)
-        g2_3 = new_tile("g2_3", [P, PACK * C], F32, "bf_last_1")
-        turn_h(0)
-        gate_last = new_tile("gate_last", [P, C], F32, "ident_0")
-        nc.scalar.copy(out=gate_last[:], in_=gate_sb[:, slots(one[3])])
         first_product(1)
-        second_layer(0)
-        turn_h(1)
-        second_layer(1)
-
-        for t in range(PACK):
-            gather(g2[:, t, slots(one[0])], 2, t, one[2], gate_sb[:, slots(one[2])])
-        quantize_head(6, 1)
-        for t in range(PACK):
-            gather(g2[:, t, slots(one[1])], 1, t, one[3], gate_sb[:, slots(one[3])])
-        quantize_last(2)
-        copy_y(0, range(0, 1))
-        copy_y(0, range(1, 2))
-
-        bf_3 = new_tile("bf_3", [P, 2 * C, PACK], BF16, "h_codes_0")
-        interleave(bf_3[:, blocks(0, 1), :], g2[:, :, slots(one[1])])
-        for t in range(PACK):
-            gather(g2_3[:, blocks(t, 1)], 2, t, one[3], gate_last[:])
-        interleave(bf_3[:, blocks(1, 1), :], g2_3[:].rearrange("p (t c) -> p t c", t=PACK))
-        codes_3 = new_tile("codes_3", [P, 2 * C], U32)
-        scales_3 = new_tile("scales_3", [P, 2 * C], U8)
-        quantize_x(bf_3[:], codes_3[:], scales_3[:], [(1, 3), (2, 3)])
-        copy_y(0, range(2, 3), after="g2_3")
-        copy_y(1, first_rows)
+        turn_h(0, after="w1_1_0")
+        quantize_h(0)
+        quantize_x(2, one[3])
         first_product(2)
-        turn_h(2)
-        second_layer(2)
-        copy_y(1, other_rows, after="ident_2")
-        copy_y(2, first_rows)
+        second_layer(0)
+        copy_y(0, range(0, N_TILES), y_sb[:, :, slots(one[0])])
+        turn_h(1, after="w1_2_0")
+        quantize_h(1)
         first_product(3)
-        turn_h(3)
-        second_layer(3)
-        copy_y(2, other_rows, after="ident_3")
-        copy_y(3, first_rows)
-        copy_y(3, other_rows)
+        for e in late:
+            turn_h(e)
+            quantize_h(e)
+        for e in range(1, E):
+            second_layer(e)
+            copy_y(e, range(0, N_TILES), y_sb[:, :, slots(one[e])])
 
-        for e in every:
-            for c in range(N_TILES):
-                scatter(c, e)
-                if e == E - 1:
-                    nc.sync.dma_start(out=out[c * P : (c + 1) * P, :], in_=out_sb[c][:])
+        scatter(0, one[0], True)
+        scatter(1, one[0], True)
+        scatter(0, one[1], True)
+        scatter(2, range(0, 3), True)
+        scatter(1, range(1, E), False)
+        store(1, nc.scalar)
+        scatter(2, one[3], False)
+        store(2, nc.scalar)
+        scatter(0, late, True)
+        store(0, nc.sync)

@@ -26,8 +26,9 @@ PASSES = K // (P * PACK)
 N_TILES = N // P
 LIST_ROWS = 16
 SCALE_ROWS = 4
-LINE = 4
 PAIR = 2
+HALF = E // 2
+LINE_SLOTS = 2
 
 
 def tile_moe_pre_mlp_relu_kernel(tc, xT, w1_words, w1_scales, w2_words, w2_scales, gate, offs, out):
@@ -35,6 +36,10 @@ def tile_moe_pre_mlp_relu_kernel(tc, xT, w1_words, w1_scales, w2_words, w2_scale
     with ExitStack() as ctx:
         keep = ctx.enter_context(tc.tile_pool(name="keep", bufs=1))
         psum = ctx.enter_context(tc.psum_pool(name="psum", bufs=1))
+
+        one = [range(e, e + 1) for e in range(E)]
+        early, late = range(0, HALF), range(HALF, E)
+        middle, others = range(1, E - 1), range(1, E)
 
         tiles = {}
         place = {}
@@ -45,19 +50,19 @@ def tile_moe_pre_mlp_relu_kernel(tc, xT, w1_words, w1_scales, w2_words, w2_scale
             return tiles[name]
 
         offsets = keep.tile([P, SLOTS // LIST_ROWS], U16, name="offsets")
-        gate_sb = new_tile("gate_sb", [P, SLOTS], F32)
+        gate_sb = new_tile("gate_sb", [P, HALF * C], F32)
         x_rows = [[new_tile(f"x_rows_{s}_{t}", [P, T], F32) for t in range(PACK)] for s in range(PASSES)]
         w1_pass = {}
-        plane_groups = [range(0, 1), range(1, 2), range(2, E)]
-        w1_plane = [new_tile(f"w1_plane_{g.start}", [P, len(g) * PASSES, H], U8) for g in plane_groups]
+        w1_plane = [new_tile(f"w1_plane_{g.start}", [P, len(g) * PASSES, H], U8) for g in (early, late)]
         w2_sb = {}
-        w2_plane = [new_tile(f"w2_plane_{g.start}", [P, len(g), N], U8) for g in (range(0, 1), range(1, E))]
+        w2_plane = [new_tile(f"w2_plane_{g.start}", [P, len(g), N], U8) for g in (one[0], others)]
         out_sb = [keep.tile([P, T], F32, name=f"out_sb_{c}") for c in range(N_TILES)]
         ident = new_tile("ident", [P, P], F32)
 
+        spread = psum.tile([P, SLOTS // LINE_SLOTS, LINE_SLOTS], F32, name="spread", tag=f"turn_{E - 1}")
         x_mx = {}
         a_acc, y_acc = {}, {}
-        h_slot, h_words = {}, {}
+        h_words = {}
         y_sb = new_tile("y_sb", [P, N_TILES, SLOTS], F32)
         raw = {}
         h_mx = {}
@@ -65,8 +70,8 @@ def tile_moe_pre_mlp_relu_kernel(tc, xT, w1_words, w1_scales, w2_words, w2_scale
         def slots(experts, first=0):
             return slice((experts.start - first) * C, (experts.stop - first) * C)
 
-        def entries(experts):
-            return offsets[:, experts.start * C // LIST_ROWS : experts.stop * C // LIST_ROWS]
+        def entries(cols):
+            return offsets[:, cols.start // LIST_ROWS : cols.stop // LIST_ROWS]
 
         def load_x(s, t):
             nc.sync.dma_start(out=x_rows[s][t][:], in_=xT.rearrange("(s p t) c -> s t p c", p=P, t=PACK)[s, t])
@@ -91,38 +96,34 @@ def tile_moe_pre_mlp_relu_kernel(tc, xT, w1_words, w1_scales, w2_words, w2_scale
                 w2_sb[e] = tile[:, e - experts.start, :]
 
         def woven(ap, order):
-            return ap.rearrange(order + " -> p c t i", i=PAIR)
+            return ap.rearrange(order + " -> p c t i", i=LINE_SLOTS)
 
-        def gates(experts):
-            return gate_sb[:, slots(experts)]
-
-        def gather_gated(s, experts, after=None):
-            gated = new_tile(f"gated_{s}_{experts.start}", [P, PACK, len(experts) * C], F32, after)
+        def gather_gated(s, experts):
+            cols = slots(experts)
+            gated = new_tile(f"gated_{s}_{experts.start}", [P, PACK, len(experts) * C], F32)
             for t in range(PACK):
-                nc.vector.tensor_tensor(gated[:, t, :], x_rows[s][t][:].indirect(entries(experts)), gates(experts), MULT)
+                nc.vector.tensor_tensor(gated[:, t, :], x_rows[s][t][:].indirect(entries(cols)), gate_sb[:, cols], MULT)
 
-        def interleave(s, experts, x_bf=None):
-            if x_bf is None:
-                x_bf = new_tile(f"bf_{s}_{experts.start}", [P, len(experts) * C, PACK], BF16)
+        def interleave(s, experts):
+            x_bf = new_tile(f"bf_{s}_{experts.start}", [P, len(experts) * C, PACK], BF16)
             gated = tiles[f"gated_{s}_{experts.start}"]
-            nc.vector.tensor_copy(woven(x_bf[:, :, :], "p (c i) t"), woven(gated[:], "p t (c i)"))
+            nc.vector.tensor_copy(woven(x_bf[:], "p (c i) t"), woven(gated[:], "p t (c i)"))
 
-        def gather_raw(s, experts, after=None):
-            tile = new_tile(f"raw_{s}_{experts.start}", [P, PACK, len(experts) * C], F32, after)
+        def gather_raw(s, experts):
+            tile = new_tile(f"raw_{s}_{experts.start}", [P, PACK, len(experts) * C], F32)
             for t in range(PACK):
-                nc.scalar.activation(tile[:, t, :], x_rows[s][t][:].indirect(entries(experts)), COPY)
+                nc.scalar.activation(tile[:, t, :], x_rows[s][t][:].indirect(entries(slots(experts))), COPY)
             for e in experts:
                 raw[s, e] = (tile, experts.start)
 
-        def gate_raw(s, experts, x_bf=None, after=None):
-            tile, base = raw[s, experts.start]
-            if x_bf is None:
-                x_bf = new_tile(f"bf_{s}_{experts.start}", [P, len(experts) * C, PACK], BF16, after)
-            per_pair = gates(experts).rearrange("p (c i) -> p c i", i=PAIR).unsqueeze(2)
+        def gate_raw(s, experts, after):
+            tile, first = raw[s, experts.start]
+            x_bf = new_tile(f"bf_{s}_{experts.start}", [P, len(experts) * C, PACK], BF16, after)
+            lines = slice(experts.start * C // LINE_SLOTS, experts.stop * C // LINE_SLOTS)
             nc.vector.tensor_tensor(
-                woven(x_bf[:, :, :], "p (c i) t"),
-                woven(tile[:, :, slots(experts, base)], "p t (c i)"),
-                per_pair.to_broadcast([P, len(experts) * C // PAIR, PACK, PAIR]),
+                woven(x_bf[:], "p (c i) t"),
+                woven(tile[:, :, slots(experts, first)], "p t (c i)"),
+                spread[:, lines, :].unsqueeze(2).to_broadcast([P, len(experts) * C // LINE_SLOTS, PACK, LINE_SLOTS]),
                 MULT,
             )
 
@@ -132,18 +133,8 @@ def tile_moe_pre_mlp_relu_kernel(tc, xT, w1_words, w1_scales, w2_words, w2_scale
             scales = new_tile(f"x_scales_{s}_{experts.start}", [P, len(experts) * C], U8)
             nc.vector.quantize_mx(out=codes[:].bitcast(FP8X4), scales=scales[:], in_=x_bf.rearrange("p c t -> p (c t)"))
             for e in experts:
-                cols = slots(range(e, e + 1), experts.start)
+                cols = slots(one[e], experts.start)
                 x_mx[s, e] = (codes[:, cols], scales[:, cols])
-
-        def late_passes(e, after, codes_after=None):
-            x_bf = new_tile(f"bf_late_{e}", [P, 2 * C, PACK], BF16, after)
-            interleave(2, one[e], x_bf[:, C : 2 * C, :])
-            gate_raw(1, one[e], x_bf[:, 0:C, :])
-            codes = new_tile(f"late_codes_{e}", [P, 2 * C], U32, codes_after)
-            scales = new_tile(f"late_scales_{e}", [P, 2 * C], U8)
-            nc.vector.quantize_mx(out=codes[:].bitcast(FP8X4), scales=scales[:], in_=x_bf[:].rearrange("p c t -> p (c t)"))
-            for s in range(1, PASSES):
-                x_mx[s, e] = (codes[:, (s - 1) * C : s * C], scales[:, (s - 1) * C : s * C])
 
         def first_product(e):
             a_acc[e] = psum.tile([P, H], F32, name=f"a_acc_{e}", tag=f"bank_{e}")
@@ -153,29 +144,30 @@ def tile_moe_pre_mlp_relu_kernel(tc, xT, w1_words, w1_scales, w2_words, w2_scale
                     lhsT=x_mx[s, e][0].bitcast(FP8X4),
                     lhsT_scale=x_mx[s, e][1],
                     rhs=w1_pass[s, e].bitcast(FP4X4),
-                    rhs_scale=w1_plane[min(e, PAIR)][:, max(e - PAIR, 0) * PASSES + s, :],
+                    rhs_scale=w1_plane[e // HALF][:, e % HALF * PASSES + s, :],
                     start=(s == 0),
                     stop=(s == PASSES - 1),
                 )
 
-        def turn_h(e, after=None):
-            own = ident
-            if after:
-                own = new_tile(f"ident_{e}", [P, P], F32, after)
-                nc.scalar.copy(out=own[:], in_=ident[:])
-            h_slot[e] = new_tile(f"h_slot_{e}", [P, H], BF16)
-            turned = psum.tile([P, 2, C], F32, name=f"turned_{e}", tag=f"turn_{e}")
-            h_out = h_slot[e][:].rearrange("j (u p d) -> j u p d", u=2, d=PAIR)
-            a_in = a_acc[e][:].rearrange("j (p u d) -> j u p d", u=2, d=PAIR)
-            if e == 2:
+        def late_identity(after):
+            own = new_tile("ident_1", [P, P], F32, after)
+            nc.scalar.copy(out=own[:], in_=ident[:])
+            return own
+
+        def turn_h(e, identity, relu_on_vector=False):
+            h_slot = new_tile(f"h_slot_{e}", [P, H], BF16)
+            turned = psum.tile([P, PACK // PAIR, C], F32, name=f"turned_{e}", tag=f"turn_{e}")
+            h_out = h_slot[:].rearrange("j (u p d) -> j u p d", p=P, d=PAIR)
+            a_in = a_acc[e][:].rearrange("j (p u d) -> j u p d", p=P, d=PAIR)
+            if relu_on_vector:
                 nc.vector.tensor_scalar_max(h_out, a_in, 0.0)
             else:
                 nc.scalar.activation(out=h_out, in_=a_in, func=RELU)
-            for u in range(2):
-                nc.tensor.transpose(turned[:, u, :], h_slot[e][:].bitcast(F32)[:, u * P : (u + 1) * P], own[:])
-            h_words[e] = new_tile(f"h_bf_{e}", [P, C * PAIR], F32)
+            for u in range(PACK // PAIR):
+                nc.tensor.transpose(turned[:, u, :], h_slot[:].bitcast(F32)[:, u * P : (u + 1) * P], identity[:])
+            h_words[e] = new_tile(f"h_bf_{e}", [P, C * PACK // PAIR], F32)
             nc.scalar.copy(
-                out=h_words[e][:].rearrange("p (j u) -> p j u", u=2),
+                out=h_words[e][:].rearrange("p (j u) -> p j u", j=C),
                 in_=turned[:].rearrange("p u j -> p j u"),
             )
 
@@ -202,19 +194,14 @@ def tile_moe_pre_mlp_relu_kernel(tc, xT, w1_words, w1_scales, w2_words, w2_scale
         def copy_y(e, row_tiles, dst):
             nc.scalar.copy(out=dst, in_=y_acc[e][:, row_tiles.start : row_tiles.stop, :])
 
-        def scatter(c, experts, on_vector, y=None):
-            window = out_sb[c][:].indirect(entries(experts))
-            y = y_sb[:, c, slots(experts)] if y is None else y
-            if on_vector:
-                nc.vector.tensor_copy(window, y)
-            else:
-                nc.scalar.activation(window, y, COPY)
+        def scatter_vector(c, cols, y):
+            nc.vector.tensor_copy(out_sb[c][:].indirect(entries(cols)), y)
+
+        def scatter_scalar(c, cols, y):
+            nc.scalar.activation(out_sb[c][:].indirect(entries(cols)), y, COPY)
 
         def store(c, queue):
             queue.dma_start(out=out[c * P : (c + 1) * P, :], in_=out_sb[c][:])
-
-        one = [range(e, e + 1) for e in range(E)]
-        early, late = range(0, PAIR), range(PAIR, E)
 
         for plane in w1_plane + w2_plane:
             nc.vector.memset(plane[:].bitcast(I32), 0)
@@ -222,53 +209,52 @@ def tile_moe_pre_mlp_relu_kernel(tc, xT, w1_words, w1_scales, w2_words, w2_scale
         for c in range(N_TILES):
             nc.gpsimd.memset(out_sb[c][:], 0.0)
 
-        gate_col = new_tile("gate_col", [P, PACK], F32)
-        nc.sync.dma_start(out=gate_col[:], in_=gate[0:1, :].rearrange("o (p q) -> p (o q)", q=PACK))
+        gate_col = [new_tile(f"gate_col_{h}", [P, LINE_SLOTS], F32) for h in range(E // HALF)]
+        gate_row = gate[0:1, :].rearrange("o (h p i) -> h p (o i)", p=P, i=LINE_SLOTS)
+        nc.sync.dma_start(out=gate_col[0][:], in_=gate_row[0])
         load_x(0, 0)
         nc.sync.dma_start(offsets[:], offs)
-        for t in range(1, PACK):
-            load_x(0, t)
-        for t in range(PACK):
-            load_x(1, t)
-        load_x(2, 0)
-        load_plane(w1_plane[0], w1_scales, slice(0, PASSES))
-        load_x(2, 1)
-        load_x(2, 2)
-        load_plane(w2_plane[0], w2_scales, slice(0, 1))
-        load_x(2, 3)
+        nc.sync.dma_start(out=gate_col[1][:], in_=gate_row[1])
+        for s in range(PASSES):
+            for t in range(PACK):
+                if (s, t) != (0, 0):
+                    load_x(s, t)
+                if (s, t) == (PASSES - 1, 1):
+                    load_plane(w2_plane[0], w2_scales, slice(0, 1))
+        load_plane(w1_plane[0], w1_scales, slice(0, HALF * PASSES))
         load_w1(0, range(0, 1))
         load_w1(0, range(1, PASSES))
-        load_plane(w1_plane[1], w1_scales, slice(PASSES, PAIR * PASSES))
-        load_w1(1, range(0, 2))
-        load_w1(1, range(2, PASSES))
-        load_plane(w1_plane[2], w1_scales, slice(PAIR * PASSES, E * PASSES))
-        load_w1(2, range(0, 2))
-        load_w1(2, range(2, PASSES))
+        load_w1(1, range(0, PASSES - 1))
+        load_w1(1, range(PASSES - 1, PASSES))
+        load_plane(w1_plane[1], w1_scales, slice(HALF * PASSES, E * PASSES))
+        load_w1(2, range(0, PASSES - 1))
+        load_w1(2, range(PASSES - 1, PASSES))
+        load_w1(3, range(0, PASSES - 1))
         load_w2(one[0])
-        load_w1(3, range(0, 2))
-        load_w1(3, range(2, PASSES))
+        load_w1(3, range(PASSES - 1, PASSES))
         load_plane(w2_plane[1], w2_scales, slice(1, E))
-        load_w2(range(1, E))
+        load_w2(others)
 
-        spread = psum.tile([P, PACK, P], F32, name="spread", tag="turn_3")
-        for q in range(PACK):
-            nc.tensor.transpose(spread[:, q, :], gate_col[:, q : q + 1].to_broadcast([P, P]), ident[:])
-        nc.vector.tensor_copy(gate_sb[:].rearrange("m (p q) -> m p q", q=PACK), spread[:].rearrange("m q p -> m p q"))
+        for h in range(E // HALF):
+            for i in range(LINE_SLOTS):
+                column = gate_col[h][:, i : i + 1].to_broadcast([P, P])
+                nc.tensor.transpose(spread[:, h * P : (h + 1) * P, i], column, ident[:])
+        nc.vector.tensor_copy(gate_sb[:].rearrange("m (c i) -> m c i", i=LINE_SLOTS), spread[:, 0:P, :])
 
         gather_raw(0, late)
         gather_gated(0, early)
         interleave(0, early)
-        gate_raw(0, late)
+        gate_raw(0, late, after="x_rows_0_3")
         quantize_x(0, early)
         quantize_x(0, late)
-        gather_raw(1, range(1, 3))
+        gather_raw(1, middle)
         gather_raw(1, one[3])
         gather_gated(1, one[0])
         interleave(1, one[0])
-        gate_raw(1, range(1, 3))
+        gate_raw(1, middle, after="x_rows_1_3")
         quantize_x(1, one[0])
-        quantize_x(1, range(1, 3))
-        gather_raw(2, range(1, 3))
+        quantize_x(1, middle)
+        gather_raw(2, middle)
         gather_raw(2, one[3])
         gather_gated(2, one[0])
         interleave(2, one[0])
@@ -283,29 +269,34 @@ def tile_moe_pre_mlp_relu_kernel(tc, xT, w1_words, w1_scales, w2_words, w2_scale
 
         first_product(0)
         first_product(1)
-        turn_h(0, after="w1_1_0")
+        turn_h(0, ident)
         quantize_h(0)
         quantize_x(2, one[3])
         first_product(2)
         second_layer(0)
-        copy_y(0, range(0, N_TILES), y_sb[:, :, slots(one[0])])
-        turn_h(1, after="w1_2_0")
+        copy_y(0, range(0, N_TILES - 1), y_sb[:, 0 : N_TILES - 1, slots(one[0])])
+        turn_h(1, late_identity(after="w1_2_0"))
         quantize_h(1)
         first_product(3)
-        for e in late:
-            turn_h(e)
-            quantize_h(e)
-        for e in range(1, E):
+        turn_h(2, ident, relu_on_vector=True)
+        quantize_h(2)
+        turn_h(3, ident)
+        quantize_h(3)
+        y_first = new_tile("y_first", [P, C], F32, "h_slot_3")
+        copy_y(0, range(N_TILES - 1, N_TILES), y_first[:].unsqueeze(1))
+        for e in others:
             second_layer(e)
             copy_y(e, range(0, N_TILES), y_sb[:, :, slots(one[e])])
 
-        scatter(0, one[0], True)
-        scatter(1, one[0], True)
-        scatter(0, one[1], True)
-        scatter(2, range(0, 3), True)
-        scatter(1, range(1, E), False)
-        store(1, nc.scalar)
-        scatter(2, one[3], False)
-        store(2, nc.scalar)
-        scatter(0, late, True)
+        cut = SLOTS - len(others) * C // 2
+        scatter_vector(0, slots(one[0]), y_sb[:, 0, slots(one[0])])
+        scatter_vector(1, slots(one[0]), y_sb[:, 1, slots(one[0])])
+        scatter_vector(2, slots(one[0]), y_first[:])
+        scatter_vector(0, slots(one[1]), y_sb[:, 0, slots(one[1])])
+        scatter_scalar(2, slice(cut, SLOTS), y_sb[:, 2, cut:SLOTS])
+        scatter_vector(0, slots(late), y_sb[:, 0, slots(late)])
         store(0, nc.sync)
+        scatter_vector(2, slice(C, cut), y_sb[:, 2, C:cut])
+        store(2, nc.sync)
+        scatter_scalar(1, slots(others), y_sb[:, 1, slots(others)])
+        store(1, nc.scalar)

@@ -17,18 +17,20 @@ U8 = mybir.dt.uint8
 FP8X4 = mybir.dt.float8_e4m3fn_x4
 FP4X4 = mybir.dt.float4_e2m1fn_x4
 MULT = mybir.AluOpType.mult
+ADD = mybir.AluOpType.add
 RELU = mybir.ActivationFunctionType.Relu
 COPY = mybir.ActivationFunctionType.Copy
 
 P = 128
 PACK = 4
 PASSES = K // (P * PACK)
+LAST = PASSES - 1
 N_TILES = N // P
 LIST_ROWS = 16
 SCALE_ROWS = 4
 PAIR = 2
-HALF = E // 2
 LINE_SLOTS = 2
+GATED = 192
 
 
 def tile_moe_pre_mlp_relu_kernel(tc, xT, w1_words, w1_scales, w2_words, w2_scales, gate, offs, out):
@@ -37,38 +39,35 @@ def tile_moe_pre_mlp_relu_kernel(tc, xT, w1_words, w1_scales, w2_words, w2_scale
         keep = ctx.enter_context(tc.tile_pool(name="keep", bufs=1))
         psum = ctx.enter_context(tc.psum_pool(name="psum", bufs=1))
 
-        one = [range(e, e + 1) for e in range(E)]
-        early, late = range(0, HALF), range(HALF, E)
-        middle, others = range(1, E - 1), range(1, E)
+        def new_tile(name, shape, dtype, place=None):
+            return keep.tile(shape, dtype, name=name, tag=place or name, align_bytes=64)
 
-        tiles = {}
-        place = {}
-
-        def new_tile(name, shape, dtype, after=None):
-            place[name] = place[after] if after else name
-            tiles[name] = keep.tile(shape, dtype, name=name, tag=place[name], align_bytes=64)
-            return tiles[name]
+        def slots(first, last=None):
+            return slice(first * C, ((first if last is None else last) + 1) * C)
 
         offsets = keep.tile([P, SLOTS // LIST_ROWS], U16, name="offsets")
-        gate_sb = new_tile("gate_sb", [P, HALF * C], F32)
         x_rows = [[new_tile(f"x_rows_{s}_{t}", [P, T], F32) for t in range(PACK)] for s in range(PASSES)]
-        w1_pass = {}
-        w1_plane = [new_tile(f"w1_plane_{g.start}", [P, len(g) * PASSES, H], U8) for g in (early, late)]
-        w2_sb = {}
-        w2_plane = [new_tile(f"w2_plane_{g.start}", [P, len(g), N], U8) for g in (one[0], others)]
-        out_sb = [keep.tile([P, T], F32, name=f"out_sb_{c}") for c in range(N_TILES)]
+        out_sb = [new_tile(f"out_sb_{c}", [P, T], F32) for c in range(N_TILES)]
         ident = new_tile("ident", [P, P], F32)
-
-        spread = psum.tile([P, SLOTS // LINE_SLOTS, LINE_SLOTS], F32, name="spread", tag=f"turn_{E - 1}")
-        x_mx = {}
-        a_acc, y_acc = {}, {}
-        h_words = {}
-        y_sb = new_tile("y_sb", [P, N_TILES, SLOTS], F32)
-        raw = {}
-        h_mx = {}
-
-        def slots(experts, first=0):
-            return slice((experts.start - first) * C, (experts.stop - first) * C)
+        plane_groups = [range(0, E // 2), range(E // 2, E)]
+        w1_plane = [new_tile(f"w1_plane_{g.start}", [P, len(g) * PASSES, H], U8) for g in plane_groups]
+        w2_plane = new_tile("w2_plane", [P, E, N], U8)
+        gate_col = new_tile("gate_col", [P, PACK], F32)
+        gate_sb = new_tile("gate_sb", [P, GATED], F32)
+        spread = psum.tile([P, SLOTS], F32, name="spread", tag=f"turn_{E - 1}")
+        y_flat = new_tile("y_sb", [P, N_TILES * SLOTS], F32)
+        y_sb = y_flat[:].rearrange("p (c j) -> p c j", c=N_TILES)
+        y_as_bf = y_flat[:].bitcast(BF16).rearrange("p (c j) -> p c j", c=N_TILES)
+        gated = [new_tile(f"gated_{s}", [P, PACK, GATED], F32) for s in range(LAST)]
+        raw = [new_tile(f"raw_{s}", [P, PACK, SLOTS - GATED], F32) for s in range(LAST)]
+        HALF = SLOTS // 2
+        pitch = HALF + C
+        raw_flat = new_tile("raw_last", [P, 2 * PACK * pitch], F32)
+        raw_early = raw_flat[:, pitch : (PACK + 1) * pitch].rearrange("p (t c) -> p t c", t=PACK)[:, :, C:pitch]
+        raw_late = raw_flat[:].rearrange("p (t c) -> p t c", t=PACK)[:, :, 0:HALF]
+        x_bf = {}
+        x_bf_last = [new_tile(f"x_bf_last_{e}", [P, C, PACK], BF16) for e in range(E)]
+        x_mx, w1_pass, w2_sb, a_acc, y_acc, h_words, h_mx, turned = {}, {}, {}, {}, {}, {}, {}, {}
 
         def entries(cols):
             return offsets[:, cols.start // LIST_ROWS : cols.stop // LIST_ROWS]
@@ -80,6 +79,10 @@ def tile_moe_pre_mlp_relu_kernel(tc, xT, w1_words, w1_scales, w2_words, w2_scale
             rows = scales.rearrange("e s (g r) i -> r g (e s) i", r=SCALE_ROWS)
             for r in range(SCALE_ROWS):
                 nc.sync.dma_start(out=plane[r:P:32, :, :].bitcast(I32), in_=rows[r, :, passes, :].bitcast(I32))
+
+        def load_w1_plane(g):
+            group = plane_groups[g]
+            load_plane(w1_plane[g], w1_scales, slice(group.start * PASSES, group.stop * PASSES))
 
         def load_w1(e, passes):
             tile = new_tile(f"w1_{e}_{passes.start}", [P, len(passes), 2 * H], U8)
@@ -98,205 +101,210 @@ def tile_moe_pre_mlp_relu_kernel(tc, xT, w1_words, w1_scales, w2_words, w2_scale
         def woven(ap, order):
             return ap.rearrange(order + " -> p c t i", i=LINE_SLOTS)
 
-        def gather_gated(s, experts):
-            cols = slots(experts)
-            gated = new_tile(f"gated_{s}_{experts.start}", [P, PACK, len(experts) * C], F32)
-            for t in range(PACK):
-                nc.vector.tensor_tensor(gated[:, t, :], x_rows[s][t][:].indirect(entries(cols)), gate_sb[:, cols], MULT)
+        def gather_gated(s, t):
+            cols = slice(0, GATED)
+            nc.vector.tensor_tensor(gated[s][:, t, :], x_rows[s][t][:].indirect(entries(cols)), gate_sb[:], MULT)
 
-        def interleave(s, experts):
-            x_bf = new_tile(f"bf_{s}_{experts.start}", [P, len(experts) * C, PACK], BF16)
-            gated = tiles[f"gated_{s}_{experts.start}"]
-            nc.vector.tensor_copy(woven(x_bf[:], "p (c i) t"), woven(gated[:], "p t (c i)"))
+        def gather_raw(s, t, cols, dst):
+            nc.scalar.activation(dst, x_rows[s][t][:].indirect(entries(cols)), COPY)
 
-        def gather_raw(s, experts):
-            tile = new_tile(f"raw_{s}_{experts.start}", [P, PACK, len(experts) * C], F32)
-            for t in range(PACK):
-                nc.scalar.activation(tile[:, t, :], x_rows[s][t][:].indirect(entries(slots(experts))), COPY)
-            for e in experts:
-                raw[s, e] = (tile, experts.start)
+        def interleave(s):
+            nc.gpsimd.tensor_scalar(x_bf[s][:, 0:GATED, :], gated[s][:].rearrange("p t c -> p c t"), 1.0, 0.0, MULT, ADD)
 
-        def gate_raw(s, experts, after):
-            tile, first = raw[s, experts.start]
-            x_bf = new_tile(f"bf_{s}_{experts.start}", [P, len(experts) * C, PACK], BF16, after)
-            lines = slice(experts.start * C // LINE_SLOTS, experts.stop * C // LINE_SLOTS)
+        def product(src, cols, dst):
+            lines = (cols.stop - cols.start) // LINE_SLOTS
             nc.vector.tensor_tensor(
-                woven(x_bf[:], "p (c i) t"),
-                woven(tile[:, :, slots(experts, first)], "p t (c i)"),
-                spread[:, lines, :].unsqueeze(2).to_broadcast([P, len(experts) * C // LINE_SLOTS, PACK, LINE_SLOTS]),
+                woven(dst, "p (c i) t"),
+                woven(src, "p t (c i)"),
+                spread[:, cols].rearrange("p (c i) -> p c i", i=LINE_SLOTS).unsqueeze(2).to_broadcast([P, lines, PACK, LINE_SLOTS]),
                 MULT,
             )
 
-        def quantize_x(s, experts):
-            x_bf = tiles[f"bf_{s}_{experts.start}"][:]
-            codes = new_tile(f"x_codes_{s}_{experts.start}", [P, len(experts) * C], U32)
-            scales = new_tile(f"x_scales_{s}_{experts.start}", [P, len(experts) * C], U8)
-            nc.vector.quantize_mx(out=codes[:].bitcast(FP8X4), scales=scales[:], in_=x_bf.rearrange("p c t -> p (c t)"))
-            for e in experts:
-                cols = slots(one[e], experts.start)
-                x_mx[s, e] = (codes[:, cols], scales[:, cols])
+        def quantize(name, src, width):
+            codes = new_tile(f"{name}_codes", [P, width], U32)
+            scales = new_tile(f"{name}_scales", [P, width], U8)
+            nc.vector.quantize_mx(out=codes[:].bitcast(FP8X4), scales=scales[:], in_=src)
+            return codes, scales
+
+        def quantize_pass(s):
+            codes, scales = quantize(f"x_{s}", x_bf[s][:].rearrange("p c t -> p (c t)"), SLOTS)
+            for e in range(E):
+                x_mx[s, e] = (codes[:, slots(e)], scales[:, slots(e)])
+
+        def last_place(e):
+            return (raw_early if e < E // 2 else raw_late)[:, :, slots(e % (E // 2))]
+
+        def product_last(e):
+            product(last_place(e), slots(e), x_bf_last[e][:])
+
+        def quantize_last(e):
+            codes, scales = quantize(f"x_last_{e}", x_bf_last[e][:].rearrange("p c t -> p (c t)"), C)
+            x_mx[LAST, e] = (codes[:], scales[:])
 
         def first_product(e):
             a_acc[e] = psum.tile([P, H], F32, name=f"a_acc_{e}", tag=f"bank_{e}")
+            g = e // (E // 2)
             for s in range(PASSES):
                 nc.tensor.matmul_mx(
                     out=a_acc[e][:],
                     lhsT=x_mx[s, e][0].bitcast(FP8X4),
                     lhsT_scale=x_mx[s, e][1],
                     rhs=w1_pass[s, e].bitcast(FP4X4),
-                    rhs_scale=w1_plane[e // HALF][:, e % HALF * PASSES + s, :],
+                    rhs_scale=w1_plane[g][:, (e - plane_groups[g].start) * PASSES + s, :],
                     start=(s == 0),
                     stop=(s == PASSES - 1),
                 )
 
-        def late_identity(after):
-            own = new_tile("ident_1", [P, P], F32, after)
-            nc.scalar.copy(out=own[:], in_=ident[:])
-            return own
-
-        def turn_h(e, identity, relu_on_vector=False):
-            h_slot = new_tile(f"h_slot_{e}", [P, H], BF16)
-            turned = psum.tile([P, PACK // PAIR, C], F32, name=f"turned_{e}", tag=f"turn_{e}")
-            h_out = h_slot[:].rearrange("j (u p d) -> j u p d", p=P, d=PAIR)
-            a_in = a_acc[e][:].rearrange("j (p u d) -> j u p d", p=P, d=PAIR)
-            if relu_on_vector:
-                nc.vector.tensor_scalar_max(h_out, a_in, 0.0)
-            else:
-                nc.scalar.activation(out=h_out, in_=a_in, func=RELU)
-            for u in range(PACK // PAIR):
-                nc.tensor.transpose(turned[:, u, :], h_slot[:].bitcast(F32)[:, u * P : (u + 1) * P], identity[:])
-            h_words[e] = new_tile(f"h_bf_{e}", [P, C * PACK // PAIR], F32)
-            nc.scalar.copy(
-                out=h_words[e][:].rearrange("p (j u) -> p j u", j=C),
-                in_=turned[:].rearrange("p u j -> p j u"),
+        def relu(e):
+            before = (e - 1) % E
+            h_out = y_as_bf[:, 1:N_TILES, PAIR * C * before : PAIR * C * (before + 1)]
+            nc.scalar.activation(
+                out=h_out.rearrange("j u (p d) -> j u p d", d=PAIR),
+                in_=a_acc[e][:].rearrange("j (p u d) -> j u p d", p=P, d=PAIR),
+                func=RELU,
             )
 
-        def quantize_h(e):
-            codes = new_tile(f"h_codes_{e}", [P, C], U32)
-            scales = new_tile(f"h_scales_{e}", [P, C], U8)
-            nc.vector.quantize_mx(out=codes[:].bitcast(FP8X4), scales=scales[:], in_=h_words[e][:].bitcast(BF16))
-            h_mx[e] = (codes, scales)
+        def turn_h(e):
+            turned[e] = psum.tile([P, PACK // PAIR, C], F32, name=f"turned_{e}", tag=f"turn_{e}")
+            for u in range(PACK // PAIR):
+                nc.tensor.transpose(turned[e][:, u, :], y_sb[:, 1 + u, slots((e - 1) % E)], ident[:])
 
-        def second_layer(e):
+        def copy_h(e):
+            h_words[e] = new_tile(f"h_words_{e}", [P, C * PACK // PAIR], F32)
+            nc.scalar.copy(out=h_words[e][:].rearrange("p (j u) -> p j u", j=C), in_=turned[e][:].rearrange("p u j -> p j u"))
+
+        def quantize_h(e):
+            h_mx[e] = quantize(f"h_{e}", h_words[e][:].bitcast(BF16), C)
+
+        def second_product(e):
             codes, scales = h_mx[e]
             y_acc[e] = psum.tile([P, N_TILES, C], F32, name=f"y_acc_{e}", tag=f"bank_{e}")
             for c in range(N_TILES):
                 nc.tensor.matmul_mx(
                     out=y_acc[e][:, c, :],
                     lhsT=w2_sb[e][:, 2 * P * c : 2 * P * (c + 1)].bitcast(FP4X4),
-                    lhsT_scale=w2_plane[min(e, 1)][:, max(e - 1, 0), P * c : P * (c + 1)],
+                    lhsT_scale=w2_plane[:, e, P * c : P * (c + 1)],
                     rhs=codes[:].bitcast(FP8X4),
                     rhs_scale=scales[:],
                     start=True,
                     stop=True,
                 )
 
-        def copy_y(e, row_tiles, dst):
-            nc.scalar.copy(out=dst, in_=y_acc[e][:, row_tiles.start : row_tiles.stop, :])
+        def copy_y(e, first, stop):
+            nc.scalar.copy(out=y_sb[:, first:stop, slots(e)], in_=y_acc[e][:, first:stop, :])
 
-        def scatter_vector(c, cols, y):
-            nc.vector.tensor_copy(out_sb[c][:].indirect(entries(cols)), y)
+        def scatter_vector(c, cols):
+            nc.vector.tensor_copy(out_sb[c][:].indirect(entries(cols)), y_sb[:, c, cols])
 
-        def scatter_scalar(c, cols, y):
-            nc.scalar.activation(out_sb[c][:].indirect(entries(cols)), y, COPY)
+        def scatter_scalar(c, cols):
+            nc.scalar.activation(out_sb[c][:].indirect(entries(cols)), y_sb[:, c, cols], COPY)
 
         def store(c, queue):
             queue.dma_start(out=out[c * P : (c + 1) * P, :], in_=out_sb[c][:])
 
-        for plane in w1_plane + w2_plane:
-            nc.vector.memset(plane[:].bitcast(I32), 0)
         make_identity(nc, ident[:])
-        for c in range(N_TILES):
-            nc.gpsimd.memset(out_sb[c][:], 0.0)
+        nc.gpsimd.memset(out_sb[0][:], 0.0)
+        nc.gpsimd.memset(out_sb[1][:], 0.0)
+        nc.scalar.activation(out_sb[2][:], out_sb[0][:], COPY)
+        for plane in w1_plane + [w2_plane]:
+            nc.gpsimd.memset(plane[:].bitcast(I32), 0)
 
-        gate_col = [new_tile(f"gate_col_{h}", [P, LINE_SLOTS], F32) for h in range(E // HALF)]
-        gate_row = gate[0:1, :].rearrange("o (h p i) -> h p (o i)", p=P, i=LINE_SLOTS)
-        nc.sync.dma_start(out=gate_col[0][:], in_=gate_row[0])
+        nc.sync.dma_start(out=gate_col[:], in_=gate[0:1, :].rearrange("o (p i) -> p (o i)", i=PACK))
         load_x(0, 0)
         nc.sync.dma_start(offsets[:], offs)
-        nc.sync.dma_start(out=gate_col[1][:], in_=gate_row[1])
         for s in range(PASSES):
             for t in range(PACK):
                 if (s, t) != (0, 0):
                     load_x(s, t)
-                if (s, t) == (PASSES - 1, 1):
-                    load_plane(w2_plane[0], w2_scales, slice(0, 1))
-        load_plane(w1_plane[0], w1_scales, slice(0, HALF * PASSES))
+        load_w1_plane(0)
         load_w1(0, range(0, 1))
         load_w1(0, range(1, PASSES))
-        load_w1(1, range(0, PASSES - 1))
-        load_w1(1, range(PASSES - 1, PASSES))
-        load_plane(w1_plane[1], w1_scales, slice(HALF * PASSES, E * PASSES))
-        load_w1(2, range(0, PASSES - 1))
-        load_w1(2, range(PASSES - 1, PASSES))
-        load_w1(3, range(0, PASSES - 1))
-        load_w2(one[0])
-        load_w1(3, range(PASSES - 1, PASSES))
-        load_plane(w2_plane[1], w2_scales, slice(1, E))
-        load_w2(others)
+        load_w1(1, range(0, LAST))
+        load_plane(w2_plane, w2_scales, slice(0, E))
+        load_w1_plane(1)
+        load_w1(1, range(LAST, PASSES))
+        load_w2(range(0, 1))
+        load_w1(2, range(0, LAST))
+        load_w1(2, range(LAST, PASSES))
+        load_w1(3, range(0, LAST))
+        load_w1(3, range(LAST, PASSES))
+        load_w2(range(1, 2))
+        load_w2(range(2, E))
 
-        for h in range(E // HALF):
-            for i in range(LINE_SLOTS):
-                column = gate_col[h][:, i : i + 1].to_broadcast([P, P])
-                nc.tensor.transpose(spread[:, h * P : (h + 1) * P, i], column, ident[:])
-        nc.vector.tensor_copy(gate_sb[:].rearrange("m (c i) -> m c i", i=LINE_SLOTS), spread[:, 0:P, :])
+        for i in range(PACK):
+            column = gate_col[:, i : i + 1].to_broadcast([P, P])
+            nc.tensor.transpose(spread[:, i:SLOTS:PACK], column, ident[:])
+        nc.vector.tensor_copy(gate_sb[:], spread[:, 0:GATED])
 
-        gather_raw(0, late)
-        gather_gated(0, early)
-        interleave(0, early)
-        gate_raw(0, late, after="x_rows_0_3")
-        quantize_x(0, early)
-        quantize_x(0, late)
-        gather_raw(1, middle)
-        gather_raw(1, one[3])
-        gather_gated(1, one[0])
-        interleave(1, one[0])
-        gate_raw(1, middle, after="x_rows_1_3")
-        quantize_x(1, one[0])
-        quantize_x(1, middle)
-        gather_raw(2, middle)
-        gather_raw(2, one[3])
-        gather_gated(2, one[0])
-        interleave(2, one[0])
-        quantize_x(2, one[0])
-        gate_raw(1, one[3], after="gated_2_0")
-        gate_raw(2, one[1], after="bf_2_0")
-        quantize_x(1, one[3])
-        gate_raw(2, one[2], after="bf_1_3")
-        quantize_x(2, one[1])
-        quantize_x(2, one[2])
-        gate_raw(2, one[3], after="bf_2_1")
+        rest = slice(GATED, SLOTS)
+        for s in range(LAST):
+            for t in range(PACK):
+                gather_gated(s, t)
+                gather_raw(s, t, rest, raw[s][:, t, :])
+                if s > 0 and t == 1:
+                    quantize_pass(s - 1)
+            x_bf[s] = new_tile(f"x_bf_{s}", [P, SLOTS, PACK], BF16, place=f"x_rows_{s}_{PACK - 1}")
+            interleave(s)
+            product(raw[s][:], rest, x_bf[s][:, rest, :])
+        quantize_pass(LAST - 1)
+        early, late = slice(0, HALF), slice(HALF, SLOTS)
+        gather_raw(LAST, 0, early, raw_early[:, 0, :])
+        gather_raw(LAST, 0, late, raw_late[:, 0, :])
+        gather_raw(LAST, 1, early, raw_early[:, 1, :])
+        gather_raw(LAST, 2, early, raw_early[:, 2, :])
+        gather_raw(LAST, 3, slots(0), raw_early[:, 3, slots(0)])
+        gather_raw(LAST, 3, slots(1), raw_early[:, 3, slots(1)])
+        gather_raw(LAST, 3, late, raw_late[:, 3, :])
+        product_last(0)
+        quantize_last(0)
+        gather_raw(LAST, 1, late, raw_late[:, 1, :])
+        gather_raw(LAST, 2, late, raw_late[:, 2, :])
+        product_last(1)
+        quantize_last(1)
+        product_last(2)
+        product_last(3)
+        quantize_last(2)
+        quantize_last(3)
 
         first_product(0)
+        relu(0)
         first_product(1)
-        turn_h(0, ident)
+        turn_h(0)
+        copy_h(0)
         quantize_h(0)
-        quantize_x(2, one[3])
+        relu(1)
+        second_product(0)
+        copy_y(0, 0, 1)
+        scatter_vector(0, slots(0))
         first_product(2)
-        second_layer(0)
-        copy_y(0, range(0, N_TILES - 1), y_sb[:, 0 : N_TILES - 1, slots(one[0])])
-        turn_h(1, late_identity(after="w1_2_0"))
+        turn_h(1)
+        copy_h(1)
         quantize_h(1)
+        copy_y(0, 1, N_TILES)
+        scatter_vector(1, slots(0))
+        scatter_vector(2, slots(0))
+        relu(2)
         first_product(3)
-        turn_h(2, ident, relu_on_vector=True)
+        relu(3)
+        turn_h(2)
+        copy_h(2)
         quantize_h(2)
-        turn_h(3, ident)
+        second_product(1)
+        copy_y(1, 0, 1)
+        scatter_vector(0, slots(1))
+        turn_h(3)
+        copy_h(3)
         quantize_h(3)
-        y_first = new_tile("y_first", [P, C], F32, "h_slot_3")
-        copy_y(0, range(N_TILES - 1, N_TILES), y_first[:].unsqueeze(1))
-        for e in others:
-            second_layer(e)
-            copy_y(e, range(0, N_TILES), y_sb[:, :, slots(one[e])])
-
-        cut = SLOTS - len(others) * C // 2
-        scatter_vector(0, slots(one[0]), y_sb[:, 0, slots(one[0])])
-        scatter_vector(1, slots(one[0]), y_sb[:, 1, slots(one[0])])
-        scatter_vector(2, slots(one[0]), y_first[:])
-        scatter_vector(0, slots(one[1]), y_sb[:, 0, slots(one[1])])
-        scatter_scalar(2, slice(cut, SLOTS), y_sb[:, 2, cut:SLOTS])
-        scatter_vector(0, slots(late), y_sb[:, 0, slots(late)])
-        store(0, nc.sync)
-        scatter_vector(2, slice(C, cut), y_sb[:, 2, C:cut])
+        copy_y(1, 1, N_TILES)
+        second_product(2)
+        copy_y(2, 0, N_TILES)
+        second_product(3)
+        copy_y(3, 0, N_TILES)
+        scatter_vector(1, slots(1))
+        scatter_vector(1, slots(2))
+        scatter_scalar(0, slots(2, 3))
+        store(0, nc.scalar)
+        scatter_vector(2, slots(1, 3))
         store(2, nc.sync)
-        scatter_scalar(1, slots(others), y_sb[:, 1, slots(others)])
+        scatter_scalar(1, slots(3))
         store(1, nc.scalar)

@@ -17,7 +17,6 @@ U8 = mybir.dt.uint8
 FP8X4 = mybir.dt.float8_e4m3fn_x4
 FP4X4 = mybir.dt.float4_e2m1fn_x4
 MULT = mybir.AluOpType.mult
-ADD = mybir.AluOpType.add
 RELU = mybir.ActivationFunctionType.Relu
 COPY = mybir.ActivationFunctionType.Copy
 
@@ -51,22 +50,17 @@ def tile_moe_pre_mlp_relu_kernel(tc, xT, w1_words, w1_scales, w2_words, w2_scale
         ident = new_tile("ident", [P, P], F32)
         plane_groups = [range(0, E // 2), range(E // 2, E)]
         w1_plane = [new_tile(f"w1_plane_{g.start}", [P, len(g) * PASSES, H], U8) for g in plane_groups]
-        w2_plane = new_tile("w2_plane", [P, E, N], U8)
+        w2_plane = [new_tile("w2_plane_0", [P, 1, N], U8), new_tile("w2_plane_1", [P, E - 1, N], U8)]
         gate_col = new_tile("gate_col", [P, PACK], F32)
         gate_sb = new_tile("gate_sb", [P, GATED], F32)
         spread = psum.tile([P, SLOTS], F32, name="spread", tag=f"turn_{E - 1}")
         y_flat = new_tile("y_sb", [P, N_TILES * SLOTS], F32)
         y_sb = y_flat[:].rearrange("p (c j) -> p c j", c=N_TILES)
         y_as_bf = y_flat[:].bitcast(BF16).rearrange("p (c j) -> p c j", c=N_TILES)
-        gated = [new_tile(f"gated_{s}", [P, PACK, GATED], F32) for s in range(LAST)]
-        raw = [new_tile(f"raw_{s}", [P, PACK, SLOTS - GATED], F32) for s in range(LAST)]
-        HALF = SLOTS // 2
-        pitch = HALF + C
-        raw_flat = new_tile("raw_last", [P, 2 * PACK * pitch], F32)
-        raw_early = raw_flat[:, pitch : (PACK + 1) * pitch].rearrange("p (t c) -> p t c", t=PACK)[:, :, C:pitch]
-        raw_late = raw_flat[:].rearrange("p (t c) -> p t c", t=PACK)[:, :, 0:HALF]
-        x_bf = {}
-        x_bf_last = [new_tile(f"x_bf_last_{e}", [P, C, PACK], BF16) for e in range(E)]
+        h_own = new_tile("h_own", [P, 2 * C], F32)
+        gated_width = [GATED, C, C]
+        gated = [new_tile(f"gated_{s}", [P, PACK, gated_width[s]], F32) for s in range(PASSES)]
+        raw = [new_tile(f"raw_{s}", [P, PACK, SLOTS - gated_width[s]], F32) for s in range(PASSES)]
         x_mx, w1_pass, w2_sb, a_acc, y_acc, h_words, h_mx, turned = {}, {}, {}, {}, {}, {}, {}, {}
 
         def entries(cols):
@@ -102,23 +96,29 @@ def tile_moe_pre_mlp_relu_kernel(tc, xT, w1_words, w1_scales, w2_words, w2_scale
             return ap.rearrange(order + " -> p c t i", i=LINE_SLOTS)
 
         def gather_gated(s, t):
-            cols = slice(0, GATED)
-            nc.vector.tensor_tensor(gated[s][:, t, :], x_rows[s][t][:].indirect(entries(cols)), gate_sb[:], MULT)
+            cols = slice(0, gated_width[s])
+            nc.vector.tensor_tensor(gated[s][:, t, :], x_rows[s][t][:].indirect(entries(cols)), gate_sb[:, cols], MULT)
 
-        def gather_raw(s, t, cols, dst):
-            nc.scalar.activation(dst, x_rows[s][t][:].indirect(entries(cols)), COPY)
+        def raw_part(s, cols):
+            return raw[s][:, :, cols.start - gated_width[s] : cols.stop - gated_width[s]]
 
-        def interleave(s):
-            nc.gpsimd.tensor_scalar(x_bf[s][:, 0:GATED, :], gated[s][:].rearrange("p t c -> p c t"), 1.0, 0.0, MULT, ADD)
+        def gather_raw(s, t, cols):
+            nc.scalar.activation(raw_part(s, cols)[:, t, :], x_rows[s][t][:].indirect(entries(cols)), COPY)
 
-        def product(src, cols, dst):
+        def interleave(s, dst):
+            nc.vector.tensor_copy(woven(dst, "p (c i) t"), woven(gated[s][:], "p t (c i)"))
+
+        def product(s, cols, dst):
             lines = (cols.stop - cols.start) // LINE_SLOTS
             nc.vector.tensor_tensor(
                 woven(dst, "p (c i) t"),
-                woven(src, "p t (c i)"),
+                woven(raw_part(s, cols), "p t (c i)"),
                 spread[:, cols].rearrange("p (c i) -> p c i", i=LINE_SLOTS).unsqueeze(2).to_broadcast([P, lines, PACK, LINE_SLOTS]),
                 MULT,
             )
+
+        def x_bf(s, first, last, place=None):
+            return new_tile(f"x_bf_{s}_{first}", [P, (last - first + 1) * C, PACK], BF16, place)
 
         def quantize(name, src, width):
             codes = new_tile(f"{name}_codes", [P, width], U32)
@@ -126,20 +126,10 @@ def tile_moe_pre_mlp_relu_kernel(tc, xT, w1_words, w1_scales, w2_words, w2_scale
             nc.vector.quantize_mx(out=codes[:].bitcast(FP8X4), scales=scales[:], in_=src)
             return codes, scales
 
-        def quantize_pass(s):
-            codes, scales = quantize(f"x_{s}", x_bf[s][:].rearrange("p c t -> p (c t)"), SLOTS)
-            for e in range(E):
-                x_mx[s, e] = (codes[:, slots(e)], scales[:, slots(e)])
-
-        def last_place(e):
-            return (raw_early if e < E // 2 else raw_late)[:, :, slots(e % (E // 2))]
-
-        def product_last(e):
-            product(last_place(e), slots(e), x_bf_last[e][:])
-
-        def quantize_last(e):
-            codes, scales = quantize(f"x_last_{e}", x_bf_last[e][:].rearrange("p c t -> p (c t)"), C)
-            x_mx[LAST, e] = (codes[:], scales[:])
+        def quantize_x(s, first, last, tile):
+            codes, scales = quantize(f"x_{s}_{first}", tile[:].rearrange("p c t -> p (c t)"), (last - first + 1) * C)
+            for e in range(first, last + 1):
+                x_mx[s, e] = (codes[:, slots(e - first)], scales[:, slots(e - first)])
 
         def first_product(e):
             a_acc[e] = psum.tile([P, H], F32, name=f"a_acc_{e}", tag=f"bank_{e}")
@@ -155,19 +145,24 @@ def tile_moe_pre_mlp_relu_kernel(tc, xT, w1_words, w1_scales, w2_words, w2_scale
                     stop=(s == PASSES - 1),
                 )
 
-        def relu(e):
-            before = (e - 1) % E
-            h_out = y_as_bf[:, 1:N_TILES, PAIR * C * before : PAIR * C * (before + 1)]
-            nc.scalar.activation(
-                out=h_out.rearrange("j u (p d) -> j u p d", d=PAIR),
-                in_=a_acc[e][:].rearrange("j (p u d) -> j u p d", p=P, d=PAIR),
-                func=RELU,
-            )
+        def h_place(e, view, width):
+            if e == 2:
+                return h_own[:].bitcast(view.dtype).rearrange("j (u w) -> j u w", u=2)
+            owner = (e + 2) % E
+            return view[:, 1:N_TILES, owner * width : (owner + 1) * width]
+
+        def relu(e, on_vector=False):
+            h_out = h_place(e, y_as_bf, PAIR * C).rearrange("j u (p d) -> j u p d", d=PAIR)
+            a_in = a_acc[e][:].rearrange("j (p u d) -> j u p d", p=P, d=PAIR)
+            if on_vector:
+                nc.vector.tensor_scalar_max(h_out, a_in, 0.0)
+            else:
+                nc.scalar.activation(out=h_out, in_=a_in, func=RELU)
 
         def turn_h(e):
             turned[e] = psum.tile([P, PACK // PAIR, C], F32, name=f"turned_{e}", tag=f"turn_{e}")
             for u in range(PACK // PAIR):
-                nc.tensor.transpose(turned[e][:, u, :], y_sb[:, 1 + u, slots((e - 1) % E)], ident[:])
+                nc.tensor.transpose(turned[e][:, u, :], h_place(e, y_sb, C)[:, u, :], ident[:])
 
         def copy_h(e):
             h_words[e] = new_tile(f"h_words_{e}", [P, C * PACK // PAIR], F32)
@@ -183,7 +178,7 @@ def tile_moe_pre_mlp_relu_kernel(tc, xT, w1_words, w1_scales, w2_words, w2_scale
                 nc.tensor.matmul_mx(
                     out=y_acc[e][:, c, :],
                     lhsT=w2_sb[e][:, 2 * P * c : 2 * P * (c + 1)].bitcast(FP4X4),
-                    lhsT_scale=w2_plane[:, e, P * c : P * (c + 1)],
+                    lhsT_scale=w2_plane[min(e, 1)][:, max(e - 1, 0), P * c : P * (c + 1)],
                     rhs=codes[:].bitcast(FP8X4),
                     rhs_scale=scales[:],
                     start=True,
@@ -206,8 +201,8 @@ def tile_moe_pre_mlp_relu_kernel(tc, xT, w1_words, w1_scales, w2_words, w2_scale
         nc.gpsimd.memset(out_sb[0][:], 0.0)
         nc.gpsimd.memset(out_sb[1][:], 0.0)
         nc.scalar.activation(out_sb[2][:], out_sb[0][:], COPY)
-        for plane in w1_plane + [w2_plane]:
-            nc.gpsimd.memset(plane[:].bitcast(I32), 0)
+        for plane in w1_plane + w2_plane:
+            nc.vector.memset(plane[:].bitcast(I32), 0)
 
         nc.sync.dma_start(out=gate_col[:], in_=gate[0:1, :].rearrange("o (p i) -> p (o i)", i=PACK))
         load_x(0, 0)
@@ -216,17 +211,19 @@ def tile_moe_pre_mlp_relu_kernel(tc, xT, w1_words, w1_scales, w2_words, w2_scale
             for t in range(PACK):
                 if (s, t) != (0, 0):
                     load_x(s, t)
+                if (s, t) == (LAST, 1):
+                    load_plane(w2_plane[0], w2_scales, slice(0, 1))
         load_w1_plane(0)
         load_w1(0, range(0, 1))
         load_w1(0, range(1, PASSES))
         load_w1(1, range(0, LAST))
-        load_plane(w2_plane, w2_scales, slice(0, E))
-        load_w1_plane(1)
         load_w1(1, range(LAST, PASSES))
-        load_w2(range(0, 1))
+        load_w1_plane(1)
         load_w1(2, range(0, LAST))
         load_w1(2, range(LAST, PASSES))
+        load_w2(range(0, 1))
         load_w1(3, range(0, LAST))
+        load_plane(w2_plane[1], w2_scales, slice(1, E))
         load_w1(3, range(LAST, PASSES))
         load_w2(range(1, 2))
         load_w2(range(2, E))
@@ -236,54 +233,58 @@ def tile_moe_pre_mlp_relu_kernel(tc, xT, w1_words, w1_scales, w2_words, w2_scale
             nc.tensor.transpose(spread[:, i:SLOTS:PACK], column, ident[:])
         nc.vector.tensor_copy(gate_sb[:], spread[:, 0:GATED])
 
-        rest = slice(GATED, SLOTS)
-        for s in range(LAST):
-            for t in range(PACK):
-                gather_gated(s, t)
-                gather_raw(s, t, rest, raw[s][:, t, :])
-                if s > 0 and t == 1:
-                    quantize_pass(s - 1)
-            x_bf[s] = new_tile(f"x_bf_{s}", [P, SLOTS, PACK], BF16, place=f"x_rows_{s}_{PACK - 1}")
-            interleave(s)
-            product(raw[s][:], rest, x_bf[s][:, rest, :])
-        quantize_pass(LAST - 1)
-        early, late = slice(0, HALF), slice(HALF, SLOTS)
-        gather_raw(LAST, 0, early, raw_early[:, 0, :])
-        gather_raw(LAST, 0, late, raw_late[:, 0, :])
-        gather_raw(LAST, 1, early, raw_early[:, 1, :])
-        gather_raw(LAST, 2, early, raw_early[:, 2, :])
-        gather_raw(LAST, 3, slots(0), raw_early[:, 3, slots(0)])
-        gather_raw(LAST, 3, slots(1), raw_early[:, 3, slots(1)])
-        gather_raw(LAST, 3, late, raw_late[:, 3, :])
-        product_last(0)
-        quantize_last(0)
-        gather_raw(LAST, 1, late, raw_late[:, 1, :])
-        gather_raw(LAST, 2, late, raw_late[:, 2, :])
-        product_last(1)
-        quantize_last(1)
-        product_last(2)
-        product_last(3)
-        quantize_last(2)
-        quantize_last(3)
+        for t in range(PACK):
+            gather_gated(0, t)
+            gather_raw(0, t, slice(GATED, SLOTS))
+        bf_0 = x_bf(0, 0, 3, f"x_rows_0_{PACK - 1}")
+        interleave(0, bf_0[:, 0:GATED, :])
+        product(0, slice(GATED, SLOTS), bf_0[:, GATED:SLOTS, :])
+        for t in range(PACK):
+            gather_gated(1, t)
+            gather_raw(1, t, slots(1, 3))
+            if t == 1:
+                quantize_x(0, 0, 3, bf_0)
+        bf_1 = x_bf(1, 0, 1)
+        interleave(1, bf_1[:, slots(0), :])
+        product(1, slots(1), bf_1[:, slots(1), :])
+        for t in range(PACK):
+            gather_gated(2, t)
+            if t == 0:
+                quantize_x(1, 0, 1, bf_1)
+            if t < PACK - 1:
+                gather_raw(2, t, slots(1, 3))
+        gather_raw(2, PACK - 1, slots(1))
+        gather_raw(2, PACK - 1, slots(2, 3))
+        bf_2 = [x_bf(2, e, e) for e in range(E)]
+        interleave(2, bf_2[0][:])
+        quantize_x(2, 0, 0, bf_2[0])
+        product(2, slots(1), bf_2[1][:])
+        bf_late = x_bf(1, 2, 3, "x_bf_2_0")
+        product(1, slots(2, 3), bf_late[:])
+        quantize_x(2, 1, 1, bf_2[1])
+        product(2, slots(2), bf_2[2][:])
+        quantize_x(1, 2, 3, bf_late)
+        quantize_x(2, 2, 2, bf_2[2])
+        product(2, slots(3), bf_2[3][:])
+        quantize_x(2, 3, 3, bf_2[3])
 
         first_product(0)
         relu(0)
         first_product(1)
+        relu(1)
         turn_h(0)
         copy_h(0)
         quantize_h(0)
-        relu(1)
-        second_product(0)
-        copy_y(0, 0, 1)
-        scatter_vector(0, slots(0))
-        first_product(2)
         turn_h(1)
         copy_h(1)
         quantize_h(1)
-        copy_y(0, 1, N_TILES)
-        scatter_vector(1, slots(0))
+        first_product(2)
+        second_product(0)
+        copy_y(0, 0, N_TILES)
+        relu(2, on_vector=True)
+        scatter_vector(0, slots(0))
+        scatter_scalar(1, slots(0))
         scatter_vector(2, slots(0))
-        relu(2)
         first_product(3)
         relu(3)
         turn_h(2)
@@ -298,13 +299,14 @@ def tile_moe_pre_mlp_relu_kernel(tc, xT, w1_words, w1_scales, w2_words, w2_scale
         copy_y(1, 1, N_TILES)
         second_product(2)
         copy_y(2, 0, N_TILES)
+        scatter_vector(1, slots(1))
+        scatter_scalar(2, slots(1))
         second_product(3)
         copy_y(3, 0, N_TILES)
-        scatter_vector(1, slots(1))
-        scatter_vector(1, slots(2))
-        scatter_scalar(0, slots(2, 3))
+        scatter_vector(0, slots(2))
+        scatter_scalar(0, slots(3))
         store(0, nc.scalar)
-        scatter_vector(2, slots(1, 3))
-        store(2, nc.sync)
-        scatter_scalar(1, slots(3))
-        store(1, nc.scalar)
+        scatter_vector(1, slots(2, 3))
+        store(1, nc.sync)
+        scatter_scalar(2, slots(2, 3))
+        store(2, nc.scalar)

@@ -48,20 +48,19 @@ def tile_moe_pre_mlp_relu_kernel(tc, xT, w1_words, w1_scales, w2_words, w2_scale
         x_rows = [[new_tile(f"x_rows_{s}_{t}", [P, T], F32) for t in range(PACK)] for s in range(PASSES)]
         out_sb = [new_tile(f"out_sb_{c}", [P, T], F32) for c in range(N_TILES)]
         ident = new_tile("ident", [P, P], F32)
-        plane_groups = [range(0, E // 2), range(E // 2, E)]
+        plane_groups = [range(0, 1), range(1, E)]
         w1_plane = [new_tile(f"w1_plane_{g.start}", [P, len(g) * PASSES, H], U8) for g in plane_groups]
-        w2_plane = [new_tile("w2_plane_0", [P, 1, N], U8), new_tile("w2_plane_1", [P, E - 1, N], U8)]
+        w2_plane = [new_tile(f"w2_plane_{g}", [P, E // 2, N], U8) for g in range(2)]
         gate_col = new_tile("gate_col", [P, PACK], F32)
         gate_sb = new_tile("gate_sb", [P, GATED], F32)
         spread = psum.tile([P, SLOTS], F32, name="spread", tag=f"turn_{E - 1}")
         y_flat = new_tile("y_sb", [P, N_TILES * SLOTS], F32)
         y_sb = y_flat[:].rearrange("p (c j) -> p c j", c=N_TILES)
         y_as_bf = y_flat[:].bitcast(BF16).rearrange("p (c j) -> p c j", c=N_TILES)
-        h_own = new_tile("h_own", [P, 2 * C], F32)
         gated_width = [GATED, C, C]
         gated = [new_tile(f"gated_{s}", [P, PACK, gated_width[s]], F32) for s in range(PASSES)]
         raw = [new_tile(f"raw_{s}", [P, PACK, SLOTS - gated_width[s]], F32) for s in range(PASSES)]
-        x_mx, w1_pass, w2_sb, a_acc, y_acc, h_words, h_mx, turned = {}, {}, {}, {}, {}, {}, {}, {}
+        x_mx, w1_pass, w2_sb, a_acc, y_acc, h_words, h_mx, turned, y_first = {}, {}, {}, {}, {}, {}, {}, {}, {}
 
         def entries(cols):
             return offsets[:, cols.start // LIST_ROWS : cols.stop // LIST_ROWS]
@@ -133,7 +132,7 @@ def tile_moe_pre_mlp_relu_kernel(tc, xT, w1_words, w1_scales, w2_words, w2_scale
 
         def first_product(e):
             a_acc[e] = psum.tile([P, H], F32, name=f"a_acc_{e}", tag=f"bank_{e}")
-            g = e // (E // 2)
+            g = min(e, 1)
             for s in range(PASSES):
                 nc.tensor.matmul_mx(
                     out=a_acc[e][:],
@@ -146,9 +145,9 @@ def tile_moe_pre_mlp_relu_kernel(tc, xT, w1_words, w1_scales, w2_words, w2_scale
                 )
 
         def h_place(e, view, width):
-            if e == 2:
-                return h_own[:].bitcast(view.dtype).rearrange("j (u w) -> j u w", u=2)
-            owner = (e + 2) % E
+            if e == 1:
+                return view[:, 2, 0 : 2 * width].rearrange("j (u w) -> j u w", u=2)
+            owner = {0: 2, 2: 3, 3: 1}[e]
             return view[:, 1:N_TILES, owner * width : (owner + 1) * width]
 
         def relu(e, on_vector=False):
@@ -173,12 +172,13 @@ def tile_moe_pre_mlp_relu_kernel(tc, xT, w1_words, w1_scales, w2_words, w2_scale
 
         def second_product(e):
             codes, scales = h_mx[e]
-            y_acc[e] = psum.tile([P, N_TILES, C], F32, name=f"y_acc_{e}", tag=f"bank_{e}")
+            y_first[e] = psum.tile([P, 1, C], F32, name=f"y_first_{e}", tag=f"turn_{e}")
+            y_acc[e] = psum.tile([P, N_TILES - 1, C], F32, name=f"y_acc_{e}", tag=f"bank_{e}")
             for c in range(N_TILES):
                 nc.tensor.matmul_mx(
-                    out=y_acc[e][:, c, :],
+                    out=y_first[e][:, 0, :] if c == 0 else y_acc[e][:, c - 1, :],
                     lhsT=w2_sb[e][:, 2 * P * c : 2 * P * (c + 1)].bitcast(FP4X4),
-                    lhsT_scale=w2_plane[min(e, 1)][:, max(e - 1, 0), P * c : P * (c + 1)],
+                    lhsT_scale=w2_plane[e // 2][:, e % 2, P * c : P * (c + 1)],
                     rhs=codes[:].bitcast(FP8X4),
                     rhs_scale=scales[:],
                     start=True,
@@ -186,7 +186,7 @@ def tile_moe_pre_mlp_relu_kernel(tc, xT, w1_words, w1_scales, w2_words, w2_scale
                 )
 
         def copy_y(e, first, stop):
-            nc.scalar.copy(out=y_sb[:, first:stop, slots(e)], in_=y_acc[e][:, first:stop, :])
+            nc.scalar.copy(out=y_sb[:, first:stop, slots(e)], in_=y_first[e][:] if first == 0 else y_acc[e][:, first - 1 : stop - 1, :])
 
         def scatter_vector(c, cols):
             nc.vector.tensor_copy(out_sb[c][:].indirect(entries(cols)), y_sb[:, c, cols])
@@ -211,21 +211,19 @@ def tile_moe_pre_mlp_relu_kernel(tc, xT, w1_words, w1_scales, w2_words, w2_scale
             for t in range(PACK):
                 if (s, t) != (0, 0):
                     load_x(s, t)
-                if (s, t) == (LAST, 1):
-                    load_plane(w2_plane[0], w2_scales, slice(0, 1))
         load_w1_plane(0)
-        load_w1(0, range(0, 1))
-        load_w1(0, range(1, PASSES))
-        load_w1(1, range(0, LAST))
-        load_w1(1, range(LAST, PASSES))
+        for s in range(PASSES):
+            load_w1(0, range(s, s + 1))
         load_w1_plane(1)
-        load_w1(2, range(0, LAST))
-        load_w1(2, range(LAST, PASSES))
+        load_w1(1, range(0, LAST))
+        load_plane(w2_plane[0], w2_scales, slice(0, 2))
+        load_w1(1, range(LAST, PASSES))
         load_w2(range(0, 1))
-        load_w1(3, range(0, LAST))
-        load_plane(w2_plane[1], w2_scales, slice(1, E))
-        load_w1(3, range(LAST, PASSES))
+        for e in range(2, E):
+            load_w1(e, range(0, LAST))
+            load_w1(e, range(LAST, PASSES))
         load_w2(range(1, 2))
+        load_plane(w2_plane[1], w2_scales, slice(2, E))
         load_w2(range(2, E))
 
         for i in range(PACK):
@@ -255,7 +253,7 @@ def tile_moe_pre_mlp_relu_kernel(tc, xT, w1_words, w1_scales, w2_words, w2_scale
                 gather_raw(2, t, slots(1, 3))
         gather_raw(2, PACK - 1, slots(1))
         gather_raw(2, PACK - 1, slots(2, 3))
-        bf_2 = [x_bf(2, e, e) for e in range(E)]
+        bf_2 = [x_bf(2, e, e) for e in range(E - 1)]
         interleave(2, bf_2[0][:])
         quantize_x(2, 0, 0, bf_2[0])
         product(2, slots(1), bf_2[1][:])
@@ -265,25 +263,28 @@ def tile_moe_pre_mlp_relu_kernel(tc, xT, w1_words, w1_scales, w2_words, w2_scale
         product(2, slots(2), bf_2[2][:])
         quantize_x(1, 2, 3, bf_late)
         quantize_x(2, 2, 2, bf_2[2])
-        product(2, slots(3), bf_2[3][:])
-        quantize_x(2, 3, 3, bf_2[3])
 
         first_product(0)
         relu(0)
-        first_product(1)
-        relu(1)
         turn_h(0)
         copy_h(0)
         quantize_h(0)
+        bf_last = x_bf(2, 3, 3, "h_words_0")
+        product(2, slots(3), bf_last[:])
+        quantize_x(2, 3, 3, bf_last)
+        first_product(1)
+        relu(1)
+        second_product(0)
+        copy_y(0, 0, 1)
+        copy_y(0, 1, 2)
+        scatter_vector(0, slots(0))
+        scatter_vector(1, slots(0))
+        first_product(2)
+        relu(2)
         turn_h(1)
         copy_h(1)
         quantize_h(1)
-        first_product(2)
-        second_product(0)
-        copy_y(0, 0, N_TILES)
-        relu(2, on_vector=True)
-        scatter_vector(0, slots(0))
-        scatter_scalar(1, slots(0))
+        copy_y(0, 2, N_TILES)
         scatter_vector(2, slots(0))
         first_product(3)
         relu(3)
@@ -298,12 +299,14 @@ def tile_moe_pre_mlp_relu_kernel(tc, xT, w1_words, w1_scales, w2_words, w2_scale
         quantize_h(3)
         copy_y(1, 1, N_TILES)
         second_product(2)
-        copy_y(2, 0, N_TILES)
+        copy_y(2, 0, 1)
+        copy_y(2, 1, N_TILES)
         scatter_vector(1, slots(1))
-        scatter_scalar(2, slots(1))
+        scatter_scalar(0, slots(2))
         second_product(3)
-        copy_y(3, 0, N_TILES)
-        scatter_vector(0, slots(2))
+        copy_y(3, 0, 1)
+        copy_y(3, 1, N_TILES)
+        scatter_vector(2, slots(1))
         scatter_scalar(0, slots(3))
         store(0, nc.scalar)
         scatter_vector(1, slots(2, 3))

@@ -45,7 +45,12 @@ def tile_moe_pre_mlp_relu_kernel(tc, xT, w1_words, w1_scales, w2_words, w2_scale
             return slice(first * C, ((first if last is None else last) + 1) * C)
 
         offsets = keep.tile([P, SLOTS // LIST_ROWS], U16, name="offsets")
-        x_rows = [[new_tile(f"x_rows_{s}_{t}", [P, T], F32) for t in range(PACK)] for s in range(PASSES)]
+        x_first = [new_tile(f"x_rows_0_{t}", [P, T], F32) for t in range(PACK)]
+        x_pairs = {(s, u): new_tile(f"x_rows_{s}_{u}", [P, PAIR, T], F32) for s in range(1, PASSES) for u in range(PACK // PAIR)}
+
+        def window(s, t):
+            return x_first[t][:] if s == 0 else x_pairs[s, t // PAIR][:, t % PAIR, :]
+
         out_sb = [new_tile(f"out_sb_{c}", [P, T], F32) for c in range(N_TILES)]
         ident = new_tile("ident", [P, P], F32)
         plane_groups = [range(0, 1), range(1, E)]
@@ -58,7 +63,7 @@ def tile_moe_pre_mlp_relu_kernel(tc, xT, w1_words, w1_scales, w2_words, w2_scale
         y_sb = y_flat[:].rearrange("p (c j) -> p c j", c=N_TILES)
         y_as_bf = y_flat[:].bitcast(BF16).rearrange("p (c j) -> p c j", c=N_TILES)
         gated_width = [GATED, C, C]
-        gated = [new_tile(f"gated_{s}", [P, PACK, gated_width[s]], F32) for s in range(PASSES)]
+        gated = {0: new_tile("gated_0", [P, PACK, GATED], F32)}
         raw = [new_tile(f"raw_{s}", [P, PACK, SLOTS - gated_width[s]], F32) for s in range(PASSES)]
         x_mx, w1_pass, w2_sb, a_acc, y_acc, h_words, h_mx, turned, y_first = {}, {}, {}, {}, {}, {}, {}, {}, {}
 
@@ -66,7 +71,10 @@ def tile_moe_pre_mlp_relu_kernel(tc, xT, w1_words, w1_scales, w2_words, w2_scale
             return offsets[:, cols.start // LIST_ROWS : cols.stop // LIST_ROWS]
 
         def load_x(s, t):
-            nc.sync.dma_start(out=x_rows[s][t][:], in_=xT.rearrange("(s p t) c -> s t p c", p=P, t=PACK)[s, t])
+            nc.sync.dma_start(out=x_first[t][:], in_=xT.rearrange("(s p t) c -> s t p c", p=P, t=PACK)[s, t])
+
+        def load_pair(s, u):
+            nc.sync.dma_start(out=x_pairs[s, u][:], in_=xT.rearrange("(s p u d) c -> s u p d c", p=P, u=PACK // PAIR, d=PAIR)[s, u])
 
         def load_plane(plane, scales, passes):
             rows = scales.rearrange("e s (g r) i -> r g (e s) i", r=SCALE_ROWS)
@@ -96,13 +104,18 @@ def tile_moe_pre_mlp_relu_kernel(tc, xT, w1_words, w1_scales, w2_words, w2_scale
 
         def gather_gated(s, t):
             cols = slice(0, gated_width[s])
-            nc.vector.tensor_tensor(gated[s][:, t, :], x_rows[s][t][:].indirect(entries(cols)), gate_sb[:, cols], MULT)
+            nc.vector.tensor_tensor(gated[s][:, t, :], window(s, t).indirect(entries(cols)), gate_sb[:, cols], MULT)
+
+        def gather_own(s, t):
+            nc.vector.tensor_copy(gated[s][:, t, :], window(s, t).indirect(entries(slots(0))))
 
         def raw_part(s, cols):
+            if cols.start < gated_width[s]:
+                return gated[s][:, :, cols]
             return raw[s][:, :, cols.start - gated_width[s] : cols.stop - gated_width[s]]
 
         def gather_raw(s, t, cols):
-            nc.scalar.activation(raw_part(s, cols)[:, t, :], x_rows[s][t][:].indirect(entries(cols)), COPY)
+            nc.scalar.activation(raw_part(s, cols)[:, t, :], window(s, t).indirect(entries(cols)), COPY)
 
         def interleave(s, dst):
             nc.vector.tensor_copy(woven(dst, "p (c i) t"), woven(gated[s][:], "p t (c i)"))
@@ -113,6 +126,15 @@ def tile_moe_pre_mlp_relu_kernel(tc, xT, w1_words, w1_scales, w2_words, w2_scale
                 woven(dst, "p (c i) t"),
                 woven(raw_part(s, cols), "p t (c i)"),
                 spread[:, cols].rearrange("p (c i) -> p c i", i=LINE_SLOTS).unsqueeze(2).to_broadcast([P, lines, PACK, LINE_SLOTS]),
+                MULT,
+            )
+
+        def product_gpsimd(s, dst):
+            cols = slots(E - 1)
+            nc.gpsimd.tensor_tensor(
+                dst,
+                raw_part(s, cols).rearrange("p t c -> p c t"),
+                gate_last[:].unsqueeze(2).to_broadcast([P, C, PACK]),
                 MULT,
             )
 
@@ -207,10 +229,11 @@ def tile_moe_pre_mlp_relu_kernel(tc, xT, w1_words, w1_scales, w2_words, w2_scale
         nc.sync.dma_start(out=gate_col[:], in_=gate[0:1, :].rearrange("o (p i) -> p (o i)", i=PACK))
         load_x(0, 0)
         nc.sync.dma_start(offsets[:], offs)
-        for s in range(PASSES):
-            for t in range(PACK):
-                if (s, t) != (0, 0):
-                    load_x(s, t)
+        for t in range(1, PACK):
+            load_x(0, t)
+        for s in range(1, PASSES):
+            for u in range(PACK // PAIR):
+                load_pair(s, u)
         load_w1_plane(0)
         for s in range(PASSES):
             load_w1(0, range(s, s + 1))
@@ -236,32 +259,41 @@ def tile_moe_pre_mlp_relu_kernel(tc, xT, w1_words, w1_scales, w2_words, w2_scale
             gather_raw(0, t, slice(GATED, SLOTS))
         bf_0 = x_bf(0, 0, 3, f"x_rows_0_{PACK - 1}")
         interleave(0, bf_0[:, 0:GATED, :])
-        product(0, slice(GATED, SLOTS), bf_0[:, GATED:SLOTS, :])
+        gate_last = new_tile("gate_last", [P, C], F32, "gate_sb")
+        nc.vector.tensor_copy(gate_last[:], spread[:, slots(E - 1)])
+        product_gpsimd(0, bf_0[:, slots(E - 1), :])
+        product(0, slice(GATED, SLOTS - C), bf_0[:, GATED : SLOTS - C, :])
+        gated[1] = new_tile("gated_1", [P, PACK, C], F32, "gated_0")
         for t in range(PACK):
-            gather_gated(1, t)
+            gather_own(1, t)
             gather_raw(1, t, slots(1, 3))
             if t == 1:
                 quantize_x(0, 0, 3, bf_0)
-        bf_1 = x_bf(1, 0, 1)
-        interleave(1, bf_1[:, slots(0), :])
-        product(1, slots(1), bf_1[:, slots(1), :])
+        bf_1 = x_bf(1, 0, 2)
+        product(1, slots(0), bf_1[:, slots(0), :])
+        product_gpsimd(1, bf_1[:, slots(2), :])
+        gated[2] = new_tile("gated_2", [P, PACK, C], F32, "gated_0")
         for t in range(PACK):
-            gather_gated(2, t)
-            if t == 0:
-                quantize_x(1, 0, 1, bf_1)
-            if t < PACK - 1:
+            gather_own(2, t)
+            if t == 1:
+                product(1, slots(1), bf_1[:, slots(1), :])
+            if t < PAIR:
                 gather_raw(2, t, slots(1, 3))
-        gather_raw(2, PACK - 1, slots(1))
-        gather_raw(2, PACK - 1, slots(2, 3))
-        bf_2 = [x_bf(2, e, e) for e in range(E - 1)]
-        interleave(2, bf_2[0][:])
+        quantize_x(1, 0, 2, bf_1)
+        x_mx[1, E - 1] = x_mx[1, 2]
+        for t in range(PAIR, PACK):
+            gather_raw(2, t, slots(1))
+        for t in range(PAIR, PACK):
+            gather_raw(2, t, slots(2, 3))
+        bf_2 = {e: x_bf(2, e, e) for e in (0, 2)}
+        product(2, slots(0), bf_2[0][:])
         quantize_x(2, 0, 0, bf_2[0])
-        product(2, slots(1), bf_2[1][:])
-        bf_late = x_bf(1, 2, 3, "x_bf_2_0")
-        product(1, slots(2, 3), bf_late[:])
-        quantize_x(2, 1, 1, bf_2[1])
+        bf_next = x_bf(2, 1, 2, "x_bf_2_0")
+        product(2, slots(1), bf_next[:, slots(0), :])
+        product(1, slots(2), bf_next[:, slots(1), :])
         product(2, slots(2), bf_2[2][:])
-        quantize_x(1, 2, 3, bf_late)
+        quantize_x(2, 1, 2, bf_next)
+        x_mx[1, 2] = x_mx[2, 2]
         quantize_x(2, 2, 2, bf_2[2])
 
         first_product(0)

@@ -45,11 +45,12 @@ def tile_moe_pre_mlp_relu_kernel(tc, xT, w1_words, w1_scales, w2_words, w2_scale
             return slice(first * C, ((first if last is None else last) + 1) * C)
 
         offsets = keep.tile([P, SLOTS // LIST_ROWS], U16, name="offsets")
-        x_first = [new_tile(f"x_rows_0_{t}", [P, T], F32) for t in range(PACK)]
-        x_pairs = {(s, u): new_tile(f"x_rows_{s}_{u}", [P, PAIR, T], F32) for s in range(1, PASSES) for u in range(PACK // PAIR)}
+        alone = [(0, t) for t in range(PACK)] + [(LAST, t) for t in range(PAIR, PACK)]
+        x_alone = {(s, t): new_tile(f"x_rows_{s}_{t}", [P, T], F32) for s, t in alone}
+        x_pairs = {(s, u): new_tile(f"x_pair_{s}_{u}", [P, PAIR, T], F32) for s, u in ((1, 0), (1, 1), (LAST, 0))}
 
         def window(s, t):
-            return x_first[t][:] if s == 0 else x_pairs[s, t // PAIR][:, t % PAIR, :]
+            return x_alone[s, t][:] if (s, t) in x_alone else x_pairs[s, t // PAIR][:, t % PAIR, :]
 
         out_sb = [new_tile(f"out_sb_{c}", [P, T], F32) for c in range(N_TILES)]
         ident = new_tile("ident", [P, P], F32)
@@ -71,7 +72,7 @@ def tile_moe_pre_mlp_relu_kernel(tc, xT, w1_words, w1_scales, w2_words, w2_scale
             return offsets[:, cols.start // LIST_ROWS : cols.stop // LIST_ROWS]
 
         def load_x(s, t):
-            nc.sync.dma_start(out=x_first[t][:], in_=xT.rearrange("(s p t) c -> s t p c", p=P, t=PACK)[s, t])
+            nc.sync.dma_start(out=x_alone[s, t][:], in_=xT.rearrange("(s p t) c -> s t p c", p=P, t=PACK)[s, t])
 
         def load_pair(s, u):
             nc.sync.dma_start(out=x_pairs[s, u][:], in_=xT.rearrange("(s p u d) c -> s u p d c", p=P, u=PACK // PAIR, d=PAIR)[s, u])
@@ -129,26 +130,26 @@ def tile_moe_pre_mlp_relu_kernel(tc, xT, w1_words, w1_scales, w2_words, w2_scale
                 MULT,
             )
 
-        def product_gpsimd(s, dst):
-            cols = slots(E - 1)
+        def product_gpsimd(s, e, dst):
+            cols = slots(e)
             nc.gpsimd.tensor_tensor(
                 dst,
                 raw_part(s, cols).rearrange("p t c -> p c t"),
-                gate_last[:].unsqueeze(2).to_broadcast([P, C, PACK]),
+                gate_late[:, slots(e - 2)].unsqueeze(2).to_broadcast([P, C, PACK]),
                 MULT,
             )
 
         def x_bf(s, first, last, place=None):
             return new_tile(f"x_bf_{s}_{first}", [P, (last - first + 1) * C, PACK], BF16, place)
 
-        def quantize(name, src, width):
-            codes = new_tile(f"{name}_codes", [P, width], U32)
+        def quantize(name, src, width, place=None):
+            codes = new_tile(f"{name}_codes", [P, width], U32, place)
             scales = new_tile(f"{name}_scales", [P, width], U8)
             nc.vector.quantize_mx(out=codes[:].bitcast(FP8X4), scales=scales[:], in_=src)
             return codes, scales
 
-        def quantize_x(s, first, last, tile):
-            codes, scales = quantize(f"x_{s}_{first}", tile[:].rearrange("p c t -> p (c t)"), (last - first + 1) * C)
+        def quantize_x(s, first, last, tile, place=None):
+            codes, scales = quantize(f"x_{s}_{first}", tile[:].rearrange("p c t -> p (c t)"), (last - first + 1) * C, place)
             for e in range(first, last + 1):
                 x_mx[s, e] = (codes[:, slots(e - first)], scales[:, slots(e - first)])
 
@@ -231,9 +232,10 @@ def tile_moe_pre_mlp_relu_kernel(tc, xT, w1_words, w1_scales, w2_words, w2_scale
         nc.sync.dma_start(offsets[:], offs)
         for t in range(1, PACK):
             load_x(0, t)
-        for s in range(1, PASSES):
-            for u in range(PACK // PAIR):
-                load_pair(s, u)
+        for s, u in x_pairs:
+            load_pair(s, u)
+        for t in range(PAIR, PACK):
+            load_x(LAST, t)
         load_w1_plane(0)
         for s in range(PASSES):
             load_w1(0, range(s, s + 1))
@@ -259,9 +261,9 @@ def tile_moe_pre_mlp_relu_kernel(tc, xT, w1_words, w1_scales, w2_words, w2_scale
             gather_raw(0, t, slice(GATED, SLOTS))
         bf_0 = x_bf(0, 0, 3, f"x_rows_0_{PACK - 1}")
         interleave(0, bf_0[:, 0:GATED, :])
-        gate_last = new_tile("gate_last", [P, C], F32, "gate_sb")
-        nc.vector.tensor_copy(gate_last[:], spread[:, slots(E - 1)])
-        product_gpsimd(0, bf_0[:, slots(E - 1), :])
+        gate_late = new_tile("gate_late", [P, 2 * C], F32, "gate_sb")
+        nc.vector.tensor_copy(gate_late[:], spread[:, slots(2, 3)])
+        product_gpsimd(0, 3, bf_0[:, slots(E - 1), :])
         product(0, slice(GATED, SLOTS - C), bf_0[:, GATED : SLOTS - C, :])
         gated[1] = new_tile("gated_1", [P, PACK, C], F32, "gated_0")
         for t in range(PACK):
@@ -269,32 +271,31 @@ def tile_moe_pre_mlp_relu_kernel(tc, xT, w1_words, w1_scales, w2_words, w2_scale
             gather_raw(1, t, slots(1, 3))
             if t == 1:
                 quantize_x(0, 0, 3, bf_0)
-        bf_1 = x_bf(1, 0, 2)
-        product(1, slots(0), bf_1[:, slots(0), :])
-        product_gpsimd(1, bf_1[:, slots(2), :])
+        bf_1 = x_bf(1, 0, 0)
+        product(1, slots(0), bf_1[:])
+        bf_13 = x_bf(1, 3, 3)
+        product_gpsimd(1, 3, bf_13[:])
         gated[2] = new_tile("gated_2", [P, PACK, C], F32, "gated_0")
         for t in range(PACK):
             gather_own(2, t)
-            if t == 1:
-                product(1, slots(1), bf_1[:, slots(1), :])
-            if t < PAIR:
+            if t == 0:
+                quantize_x(1, 0, 0, bf_1)
+            if t < PACK - 1:
                 gather_raw(2, t, slots(1, 3))
-        quantize_x(1, 0, 2, bf_1)
-        x_mx[1, E - 1] = x_mx[1, 2]
-        for t in range(PAIR, PACK):
-            gather_raw(2, t, slots(1))
-        for t in range(PAIR, PACK):
-            gather_raw(2, t, slots(2, 3))
-        bf_2 = {e: x_bf(2, e, e) for e in (0, 2)}
-        product(2, slots(0), bf_2[0][:])
-        quantize_x(2, 0, 0, bf_2[0])
-        bf_next = x_bf(2, 1, 2, "x_bf_2_0")
-        product(2, slots(1), bf_next[:, slots(0), :])
-        product(1, slots(2), bf_next[:, slots(1), :])
-        product(2, slots(2), bf_2[2][:])
-        quantize_x(2, 1, 2, bf_next)
-        x_mx[1, 2] = x_mx[2, 2]
-        quantize_x(2, 2, 2, bf_2[2])
+        gather_raw(2, PACK - 1, slots(1))
+        gather_raw(2, PACK - 1, slots(2, 3))
+        bf_2 = x_bf(2, 0, 0)
+        product(2, slots(0), bf_2[:])
+        quantize_x(2, 0, 0, bf_2)
+        bf_next = x_bf(3, 0, 3, "x_bf_2_0")
+        product_gpsimd(1, 2, bf_next[:, slots(2), :])
+        product(1, slots(1), bf_next[:, slots(0), :])
+        product(2, slots(1), bf_next[:, slots(1), :])
+        product(2, slots(2), bf_next[:, slots(3), :])
+        quantize_x(3, 0, 1, bf_next[:, slots(0, 1), :])
+        quantize_x(3, 2, 3, bf_next[:, slots(2, 3), :])
+        quantize_x(1, 3, 3, bf_13, "x_bf_2_0")
+        x_mx[1, 1], x_mx[2, 1], x_mx[1, 2], x_mx[2, 2] = (x_mx[3, j] for j in range(E))
 
         first_product(0)
         relu(0)

from contextlib import ExitStack

import concourse.mybir as mybir
from concourse.masks import make_identity

K, T, E, C, H, N = 1536, 768, 4, 128, 512, 384
SLOTS = E * C
FLOPS = 2 * SLOTS * (K * H + H * N)
BYTES = 4 * K * T + E * (K * H + H * N) * 17 // 32 + 4 * SLOTS + 2 * SLOTS + 4 * N * T

F32 = mybir.dt.float32
BF16 = mybir.dt.bfloat16
I32 = mybir.dt.int32
U32 = mybir.dt.uint32
U16 = mybir.dt.uint16
U8 = mybir.dt.uint8
FP8X4 = mybir.dt.float8_e4m3fn_x4
FP4X4 = mybir.dt.float4_e2m1fn_x4
MULT = mybir.AluOpType.mult
RELU = mybir.ActivationFunctionType.Relu
COPY = mybir.ActivationFunctionType.Copy

P = 128
PACK = 4
PASSES = K // (P * PACK)
LAST = PASSES - 1
N_TILES = N // P
LIST_ROWS = 16
SCALE_ROWS = 4
PAIR = 2
LINE_SLOTS = 2
GATED = 192


def tile_moe_pre_mlp_relu_kernel(tc, xT, w1_words, w1_scales, w2_words, w2_scales, gate, offs, out):
    nc = tc.nc
    with ExitStack() as ctx:
        keep = ctx.enter_context(tc.tile_pool(name="keep", bufs=1))
        psum = ctx.enter_context(tc.psum_pool(name="psum", bufs=1))

        def new_tile(name, shape, dtype, place=None):
            return keep.tile(shape, dtype, name=name, tag=place or name, align_bytes=64)

        def slots(first, last=None):
            return slice(first * C, ((first if last is None else last) + 1) * C)

        offsets = keep.tile([P, SLOTS // LIST_ROWS], U16, name="offsets")
        alone = [(0, t) for t in range(PACK)] + [(LAST, t) for t in range(PAIR, PACK)]
        x_alone = {(s, t): new_tile(f"x_rows_{s}_{t}", [P, T], F32) for s, t in alone}
        x_pairs = {(s, u): new_tile(f"x_pair_{s}_{u}", [P, PAIR, T], F32) for s, u in ((1, 0), (1, 1), (LAST, 0))}

        def window(s, t):
            return x_alone[s, t][:] if (s, t) in x_alone else x_pairs[s, t // PAIR][:, t % PAIR, :]

        out_sb = [new_tile(f"out_sb_{c}", [P, T], F32) for c in range(N_TILES)]
        ident = new_tile("ident", [P, P], F32)
        plane_groups = [range(0, 1), range(1, E)]
        w1_plane = [new_tile(f"w1_plane_{g.start}", [P, len(g) * PASSES, H], U8) for g in plane_groups]
        w2_plane = [new_tile(f"w2_plane_{g}", [P, E // 2, N], U8) for g in range(2)]
        gate_col = new_tile("gate_col", [P, PACK], F32)
        gate_sb = new_tile("gate_sb", [P, GATED], F32)
        spread = psum.tile([P, SLOTS], F32, name="spread", tag=f"turn_{E - 1}")
        y_flat = new_tile("y_sb", [P, N_TILES * SLOTS], F32)
        y_sb = y_flat[:].rearrange("p (c j) -> p c j", c=N_TILES)
        y_as_bf = y_flat[:].bitcast(BF16).rearrange("p (c j) -> p c j", c=N_TILES)
        gated_width = [GATED, C, C]
        gated = {0: new_tile("gated_0", [P, PACK, GATED], F32)}
        raw = [new_tile(f"raw_{s}", [P, PACK, SLOTS - gated_width[s]], F32) for s in range(PASSES)]
        x_mx, w1_pass, w2_sb, a_acc, y_acc, h_words, h_mx, turned, y_first = {}, {}, {}, {}, {}, {}, {}, {}, {}

        def entries(cols):
            return offsets[:, cols.start // LIST_ROWS : cols.stop // LIST_ROWS]

        def load_x(s, t):
            nc.sync.dma_start(out=x_alone[s, t][:], in_=xT.rearrange("(s p t) c -> s t p c", p=P, t=PACK)[s, t])

        def load_pair(s, u):
            nc.sync.dma_start(out=x_pairs[s, u][:], in_=xT.rearrange("(s p u d) c -> s u p d c", p=P, u=PACK // PAIR, d=PAIR)[s, u])

        def load_plane(plane, scales, passes):
            rows = scales.rearrange("e s (g r) i -> r g (e s) i", r=SCALE_ROWS)
            for r in range(SCALE_ROWS):
                nc.sync.dma_start(out=plane[r:P:32, :, :].bitcast(I32), in_=rows[r, :, passes, :].bitcast(I32))

        def load_w1_plane(g):
            group = plane_groups[g]
            load_plane(w1_plane[g], w1_scales, slice(group.start * PASSES, group.stop * PASSES))

        def load_w1(e, passes):
            tile = new_tile(f"w1_{e}_{passes.start}", [P, len(passes), 2 * H], U8)
            words = w1_words[e].rearrange("s p b -> p s b")
            nc.sync.dma_start(out=tile[:].bitcast(I32), in_=words[:, passes.start : passes.stop, :].bitcast(I32))
            for s in passes:
                w1_pass[s, e] = tile[:, s - passes.start, :]

        def load_w2(experts):
            tile = new_tile(f"w2_{experts.start}", [P, len(experts), 2 * N], U8)
            words = w2_words.rearrange("e s p b -> p (e s) b")
            nc.sync.dma_start(out=tile[:].bitcast(I32), in_=words[:, experts.start : experts.stop, :].bitcast(I32))
            for e in experts:
                w2_sb[e] = tile[:, e - experts.start, :]

        def woven(ap, order):
            return ap.rearrange(order + " -> p c t i", i=LINE_SLOTS)

        def gather_gated(s, t):
            cols = slice(0, gated_width[s])
            nc.vector.tensor_tensor(gated[s][:, t, :], window(s, t).indirect(entries(cols)), gate_sb[:, cols], MULT)

        def gather_own(s, t):
            nc.vector.tensor_copy(gated[s][:, t, :], window(s, t).indirect(entries(slots(0))))

        def raw_part(s, cols):
            if cols.start < gated_width[s]:
                return gated[s][:, :, cols]
            return raw[s][:, :, cols.start - gated_width[s] : cols.stop - gated_width[s]]

        def gather_raw(s, t, cols):
            nc.scalar.activation(raw_part(s, cols)[:, t, :], window(s, t).indirect(entries(cols)), COPY)

        def interleave(s, dst):
            nc.vector.tensor_copy(woven(dst, "p (c i) t"), woven(gated[s][:], "p t (c i)"))

        def product(s, cols, dst):
            lines = (cols.stop - cols.start) // LINE_SLOTS
            nc.vector.tensor_tensor(
                woven(dst, "p (c i) t"),
                woven(raw_part(s, cols), "p t (c i)"),
                spread[:, cols].rearrange("p (c i) -> p c i", i=LINE_SLOTS).unsqueeze(2).to_broadcast([P, lines, PACK, LINE_SLOTS]),
                MULT,
            )

        def product_gpsimd(s, e, dst):
            cols = slots(e)
            nc.gpsimd.tensor_tensor(
                dst,
                raw_part(s, cols).rearrange("p t c -> p c t"),
                gate_late[:, slots(e - 2)].unsqueeze(2).to_broadcast([P, C, PACK]),
                MULT,
            )

        def x_bf(s, first, last, place=None):
            return new_tile(f"x_bf_{s}_{first}", [P, (last - first + 1) * C, PACK], BF16, place)

        def quantize(name, src, width, place=None):
            codes = new_tile(f"{name}_codes", [P, width], U32, place)
            scales = new_tile(f"{name}_scales", [P, width], U8)
            nc.vector.quantize_mx(out=codes[:].bitcast(FP8X4), scales=scales[:], in_=src)
            return codes, scales

        def quantize_x(s, first, last, tile, place=None):
            codes, scales = quantize(f"x_{s}_{first}", tile[:].rearrange("p c t -> p (c t)"), (last - first + 1) * C, place)
            for e in range(first, last + 1):
                x_mx[s, e] = (codes[:, slots(e - first)], scales[:, slots(e - first)])

        def first_product(e):
            a_acc[e] = psum.tile([P, H], F32, name=f"a_acc_{e}", tag=f"bank_{e}")
            g = min(e, 1)
            for s in range(PASSES):
                nc.tensor.matmul_mx(
                    out=a_acc[e][:],
                    lhsT=x_mx[s, e][0].bitcast(FP8X4),
                    lhsT_scale=x_mx[s, e][1],
                    rhs=w1_pass[s, e].bitcast(FP4X4),
                    rhs_scale=w1_plane[g][:, (e - plane_groups[g].start) * PASSES + s, :],
                    start=(s == 0),
                    stop=(s == PASSES - 1),
                )

        def h_place(e, view, width):
            if e == 1:
                return view[:, 2, 0 : 2 * width].rearrange("j (u w) -> j u w", u=2)
            owner = {0: 2, 2: 3, 3: 1}[e]
            return view[:, 1:N_TILES, owner * width : (owner + 1) * width]

        def relu(e, on_vector=False):
            h_out = h_place(e, y_as_bf, PAIR * C).rearrange("j u (p d) -> j u p d", d=PAIR)
            a_in = a_acc[e][:].rearrange("j (p u d) -> j u p d", p=P, d=PAIR)
            if on_vector:
                nc.vector.tensor_scalar_max(h_out, a_in, 0.0)
            else:
                nc.scalar.activation(out=h_out, in_=a_in, func=RELU)

        def turn_h(e):
            turned[e] = psum.tile([P, PACK // PAIR, C], F32, name=f"turned_{e}", tag=f"turn_{e}")
            for u in range(PACK // PAIR):
                nc.tensor.transpose(turned[e][:, u, :], h_place(e, y_sb, C)[:, u, :], ident[:])

        def copy_h(e):
            h_words[e] = new_tile(f"h_words_{e}", [P, C * PACK // PAIR], F32)
            nc.scalar.copy(out=h_words[e][:].rearrange("p (j u) -> p j u", j=C), in_=turned[e][:].rearrange("p u j -> p j u"))

        def quantize_h(e):
            h_mx[e] = quantize(f"h_{e}", h_words[e][:].bitcast(BF16), C)

        def second_product(e):
            codes, scales = h_mx[e]
            y_first[e] = psum.tile([P, 1, C], F32, name=f"y_first_{e}", tag=f"turn_{e}")
            y_acc[e] = psum.tile([P, N_TILES - 1, C], F32, name=f"y_acc_{e}", tag=f"bank_{e}")
            for c in range(N_TILES):
                nc.tensor.matmul_mx(
                    out=y_first[e][:, 0, :] if c == 0 else y_acc[e][:, c - 1, :],
                    lhsT=w2_sb[e][:, 2 * P * c : 2 * P * (c + 1)].bitcast(FP4X4),
                    lhsT_scale=w2_plane[e // 2][:, e % 2, P * c : P * (c + 1)],
                    rhs=codes[:].bitcast(FP8X4),
                    rhs_scale=scales[:],
                    start=True,
                    stop=True,
                )

        def copy_y(e, first, stop):
            nc.scalar.copy(out=y_sb[:, first:stop, slots(e)], in_=y_first[e][:] if first == 0 else y_acc[e][:, first - 1 : stop - 1, :])

        def scatter_vector(c, cols):
            nc.vector.tensor_copy(out_sb[c][:].indirect(entries(cols)), y_sb[:, c, cols])

        def scatter_scalar(c, cols):
            nc.scalar.activation(out_sb[c][:].indirect(entries(cols)), y_sb[:, c, cols], COPY)

        def store(c, queue):
            queue.dma_start(out=out[c * P : (c + 1) * P, :], in_=out_sb[c][:])

        make_identity(nc, ident[:])
        nc.gpsimd.memset(out_sb[0][:], 0.0)
        nc.gpsimd.memset(out_sb[1][:], 0.0)
        nc.scalar.activation(out_sb[2][:], out_sb[0][:], COPY)
        for plane in w1_plane + w2_plane:
            nc.vector.memset(plane[:].bitcast(I32), 0)

        nc.sync.dma_start(out=gate_col[:], in_=gate[0:1, :].rearrange("o (p i) -> p (o i)", i=PACK))
        load_x(0, 0)
        nc.sync.dma_start(offsets[:], offs)
        for t in range(1, PACK):
            load_x(0, t)
        for s, u in x_pairs:
            load_pair(s, u)
        for t in range(PAIR, PACK):
            load_x(LAST, t)
        load_w1_plane(0)
        for s in range(PASSES):
            load_w1(0, range(s, s + 1))
        load_w1_plane(1)
        load_w1(1, range(0, LAST))
        load_plane(w2_plane[0], w2_scales, slice(0, 2))
        load_w1(1, range(LAST, PASSES))
        load_w2(range(0, 1))
        for e in range(2, E):
            load_w1(e, range(0, LAST))
            load_w1(e, range(LAST, PASSES))
        load_w2(range(1, 2))
        load_plane(w2_plane[1], w2_scales, slice(2, E))
        load_w2(range(2, E))

        for i in range(PACK):
            column = gate_col[:, i : i + 1].to_broadcast([P, P])
            nc.tensor.transpose(spread[:, i:SLOTS:PACK], column, ident[:])
        nc.vector.tensor_copy(gate_sb[:], spread[:, 0:GATED])

        for t in range(PACK):
            gather_gated(0, t)
            gather_raw(0, t, slice(GATED, SLOTS))
        bf_0 = x_bf(0, 0, 3, f"x_rows_0_{PACK - 1}")
        interleave(0, bf_0[:, 0:GATED, :])
        gate_late = new_tile("gate_late", [P, 2 * C], F32, "gate_sb")
        nc.vector.tensor_copy(gate_late[:], spread[:, slots(2, 3)])
        product_gpsimd(0, 3, bf_0[:, slots(E - 1), :])
        product(0, slice(GATED, SLOTS - C), bf_0[:, GATED : SLOTS - C, :])
        gated[1] = new_tile("gated_1", [P, PACK, C], F32, "gated_0")
        for t in range(PACK):
            gather_own(1, t)
            gather_raw(1, t, slots(1, 3))
            if t == 1:
                quantize_x(0, 0, 3, bf_0)
        bf_1 = x_bf(1, 0, 0)
        product(1, slots(0), bf_1[:])
        bf_13 = x_bf(1, 3, 3)
        product_gpsimd(1, 3, bf_13[:])
        gated[2] = new_tile("gated_2", [P, PACK, C], F32, "gated_0")
        for t in range(PACK):
            gather_own(2, t)
            if t == 0:
                quantize_x(1, 0, 0, bf_1)
            if t < PACK - 1:
                gather_raw(2, t, slots(1, 3))
        gather_raw(2, PACK - 1, slots(1))
        gather_raw(2, PACK - 1, slots(2, 3))
        bf_2 = x_bf(2, 0, 0)
        product(2, slots(0), bf_2[:])
        quantize_x(2, 0, 0, bf_2)
        bf_next = x_bf(3, 0, 3, "x_bf_2_0")
        product_gpsimd(1, 2, bf_next[:, slots(2), :])
        product(1, slots(1), bf_next[:, slots(0), :])
        product(2, slots(1), bf_next[:, slots(1), :])
        product(2, slots(2), bf_next[:, slots(3), :])
        quantize_x(3, 0, 1, bf_next[:, slots(0, 1), :])
        quantize_x(3, 2, 3, bf_next[:, slots(2, 3), :])
        quantize_x(1, 3, 3, bf_13, "x_bf_2_0")
        x_mx[1, 1], x_mx[2, 1], x_mx[1, 2], x_mx[2, 2] = (x_mx[3, j] for j in range(E))

        first_product(0)
        relu(0)
        turn_h(0)
        copy_h(0)
        quantize_h(0)
        bf_last = x_bf(2, 3, 3, "h_words_0")
        product(2, slots(3), bf_last[:])
        quantize_x(2, 3, 3, bf_last)
        first_product(1)
        relu(1)
        second_product(0)
        copy_y(0, 0, 1)
        copy_y(0, 1, 2)
        scatter_vector(0, slots(0))
        scatter_vector(1, slots(0))
        first_product(2)
        relu(2)
        turn_h(1)
        copy_h(1)
        quantize_h(1)
        copy_y(0, 2, N_TILES)
        scatter_vector(2, slots(0))
        first_product(3)
        relu(3)
        turn_h(2)
        copy_h(2)
        quantize_h(2)
        second_product(1)
        copy_y(1, 0, 1)
        scatter_vector(0, slots(1))
        turn_h(3)
        copy_h(3)
        quantize_h(3)
        copy_y(1, 1, N_TILES)
        second_product(2)
        copy_y(2, 0, 1)
        copy_y(2, 1, N_TILES)
        scatter_vector(1, slots(1))
        scatter_scalar(0, slots(2))
        second_product(3)
        copy_y(3, 0, 1)
        copy_y(3, 1, N_TILES)
        scatter_vector(2, slots(1))
        scatter_scalar(0, slots(3))
        store(0, nc.scalar)
        scatter_vector(1, slots(2, 3))
        store(1, nc.sync)
        scatter_scalar(2, slots(2, 3))
        store(2, nc.scalar)
